import numpy as np
import ml_dtypes


def mxq(x, axis, fmt="e4m3"):
    dtype, down = {"e4m3": (ml_dtypes.float8_e4m3fn, 7), "e5m2": (ml_dtypes.float8_e5m2, 14)}[fmt]
    v = np.moveaxis(np.asarray(x, np.float32).astype(ml_dtypes.bfloat16).astype(np.float64), axis, -1)
    blocks = v.reshape(v.shape[:-1] + (-1, 32))
    amax = np.abs(blocks).max(-1, keepdims=True)
    byte = np.maximum(np.where(amax > 0, np.frexp(amax)[1] - 1 + 127, 0) - down, 1)
    scale = np.exp2(byte - 127.0)
    codes = (blocks / scale).astype(np.float32).astype(dtype).astype(np.float64)
    return np.moveaxis((codes * scale).reshape(v.shape), -1, axis)


WIDE = False


def mx_kscale(k):
    if not WIDE:
        return np.ones(k)
    levels = np.array([24, -24, 12, -12, 0])
    if k % 512:
        return np.exp2(np.random.permutation(np.resize(levels, k // 32))).repeat(32)
    a = np.empty((k // 512, 16))
    for p in range(k // 512):
        a[p, :8] = np.random.permutation(np.resize(levels, 8))
        for g in range(8):
            far = levels[np.abs(levels - a[p, g]) >= 10]
            a[p, g + 8] = far[np.random.randint(len(far))]
    return np.exp2(a.ravel()).repeat(32)


def f64(x):
    return np.asarray(x).astype(np.float64)


def striped(idx):
    return np.tile(idx.reshape(-1, 16).T, (8, 1)).astype(np.uint16)


def unstriped(offs):
    return offs[:16].T.reshape(-1).astype(np.int64)


E2M1 = np.array([0.0, 0.5, 1.0, 1.5, 2.0, 3.0, 4.0, 6.0, -0.0, -0.5, -1.0, -1.5, -2.0, -3.0, -4.0, -6.0])


def pack_weight(w, fmt):
    k, n = w.shape
    w = f64(np.asarray(w, np.float32).astype(ml_dtypes.bfloat16)).reshape(k // 32, 32, n)
    amax = np.abs(w).max(1)
    if fmt == "e4m3":
        byte = np.frexp(amax)[1] - 1 + 127 - 7
    else:
        mant, ex = np.frexp(amax / 6.0)
        byte = np.where(mant > 0.5, ex, ex - 1) + 127
    byte = np.clip(np.where(amax > 0, byte, 1), 1, 254)
    scaled = (w * np.exp2(127.0 - byte)[:, None, :]).reshape(k, n).astype(np.float32)
    by_word = np.ascontiguousarray(scaled.reshape(k // 512, 128, 4, n).transpose(0, 1, 3, 2))
    if fmt == "e4m3":
        words = by_word.astype(ml_dtypes.float8_e4m3fn).view(np.uint8)
    else:
        c = by_word.astype(ml_dtypes.float4_e2m1fn).view(np.uint8) & 0xF
        words = (c[..., 0::2] | (c[..., 1::2] << 4)).reshape(k // 512, 128, 2 * n)
    return np.ascontiguousarray(words), np.ascontiguousarray(byte.astype(np.uint8).reshape(k // 512, 16, n))


def unpack_weight(words, scales, fmt):
    g, _, n = scales.shape
    words = np.ascontiguousarray(words).reshape(g, 128, n, -1)
    if fmt == "e4m3":
        vals = words.view(ml_dtypes.float8_e4m3fn).astype(np.float64)
    else:
        nib = np.empty((g, 128, n, 4), np.uint8)
        nib[..., 0::2] = words & 0xF
        nib[..., 1::2] = words >> 4
        vals = E2M1[nib]
    vals = vals * np.repeat(np.exp2(scales.astype(np.float64) - 127.0), 8, axis=1)[..., None]
    return vals.transpose(0, 1, 3, 2).reshape(g * 512, n)


def planes(y):
    n, m = y.shape
    v = y.astype(np.float32).astype(ml_dtypes.bfloat16).astype(np.float64).reshape(n // 32, 32, m)
    top = np.abs(v).max(1)
    byte = np.clip(np.where(top > 0, np.frexp(top)[1] - 1 + 127 - 7, 1), 1, 254)
    codes = (v * np.exp2(127.0 - byte)[:, None, :]).reshape(n, m).astype(np.float32).astype(ml_dtypes.float8_e4m3fn).view(np.uint8)
    words = codes.reshape(n // 512, 128, 4, m).transpose(0, 1, 3, 2)
    return np.ascontiguousarray(words), np.ascontiguousarray(byte.astype(np.uint8).reshape(n // 512, 16, m))


def sigm(f):
    return 1.0 / (1.0 + np.exp(-np.maximum(f, -700.0)))


K, M, N, T, J = 512, 512, 512, 2048, 1024


def setup_inputs():
    n = np.random.standard_normal
    s = mx_kscale(K)[:, None]
    s2 = mx_kscale(M)[:, None]
    h = np.tanh(n((N, T)))
    p_tab = pack_weight(h * s2, "e4m3")
    p_uz = pack_weight(n((M, N)) / np.sqrt(M) / s2, "e2m1")
    p_ur = pack_weight(n((M, N)) / np.sqrt(M) / s2, "e2m1")
    p_un = pack_weight(n((M, N)) / np.sqrt(M) / s2, "e2m1")
    return {
        "x": (n((K, J)) * s).astype(np.float32),
        "tab_words": p_tab[0],
        "tab_scales": p_tab[1],
        "wz": (n((K, N)) / np.sqrt(K) / s).astype(np.float32),
        "uz_words": p_uz[0],
        "uz_scales": p_uz[1],
        "wr": (n((K, N)) / np.sqrt(K) / s).astype(np.float32),
        "ur_words": p_ur[0],
        "ur_scales": p_ur[1],
        "wn": (n((K, N)) / np.sqrt(K) / s).astype(np.float32),
        "un_words": p_un[0],
        "un_scales": p_un[1],
        "bz": (0.3 * n(N)).astype(np.float32),
        "br": (0.3 * n(N)).astype(np.float32),
        "bn": (0.3 * n(N)).astype(np.float32),
        "hT": (h).astype(np.float32),
        "wgo": np.tile(np.random.uniform(0.5, 2.0, J), (128, 1)).astype(np.float32),
        "offs": striped(np.random.permutation(T)[:J]),
    }


def reference(x, tab_words, tab_scales, wz, uz_words, uz_scales, wr, ur_words, ur_scales, wn, un_words, un_scales, bz, br, bn, hT, wgo, offs):
    idx = unstriped(offs)
    x_ = mxq(f64(x), 0, "e4m3")
    tab_ = unpack_weight(tab_words, tab_scales, "e4m3")[:, idx]
    wz_ = mxq(f64(wz), 0, "e4m3")
    uz_ = unpack_weight(uz_words, uz_scales, "e2m1")
    wr_ = mxq(f64(wr), 0, "e4m3")
    ur_ = unpack_weight(ur_words, ur_scales, "e2m1")
    wn_ = mxq(f64(wn), 0, "e4m3")
    un_ = unpack_weight(un_words, un_scales, "e2m1")
    sz = wz_.T @ x_ + uz_.T @ tab_
    z = sigm(sz + f64(bz)[:, None])
    sr = wr_.T @ x_ + ur_.T @ tab_
    r = sigm(sr + f64(br)[:, None])
    xn = wn_.T @ x_
    hn = un_.T @ tab_
    cd = np.tanh(xn + f64(bn)[:, None] + r * hn)
    out = np.zeros((N, T))
    out[:, idx] = f64(wgo)[0] * (f64(hT)[:, idx] + z * (cd - f64(hT)[:, idx]))
    return (out,) + planes(out)

@@ -1,0 +1,294 @@
+from contextlib import ExitStack
+
+import concourse.mybir as mybir
+
+K, M, N, T, J = 512, 512, 512, 2048, 1024
+FLOPS = 6 * 2 * 512 * N * J
+
+F32 = mybir.dt.float32
+BF16 = mybir.dt.bfloat16
+I32 = mybir.dt.int32
+U32 = mybir.dt.uint32
+U16 = mybir.dt.uint16
+U8 = mybir.dt.uint8
+FP8X4 = mybir.dt.float8_e4m3fn_x4
+FP4X4 = mybir.dt.float4_e2m1fn_x4
+ALU = mybir.AluOpType
+ACT = mybir.ActivationFunctionType
+
+P = 128
+PACK = 4
+HALF = 512
+HALVES = J // HALF
+CHUNK = 512
+CHUNKS = T // CHUNK
+VECTOR_CHUNKS = (1, 2)
+
+
+def tile_list_tgn_gruP_kernel(
+    tc, x, tab_words, tab_scales, wz, uz_words, uz_scales, wr, ur_words, ur_scales,
+    wn, un_words, un_scales, bz, br, bn, hT, wgo, offs, out_0, out_1, out_2,
+):
+    nc = tc.nc
+    with ExitStack() as ctx:
+        keep = ctx.enter_context(tc.tile_pool(name="keep", bufs=1))
+        psum = ctx.enter_context(tc.psum_pool(name="psum", bufs=1))
+
+        def held(name, shape, dtype, on=None):
+            return keep.tile(shape, dtype, name=name, tag=on or name, align_bytes=64)
+
+        offsets = keep.tile([P, J // 16], U16, name="offsets")
+        table_words = held("table_words", [P, T], I32)
+        table_scales = held("table_scales", [P, T], U8)
+        gates = ("r", "n", "z")
+        w_dram = {"r": wr, "n": wn, "z": wz}
+        u_words_dram = {"r": ur_words, "n": un_words, "z": uz_words}
+        u_scales_dram = {"r": ur_scales, "n": un_scales, "z": uz_scales}
+        bias_dram = {"r": br, "n": bn, "z": bz}
+        w_raw = {g: held("w_raw_" + g, [P, PACK, N], F32) for g in gates}
+        u_words_raw = {g: held("u_words_raw_" + g, [P, 2 * N], U8) for g in gates}
+        u_scales_raw = {g: held("u_scales_raw_" + g, [P, N], U8) for g in gates}
+        bias = {g: held("bias_" + g, [P, PACK], F32) for g in gates}
+        x_raw = [held("x_raw_%d" % c, [P, PACK, HALF], F32) for c in range(HALVES)]
+        state = [held("state_%d" % t, [P, T], F32) for t in range(PACK)]
+        event_weight = [held("event_weight_%d" % c, [P, HALF], F32) for c in range(HALVES)]
+        result = [held("result_%d" % t, [P, T], F32) for t in range(PACK)]
+
+        warm = held("warm", [P, 8], F32)
+        warm_out = held("warm_out", [P, 8], F32)
+        nc.vector.memset(table_scales[:].bitcast(I32), 0)
+        for g in gates:
+            nc.vector.memset(u_scales_raw[g][:].bitcast(I32), 0)
+        nc.vector.memset(warm[:], 0.0)
+        nc.scalar.activation(warm_out[:], warm[:], ACT.Sigmoid)
+        for t in range(PACK):
+            nc.gpsimd.memset(result[t][:], 0.0)
+
+        def load_scale_rows(tile, dram):
+            for q in range(4):
+                nc.sync.dma_start(tile[32 * q : 32 * q + 4, :].bitcast(I32), dram[0, 4 * q : 4 * q + 4, :].bitcast(I32))
+
+        def load_rows(tile, dram):
+            nc.sync.dma_start(tile[:], dram.rearrange("(p j) c -> p j c", j=PACK))
+
+        def load_u_words(g):
+            nc.sync.dma_start(u_words_raw[g][:].bitcast(I32), u_words_dram[g][0].bitcast(I32))
+
+        def load_bias(g):
+            nc.sync.dma_start(bias[g][:], bias_dram[g].rearrange("(p t) -> p t", t=PACK))
+
+        def load_state(t):
+            nc.sync.dma_start(state[t][:], hT.rearrange("(p t) c -> p t c", t=PACK)[:, t, :])
+
+        nc.sync.dma_start(offsets[:], offs)
+        for g in gates:
+            load_bias(g)
+        nc.sync.dma_start(table_words[:], tab_words[0].rearrange("p c i -> p (c i)").bitcast(I32))
+        load_rows(x_raw[0], x[:, 0:HALF])
+        load_u_words("r")
+        load_u_words("n")
+        load_scale_rows(table_scales, tab_scales)
+        load_rows(w_raw["r"], wr)
+        load_scale_rows(u_scales_raw["r"], ur_scales)
+        load_rows(w_raw["n"], wn)
+        load_scale_rows(u_scales_raw["n"], un_scales)
+        load_rows(w_raw["z"], wz)
+        load_u_words("z")
+        load_scale_rows(u_scales_raw["z"], uz_scales)
+        load_state(0)
+        load_rows(x_raw[1], x[:, HALF:J])
+        nc.sync.dma_start(event_weight[0][:], wgo[:, 0:HALF])
+        load_state(1)
+        nc.sync.dma_start(event_weight[1][:], wgo[:, HALF:J])
+        for t in range(2, PACK):
+            load_state(t)
+
+        def listed(c):
+            return offsets[:, c * (HALF // 16) : (c + 1) * (HALF // 16)]
+
+        picked_words = [held("picked_words_%d" % c, [P, HALF], U32) for c in range(HALVES)]
+        picked_scales = [held("picked_scales_%d" % c, [P, HALF], U8) for c in range(HALVES)]
+        for c in range(HALVES):
+            nc.vector.tensor_copy(picked_words[c][:], table_words[:].bitcast(U32).indirect(listed(c)))
+            nc.vector.tensor_copy(picked_scales[c][:], table_scales[:].indirect(listed(c)))
+
+        def copy_on(engine, out, in_):
+            if engine == "scalar":
+                nc.scalar.copy(out, in_)
+            else:
+                nc.vector.tensor_copy(out, in_)
+
+        def quantise(name, grouped, width, on=None):
+            codes = held(name + "_codes", [P, width], U32)
+            scales = held(name + "_scales", [P, width], U8, on)
+            nc.vector.quantize_mx(out=codes[:].bitcast(FP8X4), scales=scales[:], in_=grouped[:])
+            return codes, scales
+
+        def round_x(c):
+            grouped = held("x_grouped_%d" % c, [P, HALF * PACK], BF16)
+            nc.scalar.copy(
+                grouped[:].rearrange("p (c i j) -> p c j i", i=4, j=PACK),
+                x_raw[c][:].rearrange("p j (c i) -> p c j i", i=4),
+            )
+            return grouped
+
+        def round_w(g, engine, on=None):
+            grouped = held("w_grouped_" + g, [P, N * PACK], BF16, on)
+            copy_on(
+                engine,
+                grouped[:].rearrange("p (t m j) -> p m j t", t=PACK, j=PACK),
+                w_raw[g][:].rearrange("p j (m t) -> p m j t", t=PACK),
+            )
+            return grouped
+
+        def deal_u(g):
+            words = held("u_words_" + g, [P, 2 * N], U8)
+            scales = held("u_scales_" + g, [P, N], U8)
+            nc.vector.tensor_copy(
+                words[:].bitcast(U16).rearrange("p (t m) -> p t m", t=PACK),
+                u_words_raw[g][:].bitcast(U16).rearrange("p (m t) -> p t m", t=PACK),
+            )
+            nc.vector.tensor_copy(
+                scales[:].rearrange("p (t m) -> p t m", t=PACK),
+                u_scales_raw[g][:].rearrange("p (m t) -> p t m", t=PACK),
+            )
+            return words, scales
+
+        x_mx, w_mx, u_mx = {}, {}, {}
+        x_grouped_0 = round_x(0)
+        w_grouped_r = round_w("r", "scalar")
+        x_mx[0] = quantise("x_0", x_grouped_0, HALF, on="table_scales")
+        u_mx["r"] = deal_u("r")
+        w_mx["r"] = quantise("w_r", w_grouped_r, N, on="u_scales_raw_r")
+        u_mx["n"] = deal_u("n")
+        w_grouped_n = round_w("n", "vector", on="u_scales_raw_n")
+        w_grouped_z = round_w("z", "scalar")
+        w_mx["n"] = quantise("w_n", w_grouped_n, N)
+        u_mx["z"] = deal_u("z")
+        w_mx["z"] = quantise("w_z", w_grouped_z, N, on="u_scales_raw_z")
+        minus_bias_z = held("minus_bias_z", [P, PACK], F32)
+        nc.vector.tensor_scalar(minus_bias_z[:], bias["z"][:], -1.0, None, ALU.mult)
+
+        def message_pass(acc, g, t, c, start, stop):
+            cols = slice(t * P, (t + 1) * P)
+            nc.tensor.matmul_mx(
+                out=acc[:], lhsT=w_mx[g][0][:, cols].bitcast(FP8X4), lhsT_scale=w_mx[g][1][:, cols],
+                rhs=x_mx[c][0][:].bitcast(FP8X4), rhs_scale=x_mx[c][1][:], start=start, stop=stop,
+            )
+
+        def state_pass(acc, g, t, c, start, stop):
+            nc.tensor.matmul_mx(
+                out=acc[:], lhsT=u_mx[g][0][:, 2 * t * P : 2 * (t + 1) * P].bitcast(FP4X4),
+                lhsT_scale=u_mx[g][1][:, t * P : (t + 1) * P],
+                rhs=picked_words[c][:].bitcast(FP8X4), rhs_scale=picked_scales[c][:], start=start, stop=stop,
+            )
+
+        units = [(0, 0), (1, 0), (0, 1), (1, 1), (2, 0), (2, 1), (3, 0), (3, 1)]
+
+        def ring(name, count):
+            tiles = [held("%s_%d" % (name, i), [P, HALF], F32) for i in range(count)]
+            return lambda u: tiles[u % count][:]
+
+        def bank_ring(name):
+            tiles = [psum.tile([P, HALF], F32, name="%s_%d" % (name, i)) for i in range(2)]
+            return lambda u: tiles[u % 2]
+
+        sr, hn, xn, sz = bank_ring("sr"), bank_ring("hn"), bank_ring("xn"), bank_ring("sz")
+        reset, keep_gate = ring("reset", 2), ring("keep_gate", 3)
+        cand, moved, updated = ring("cand", 3), ring("moved", 3), ring("updated", 2)
+
+        def products(u):
+            t, c = units[u]
+            state_pass(sr(u), "r", t, c, True, False)
+            message_pass(sr(u), "r", t, c, False, True)
+            state_pass(hn(u), "n", t, c, True, True)
+            message_pass(xn(u), "n", t, c, True, True)
+            state_pass(sz(u), "z", t, c, True, False)
+            message_pass(sz(u), "z", t, c, False, True)
+            nc.scalar.activation(reset(u), sr(u)[:], ACT.Sigmoid, bias=bias["r"][:, t : t + 1])
+            nc.scalar.activation(keep_gate(u), sz(u)[:], ACT.Sigmoid, bias=minus_bias_z[:, t : t + 1], scale=-1.0)
+
+        def reset_state(u):
+            nc.vector.tensor_tensor(cand(u), hn(u)[:], reset(u), ALU.mult)
+
+        def candidate(u):
+            t, c = units[u]
+            nc.vector.tensor_tensor(cand(u), xn(u)[:], cand(u), ALU.add)
+            nc.scalar.activation(cand(u), cand(u), ACT.Tanh, bias=bias["n"][:, t : t + 1])
+
+        def looked_up(u):
+            t, c = units[u]
+            return state[t][:].indirect(listed(c))
+
+        def gate(engine, u):
+            engine.tensor_tensor(moved(u), moved(u), keep_gate(u), ALU.mult)
+
+        def combine(engine, u):
+            engine.tensor_tensor(updated(u), moved(u), cand(u), ALU.add)
+
+        def weigh(engine, u):
+            c = units[u][1]
+            engine.tensor_tensor(updated(u), updated(u), event_weight[c][:], ALU.mult)
+
+        y_grouped = [held("y_grouped_%d" % k, [P, CHUNK, PACK], BF16) for k in range(CHUNKS)]
+        y_codes = [held("y_codes_%d" % k, [P, CHUNK], U32) for k in range(CHUNKS)]
+        y_scales = held("y_scales", [P, T], U8)
+        out_rows = out_0.rearrange("(p t) c -> p t c", t=PACK)
+
+        def round_y(t, k, engine):
+            source = result[t][:, k * CHUNK : (k + 1) * CHUNK]
+            if t == PACK - 2 and k in VECTOR_CHUNKS:
+                copy_on(engine, y_grouped[k][:, :, t : t + 2], source.unsqueeze(2).to_broadcast([P, CHUNK, 2]))
+            else:
+                copy_on(engine, y_grouped[k][:, :, t], source)
+
+        def place(u):
+            t, c = units[u]
+            nc.vector.tensor_copy(result[t][:].indirect(listed(c)), updated(u))
+            if c == HALVES - 1:
+                nc.sync.dma_start(out_rows[:, t, :], result[t][:])
+                for k in (1, 2, 0, 3):
+                    round_y(t, k, "vector" if t == PACK - 1 and k in VECTOR_CHUNKS else "scalar")
+
+        def prepare(u):
+            products(u)
+            reset_state(u)
+            nc.vector.tensor_copy(moved(u), looked_up(u))
+            candidate(u)
+
+        products(0)
+        reset_state(0)
+        candidate(0)
+        nc.vector.tensor_tensor(moved(0), looked_up(0), cand(0), ALU.subtract)
+        gate(nc.vector, 0)
+        prepare(1)
+        combine(nc.vector, 0)
+        x_mx[1] = quantise("x_1", round_x(1), HALF)
+        weigh(nc.gpsimd, 0)
+        place(0)
+        prepare(2)
+        last = len(units) - 1
+        for u in range(1, last + 2):
+            if u > 1:
+                combine(nc.gpsimd, u - 1)
+            if u <= last:
+                nc.gpsimd.tensor_tensor(moved(u), moved(u), cand(u), ALU.subtract)
+            if u > 1:
+                weigh(nc.gpsimd, u - 1)
+            if u <= last:
+                gate(nc.gpsimd, u)
+            if u + 2 <= last:
+                prepare(u + 2)
+            if u > 1:
+                place(u - 1)
+
+        out_words = out_1[0].rearrange("p c i -> p (c i)").bitcast(I32)
+        for k in range(CHUNKS):
+            cols = slice(k * CHUNK, (k + 1) * CHUNK)
+            nc.vector.quantize_mx(
+                out=y_codes[k][:].bitcast(FP8X4), scales=y_scales[:, cols],
+                in_=y_grouped[k][:].rearrange("p c i -> p (c i)"),
+            )
+            nc.sync.dma_start(out_words[:, cols], y_codes[k][:].bitcast(I32))
+        for q in range(4):
+            nc.sync.dma_start(out_2[0, 4 * q : 4 * q + 4, :].bitcast(I32), y_scales[32 * q : 32 * q + 4, :].bitcast(I32))

@@ -62,7 +62,7 @@ def tile_list_tgn_gruP_kernel(
         nc.vector.memset(warm[:], 0.0)
         nc.scalar.activation(warm_out[:], warm[:], ACT.Sigmoid)
         for t in range(PACK):
-            nc.gpsimd.memset(result[t][:], 0.0)
+            nc.vector.memset(result[t][:], 0.0)
 
         def load_scale_rows(tile, dram):
             for q in range(4):
@@ -95,11 +95,11 @@ def tile_list_tgn_gruP_kernel(
         load_rows(w_raw["z"], wz)
         load_u_words("z")
         load_scale_rows(u_scales_raw["z"], uz_scales)
-        load_state(0)
         load_rows(x_raw[1], x[:, HALF:J])
+        load_state(0)
         nc.sync.dma_start(event_weight[0][:], wgo[:, 0:HALF])
-        load_state(1)
         nc.sync.dma_start(event_weight[1][:], wgo[:, HALF:J])
+        load_state(1)
         for t in range(2, PACK):
             load_state(t)
 
@@ -132,13 +132,14 @@ def tile_list_tgn_gruP_kernel(
             )
             return grouped
 
-        def round_w(g, engine, on=None):
+        def round_w(g, shares, on=None):
             grouped = held("w_grouped_" + g, [P, N * PACK], BF16, on)
-            copy_on(
-                engine,
-                grouped[:].rearrange("p (t m j) -> p m j t", t=PACK, j=PACK),
-                w_raw[g][:].rearrange("p j (m t) -> p m j t", t=PACK),
-            )
+            for engine, m in shares:
+                copy_on(
+                    engine,
+                    grouped[:].rearrange("p (t m j) -> p m j t", t=PACK, j=PACK)[:, m],
+                    w_raw[g][:].rearrange("p j (m t) -> p m j t", t=PACK)[:, m],
+                )
             return grouped
 
         def deal_u(g):
@@ -156,16 +157,13 @@ def tile_list_tgn_gruP_kernel(
 
         x_mx, w_mx, u_mx = {}, {}, {}
         x_grouped_0 = round_x(0)
-        w_grouped_r = round_w("r", "scalar")
+        w_grouped_r = round_w("r", [("scalar", slice(0, P))])
         x_mx[0] = quantise("x_0", x_grouped_0, HALF, on="table_scales")
         u_mx["r"] = deal_u("r")
         w_mx["r"] = quantise("w_r", w_grouped_r, N, on="u_scales_raw_r")
         u_mx["n"] = deal_u("n")
-        w_grouped_n = round_w("n", "vector", on="u_scales_raw_n")
-        w_grouped_z = round_w("z", "scalar")
+        w_grouped_n = round_w("n", [("vector", slice(0, P))], on="u_scales_raw_n")
         w_mx["n"] = quantise("w_n", w_grouped_n, N)
-        u_mx["z"] = deal_u("z")
-        w_mx["z"] = quantise("w_z", w_grouped_z, N, on="u_scales_raw_z")
         minus_bias_z = held("minus_bias_z", [P, PACK], F32)
         nc.vector.tensor_scalar(minus_bias_z[:], bias["z"][:], -1.0, None, ALU.mult)
 
@@ -183,7 +181,7 @@ def tile_list_tgn_gruP_kernel(
                 rhs=picked_words[c][:].bitcast(FP8X4), rhs_scale=picked_scales[c][:], start=start, stop=stop,
             )
 
-        units = [(0, 0), (1, 0), (0, 1), (1, 1), (2, 0), (2, 1), (3, 0), (3, 1)]
+        units = [(0, 0), (0, 1), (1, 0), (1, 1), (2, 0), (2, 1), (3, 0), (3, 1)]
 
         def ring(name, count):
             tiles = [held("%s_%d" % (name, i), [P, HALF], F32) for i in range(count)]
@@ -194,8 +192,8 @@ def tile_list_tgn_gruP_kernel(
             return lambda u: tiles[u % 2]
 
         sr, hn, xn, sz = bank_ring("sr"), bank_ring("hn"), bank_ring("xn"), bank_ring("sz")
-        reset, keep_gate = ring("reset", 2), ring("keep_gate", 3)
-        cand, moved, updated = ring("cand", 3), ring("moved", 3), ring("updated", 2)
+        reset, keep_gate = ring("reset", 2), ring("keep_gate", 4)
+        cand, moved, updated = ring("cand", 3), ring("moved", 1), ring("updated", 2)
 
         def products(u):
             t, c = units[u]
@@ -203,9 +201,12 @@ def tile_list_tgn_gruP_kernel(
             message_pass(sr(u), "r", t, c, False, True)
             state_pass(hn(u), "n", t, c, True, True)
             message_pass(xn(u), "n", t, c, True, True)
+            nc.scalar.activation(reset(u), sr(u)[:], ACT.Sigmoid, bias=bias["r"][:, t : t + 1])
+
+        def update_gate(u):
+            t, c = units[u]
             state_pass(sz(u), "z", t, c, True, False)
             message_pass(sz(u), "z", t, c, False, True)
-            nc.scalar.activation(reset(u), sr(u)[:], ACT.Sigmoid, bias=bias["r"][:, t : t + 1])
             nc.scalar.activation(keep_gate(u), sz(u)[:], ACT.Sigmoid, bias=minus_bias_z[:, t : t + 1], scale=-1.0)
 
         def reset_state(u):
@@ -244,43 +245,50 @@ def tile_list_tgn_gruP_kernel(
 
         def place(u):
             t, c = units[u]
-            nc.vector.tensor_copy(result[t][:].indirect(listed(c)), updated(u))
+            if u < len(units) - 1:
+                nc.vector.tensor_copy(result[t][:].indirect(listed(c)), updated(u))
+            else:
+                nc.vector.tensor_tensor(result[t][:].indirect(listed(c)), updated(u), event_weight[c][:], ALU.mult)
             if c == HALVES - 1:
                 nc.sync.dma_start(out_rows[:, t, :], result[t][:])
                 for k in (1, 2, 0, 3):
                     round_y(t, k, "vector" if t == PACK - 1 and k in VECTOR_CHUNKS else "scalar")
 
+        def difference(u):
+            nc.vector.tensor_tensor(moved(u), looked_up(u), cand(u), ALU.subtract)
+
         def prepare(u):
             products(u)
             reset_state(u)
-            nc.vector.tensor_copy(moved(u), looked_up(u))
             candidate(u)
 
-        products(0)
-        reset_state(0)
-        candidate(0)
-        nc.vector.tensor_tensor(moved(0), looked_up(0), cand(0), ALU.subtract)
-        gate(nc.vector, 0)
-        prepare(1)
-        combine(nc.vector, 0)
-        x_mx[1] = quantise("x_1", round_x(1), HALF)
-        weigh(nc.gpsimd, 0)
-        place(0)
-        prepare(2)
         last = len(units) - 1
-        for u in range(1, last + 2):
-            if u > 1:
-                combine(nc.gpsimd, u - 1)
-            if u <= last:
-                nc.gpsimd.tensor_tensor(moved(u), moved(u), cand(u), ALU.subtract)
-            if u > 1:
-                weigh(nc.gpsimd, u - 1)
-            if u <= last:
-                gate(nc.gpsimd, u)
-            if u + 2 <= last:
-                prepare(u + 2)
-            if u > 1:
-                place(u - 1)
+        prepare(0)
+        w_grouped_z = round_w("z", [("scalar", slice(0, P))])
+        u_mx["z"] = deal_u("z")
+        w_mx["z"] = quantise("w_z", w_grouped_z, N, on="u_scales_raw_z")
+        update_gate(0)
+        x_mx[1] = quantise("x_1", round_x(1), HALF)
+        difference(0)
+        for u in range(1, 3):
+            prepare(u)
+            update_gate(u)
+        for u in range(last + 1):
+            engine = nc.gpsimd
+            gate(engine, u)
+            combine(engine, u)
+            if u < last:
+                weigh(nc.gpsimd, u)
+            ahead = u + 3
+            if ahead <= last:
+                products(ahead)
+                update_gate(ahead)
+                reset_state(ahead)
+            if u + 1 <= last:
+                difference(u + 1)
+            if ahead <= last:
+                candidate(ahead)
+            place(u)
 
         out_words = out_1[0].rearrange("p c i -> p (c i)").bitcast(I32)
         for k in range(CHUNKS):

@@ -56,13 +56,13 @@ def tile_list_tgn_gruP_kernel(
 
         warm = held("warm", [P, 8], F32)
         warm_out = held("warm_out", [P, 8], F32)
-        nc.vector.memset(table_scales[:].bitcast(I32), 0)
+        nc.gpsimd.memset(table_scales[:].bitcast(I32), 0)
         for g in gates:
-            nc.vector.memset(u_scales_raw[g][:].bitcast(I32), 0)
+            nc.gpsimd.memset(u_scales_raw[g][:].bitcast(I32), 0)
         nc.vector.memset(warm[:], 0.0)
         nc.scalar.activation(warm_out[:], warm[:], ACT.Sigmoid)
         for t in range(PACK):
-            nc.vector.memset(result[t][:], 0.0)
+            (nc.vector if t < 2 else nc.gpsimd).memset(result[t][:], 0.0)
 
         def load_scale_rows(tile, dram):
             for q in range(4):
@@ -124,9 +124,10 @@ def tile_list_tgn_gruP_kernel(
             nc.vector.quantize_mx(out=codes[:].bitcast(FP8X4), scales=scales[:], in_=grouped[:])
             return codes, scales
 
-        def round_x(c):
-            grouped = held("x_grouped_%d" % c, [P, HALF * PACK], BF16)
-            nc.scalar.copy(
+        def round_x(c, engine, on=None):
+            grouped = held("x_grouped_%d" % c, [P, HALF * PACK], BF16, on)
+            copy_on(
+                engine,
                 grouped[:].rearrange("p (c i j) -> p c j i", i=4, j=PACK),
                 x_raw[c][:].rearrange("p j (c i) -> p c j i", i=4),
             )
@@ -156,7 +157,7 @@ def tile_list_tgn_gruP_kernel(
             return words, scales
 
         x_mx, w_mx, u_mx = {}, {}, {}
-        x_grouped_0 = round_x(0)
+        x_grouped_0 = round_x(0, "scalar")
         w_grouped_r = round_w("r", [("scalar", slice(0, P))])
         x_mx[0] = quantise("x_0", x_grouped_0, HALF, on="table_scales")
         u_mx["r"] = deal_u("r")
@@ -164,6 +165,7 @@ def tile_list_tgn_gruP_kernel(
         u_mx["n"] = deal_u("n")
         w_grouped_n = round_w("n", [("vector", slice(0, P))], on="u_scales_raw_n")
         w_mx["n"] = quantise("w_n", w_grouped_n, N)
+        w_grouped_z = round_w("z", [("scalar", slice(0, P))])
         minus_bias_z = held("minus_bias_z", [P, PACK], F32)
         nc.vector.tensor_scalar(minus_bias_z[:], bias["z"][:], -1.0, None, ALU.mult)
 
@@ -183,8 +185,8 @@ def tile_list_tgn_gruP_kernel(
 
         units = [(0, 0), (0, 1), (1, 0), (1, 1), (2, 0), (2, 1), (3, 0), (3, 1)]
 
-        def ring(name, count):
-            tiles = [held("%s_%d" % (name, i), [P, HALF], F32) for i in range(count)]
+        def ring(name, count, first_on=None):
+            tiles = [held("%s_%d" % (name, i), [P, HALF], F32, first_on if i == 0 else None) for i in range(count)]
             return lambda u: tiles[u % count][:]
 
         def bank_ring(name):
@@ -193,7 +195,7 @@ def tile_list_tgn_gruP_kernel(
 
         sr, hn, xn, sz = bank_ring("sr"), bank_ring("hn"), bank_ring("xn"), bank_ring("sz")
         reset, keep_gate = ring("reset", 2), ring("keep_gate", 4)
-        cand, moved, updated = ring("cand", 3), ring("moved", 1), ring("updated", 2)
+        cand, moved, updated = ring("cand", 3, first_on="w_raw_z"), ring("moved", 1), ring("updated", 2)
 
         def products(u):
             t, c = units[u]
@@ -264,17 +266,16 @@ def tile_list_tgn_gruP_kernel(
 
         last = len(units) - 1
         prepare(0)
-        w_grouped_z = round_w("z", [("scalar", slice(0, P))])
         u_mx["z"] = deal_u("z")
         w_mx["z"] = quantise("w_z", w_grouped_z, N, on="u_scales_raw_z")
         update_gate(0)
-        x_mx[1] = quantise("x_1", round_x(1), HALF)
+        x_mx[1] = quantise("x_1", round_x(1, "vector", on="u_scales_raw_n"), HALF)
         difference(0)
         for u in range(1, 3):
             prepare(u)
             update_gate(u)
         for u in range(last + 1):
-            engine = nc.gpsimd
+            engine = nc.vector if u == 0 else nc.gpsimd
             gate(engine, u)
             combine(engine, u)
             if u < last:

@@ -32,6 +32,7 @@ def tile_list_tgn_gruP_kernel(
     nc = tc.nc
     with ExitStack() as ctx:
         keep = ctx.enter_context(tc.tile_pool(name="keep", bufs=1))
+        reused = ctx.enter_context(tc.tile_pool(name="reused", bufs=1))
         psum = ctx.enter_context(tc.psum_pool(name="psum", bufs=1))
 
         def held(name, shape, dtype, on=None):
@@ -52,17 +53,17 @@ def tile_list_tgn_gruP_kernel(
         x_raw = [held("x_raw_%d" % c, [P, PACK, HALF], F32) for c in range(HALVES)]
         state = [held("state_%d" % t, [P, T], F32) for t in range(PACK)]
         event_weight = [held("event_weight_%d" % c, [P, HALF], F32) for c in range(HALVES)]
-        result = [held("result_%d" % t, [P, T], F32) for t in range(PACK)]
+        result = [held("result_%d" % t, [P, T], F32) for t in range(2)]
 
         warm = held("warm", [P, 8], F32)
         warm_out = held("warm_out", [P, 8], F32)
-        nc.gpsimd.memset(table_scales[:].bitcast(I32), 0)
+        nc.vector.memset(table_scales[:].bitcast(I32), 0)
         for g in gates:
-            nc.gpsimd.memset(u_scales_raw[g][:].bitcast(I32), 0)
+            nc.vector.memset(u_scales_raw[g][:].bitcast(I32), 0)
         nc.vector.memset(warm[:], 0.0)
         nc.scalar.activation(warm_out[:], warm[:], ACT.Sigmoid)
-        for t in range(PACK):
-            (nc.vector if t < 2 else nc.gpsimd).memset(result[t][:], 0.0)
+        for t in range(2):
+            nc.vector.memset(result[t][:].bitcast(I32), 0)
 
         def load_scale_rows(tile, dram):
             for q in range(4):
@@ -269,7 +270,22 @@ def tile_list_tgn_gruP_kernel(
         u_mx["z"] = deal_u("z")
         w_mx["z"] = quantise("w_z", w_grouped_z, N, on="u_scales_raw_z")
         update_gate(0)
-        x_mx[1] = quantise("x_1", round_x(1, "vector", on="u_scales_raw_n"), HALF)
+        x_mx[1] = (held("x_1_codes", [P, HALF], U32), held("x_1_scales", [P, HALF], U8))
+        quarter = HALF // 2
+        x_parts = []
+        for i in range(2):
+            part = reused.tile([P, quarter * PACK], BF16, name="x_part_%d" % i, align_bytes=64, offset=i * T * 4)
+            nc.vector.tensor_copy(
+                part[:].rearrange("p (c i j) -> p c j i", i=4, j=PACK),
+                x_raw[1][:, :, i * quarter : (i + 1) * quarter].rearrange("p j (c i) -> p c j i", i=4),
+            )
+            x_parts.append(part)
+        for i in range(2):
+            cols = slice(i * quarter, (i + 1) * quarter)
+            nc.vector.quantize_mx(out=x_mx[1][0][:, cols].bitcast(FP8X4), scales=x_mx[1][1][:, cols], in_=x_parts[i][:])
+        for i in range(2):
+            result.append(reused.tile([P, T], F32, name="result_%d" % (2 + i), align_bytes=64, offset=i * T * 4))
+            nc.gpsimd.memset(result[2 + i][:].bitcast(I32), 0)
         difference(0)
         for u in range(1, 3):
             prepare(u)

@@ -23,6 +23,8 @@ HALVES = J // HALF
 CHUNK = 512
 CHUNKS = T // CHUNK
 VECTOR_CHUNKS = (1, 2)
+PAGES = 2
+ROUNDS = {4: [(0, 0), (0, 1), (0, 2), (0, 3)], 6: [(1, 0), (1, 1), (1, 2), (1, 3)], 7: [(2, 1), (2, 2), (2, 0), (2, 3)]}
 
 
 def tile_list_tgn_gruP_kernel(
@@ -32,11 +34,14 @@ def tile_list_tgn_gruP_kernel(
     nc = tc.nc
     with ExitStack() as ctx:
         keep = ctx.enter_context(tc.tile_pool(name="keep", bufs=1))
-        reused = ctx.enter_context(tc.tile_pool(name="reused", bufs=1))
+        shared = ctx.enter_context(tc.tile_pool(name="shared", bufs=1))
         psum = ctx.enter_context(tc.psum_pool(name="psum", bufs=1))
 
         def held(name, shape, dtype, on=None):
             return keep.tile(shape, dtype, name=name, tag=on or name, align_bytes=64)
+
+        def placed(name, shape, dtype, offset):
+            return shared.tile(shape, dtype, name=name, align_bytes=64, offset=offset)
 
         offsets = keep.tile([P, J // 16], U16, name="offsets")
         table_words = held("table_words", [P, T], I32)
@@ -48,22 +53,24 @@ def tile_list_tgn_gruP_kernel(
         bias_dram = {"r": br, "n": bn, "z": bz}
         w_raw = {g: held("w_raw_" + g, [P, PACK, N], F32) for g in gates}
         u_words_raw = {g: held("u_words_raw_" + g, [P, 2 * N], U8) for g in gates}
-        u_scales_raw = {g: held("u_scales_raw_" + g, [P, N], U8) for g in gates}
+        u_scales_raw = {g: held("u_scales_raw_" + g, [P, N], U8) for g in ("r",)}
+        u_scales_raw["n"] = placed("u_scales_raw_n", [P, N], U8, 12800 - 256)
+        u_scales_raw["z"] = placed("u_scales_raw_z", [P, N], U8, 10240 - 256)
         bias = {g: held("bias_" + g, [P, PACK], F32) for g in gates}
         x_raw = [held("x_raw_%d" % c, [P, PACK, HALF], F32) for c in range(HALVES)]
         state = [held("state_%d" % t, [P, T], F32) for t in range(PACK)]
         event_weight = [held("event_weight_%d" % c, [P, HALF], F32) for c in range(HALVES)]
-        result = [held("result_%d" % t, [P, T], F32) for t in range(2)]
+        pages = [held("page_%d" % i, [P, T], F32) for i in range(PAGES)]
 
         warm = held("warm", [P, 8], F32)
         warm_out = held("warm_out", [P, 8], F32)
-        nc.vector.memset(table_scales[:].bitcast(I32), 0)
-        for g in gates:
-            nc.vector.memset(u_scales_raw[g][:].bitcast(I32), 0)
         nc.vector.memset(warm[:], 0.0)
         nc.scalar.activation(warm_out[:], warm[:], ACT.Sigmoid)
-        for t in range(2):
-            nc.vector.memset(result[t][:].bitcast(I32), 0)
+        nc.gpsimd.memset(table_scales[:].bitcast(I32), 0)
+        for g in gates:
+            nc.gpsimd.memset(u_scales_raw[g][:].bitcast(I32), 0)
+        for page in pages:
+            nc.vector.memset(page[:].bitcast(I32), 0)
 
         def load_scale_rows(tile, dram):
             for q in range(4):
@@ -82,26 +89,25 @@ def tile_list_tgn_gruP_kernel(
             nc.sync.dma_start(state[t][:], hT.rearrange("(p t) c -> p t c", t=PACK)[:, t, :])
 
         nc.sync.dma_start(offsets[:], offs)
-        for g in gates:
-            load_bias(g)
         nc.sync.dma_start(table_words[:], tab_words[0].rearrange("p c i -> p (c i)").bitcast(I32))
-        load_rows(x_raw[0], x[:, 0:HALF])
         load_u_words("r")
         load_u_words("n")
+        for g in gates:
+            load_bias(g)
+        load_rows(x_raw[0], x[:, 0:HALF])
         load_scale_rows(table_scales, tab_scales)
         load_rows(w_raw["r"], wr)
         load_scale_rows(u_scales_raw["r"], ur_scales)
         load_rows(w_raw["n"], wn)
         load_scale_rows(u_scales_raw["n"], un_scales)
-        load_rows(w_raw["z"], wz)
-        load_u_words("z")
-        load_scale_rows(u_scales_raw["z"], uz_scales)
         load_rows(x_raw[1], x[:, HALF:J])
         load_state(0)
+        load_u_words("z")
+        load_scale_rows(u_scales_raw["z"], uz_scales)
+        load_rows(w_raw["z"], wz)
         nc.sync.dma_start(event_weight[0][:], wgo[:, 0:HALF])
         nc.sync.dma_start(event_weight[1][:], wgo[:, HALF:J])
-        load_state(1)
-        for t in range(2, PACK):
+        for t in range(1, PACK):
             load_state(t)
 
         def listed(c):
@@ -109,8 +115,11 @@ def tile_list_tgn_gruP_kernel(
 
         picked_words = [held("picked_words_%d" % c, [P, HALF], U32) for c in range(HALVES)]
         picked_scales = [held("picked_scales_%d" % c, [P, HALF], U8) for c in range(HALVES)]
-        for c in range(HALVES):
+
+        def pick_words(c):
             nc.vector.tensor_copy(picked_words[c][:], table_words[:].bitcast(U32).indirect(listed(c)))
+
+        def pick_scales(c):
             nc.vector.tensor_copy(picked_scales[c][:], table_scales[:].indirect(listed(c)))
 
         def copy_on(engine, out, in_):
@@ -121,90 +130,137 @@ def tile_list_tgn_gruP_kernel(
 
         def quantise(name, grouped, width, on=None):
             codes = held(name + "_codes", [P, width], U32)
-            scales = held(name + "_scales", [P, width], U8, on)
-            nc.vector.quantize_mx(out=codes[:].bitcast(FP8X4), scales=scales[:], in_=grouped[:])
+            scales = placed(name + "_scales", [P, width], U8, on) if isinstance(on, int) else held(name + "_scales", [P, width], U8, on)
+            nc.vector.quantize_mx(out=codes[:].bitcast(FP8X4), scales=scales[:], in_=grouped)
             return codes, scales
 
-        def round_x(c, engine, on=None):
-            grouped = held("x_grouped_%d" % c, [P, HALF * PACK], BF16, on)
+        def round_x(grouped, c, engine, part):
             copy_on(
                 engine,
-                grouped[:].rearrange("p (c i j) -> p c j i", i=4, j=PACK),
-                x_raw[c][:].rearrange("p j (c i) -> p c j i", i=4),
+                grouped[:].rearrange("p (c i j) -> p c j i", i=4, j=PACK)[:, part],
+                x_raw[c][:].rearrange("p j (c i) -> p c j i", i=4)[:, part],
             )
-            return grouped
 
-        def round_w(g, shares, on=None):
-            grouped = held("w_grouped_" + g, [P, N * PACK], BF16, on)
-            for engine, m in shares:
-                copy_on(
-                    engine,
-                    grouped[:].rearrange("p (t m j) -> p m j t", t=PACK, j=PACK)[:, m],
-                    w_raw[g][:].rearrange("p j (m t) -> p m j t", t=PACK)[:, m],
-                )
-            return grouped
+        def round_w(g, pair, engine):
+            copy_on(
+                engine,
+                w_grouped[g, pair][:].rearrange("p (t m j) -> p m j t", t=2, j=PACK),
+                w_raw[g][:].rearrange("p j (m t) -> p m j t", t=PACK)[:, :, :, 2 * pair : 2 * pair + 2],
+            )
 
-        def deal_u(g):
-            words = held("u_words_" + g, [P, 2 * N], U8)
-            scales = held("u_scales_" + g, [P, N], U8)
+        def deal_words(g, on=None):
+            words = placed("u_words_z", [P, 2 * N], U8, on) if on else held("u_words_" + g, [P, 2 * N], U8)
             nc.vector.tensor_copy(
                 words[:].bitcast(U16).rearrange("p (t m) -> p t m", t=PACK),
                 u_words_raw[g][:].bitcast(U16).rearrange("p (m t) -> p t m", t=PACK),
             )
+            return words
+
+        def deal_scales(g, on=None):
+            scales = held("u_scales_" + g, [P, N], U8, on)
             nc.vector.tensor_copy(
                 scales[:].rearrange("p (t m) -> p t m", t=PACK),
                 u_scales_raw[g][:].rearrange("p (m t) -> p t m", t=PACK),
             )
-            return words, scales
+            return scales
 
-        x_mx, w_mx, u_mx = {}, {}, {}
-        x_grouped_0 = round_x(0, "scalar")
-        w_grouped_r = round_w("r", [("scalar", slice(0, P))])
-        x_mx[0] = quantise("x_0", x_grouped_0, HALF, on="table_scales")
-        u_mx["r"] = deal_u("r")
-        w_mx["r"] = quantise("w_r", w_grouped_r, N, on="u_scales_raw_r")
-        u_mx["n"] = deal_u("n")
-        w_grouped_n = round_w("n", [("vector", slice(0, P))], on="u_scales_raw_n")
-        w_mx["n"] = quantise("w_n", w_grouped_n, N)
-        w_grouped_z = round_w("z", [("scalar", slice(0, P))])
+        x_mx, w_mx, u_words, u_scales = {}, {}, {}, {}
         minus_bias_z = held("minus_bias_z", [P, PACK], F32)
+        x_grouped = [held("x_grouped_0", [P, HALF * PACK], BF16)]
+        w_grouped = {key: held("w_grouped_%s%d" % key, [P, 2 * P * PACK], BF16) for key in (("r", 0), ("r", 1), ("z", 0), ("z", 1))}
+        w_grouped["n", 0] = shared.tile([P, 2 * P * PACK], BF16, name="w_grouped_n0", align_bytes=64, offset=3072)
+
+        def quantise_w(g, pair, on=None):
+            codes, scales = quantise("w_%s%d" % (g, pair), w_grouped[g, pair][:], 2 * P, on)
+            for t in range(2):
+                w_mx[g, 2 * pair + t] = (codes[:, t * P : (t + 1) * P], scales[:, t * P : (t + 1) * P])
+
+        round_x(x_grouped[0], 0, "scalar", slice(0, P))
+        round_w("r", 0, "scalar")
+        round_w("r", 1, "scalar")
+        pick_words(0)
+        u_words["r"] = deal_words("r")
+        u_words["n"] = deal_words("n")
+        pick_words(1)
         nc.vector.tensor_scalar(minus_bias_z[:], bias["z"][:], -1.0, None, ALU.mult)
+        pick_scales(0)
+        pick_scales(1)
+        x_mx[0] = quantise("x_0", x_grouped[0][:], HALF, on="table_scales")
+        u_scales["r"] = deal_scales("r")
+        quantise_w("r", 0, on="u_scales_raw_r")
+        quantise_w("r", 1, on="w_grouped_r0")
+        round_w("n", 0, "scalar")
+        u_scales["n"] = deal_scales("n")
+        w_grouped["n", 1] = placed("w_grouped_n1", [P, 2 * P * PACK], BF16, 10752)
+        round_w("n", 1, "vector")
+        quantise_w("n", 0, on=12800)
+        quantise_w("n", 1)
 
         def message_pass(acc, g, t, c, start, stop):
-            cols = slice(t * P, (t + 1) * P)
             nc.tensor.matmul_mx(
-                out=acc[:], lhsT=w_mx[g][0][:, cols].bitcast(FP8X4), lhsT_scale=w_mx[g][1][:, cols],
+                out=acc[:], lhsT=w_mx[g, t][0].bitcast(FP8X4), lhsT_scale=w_mx[g, t][1],
                 rhs=x_mx[c][0][:].bitcast(FP8X4), rhs_scale=x_mx[c][1][:], start=start, stop=stop,
             )
 
         def state_pass(acc, g, t, c, start, stop):
             nc.tensor.matmul_mx(
-                out=acc[:], lhsT=u_mx[g][0][:, 2 * t * P : 2 * (t + 1) * P].bitcast(FP4X4),
-                lhsT_scale=u_mx[g][1][:, t * P : (t + 1) * P],
+                out=acc[:], lhsT=u_words[g][:, 2 * t * P : 2 * (t + 1) * P].bitcast(FP4X4),
+                lhsT_scale=u_scales[g][:, t * P : (t + 1) * P],
                 rhs=picked_words[c][:].bitcast(FP8X4), rhs_scale=picked_scales[c][:], start=start, stop=stop,
             )
 
-        units = [(0, 0), (0, 1), (1, 0), (1, 1), (2, 0), (2, 1), (3, 0), (3, 1)]
+        units = [(t, c) for t in range(PACK) for c in range(HALVES)]
+
+        def slot(u):
+            return {1: 2, 2: 1}.get(u, u)
 
         def ring(name, count, first_on=None):
             tiles = [held("%s_%d" % (name, i), [P, HALF], F32, first_on if i == 0 else None) for i in range(count)]
             return lambda u: tiles[u % count][:]
 
-        def bank_ring(name):
+        def bank_ring(name, turn):
             tiles = [psum.tile([P, HALF], F32, name="%s_%d" % (name, i)) for i in range(2)]
-            return lambda u: tiles[u % 2]
+            return lambda u: tiles[turn(u) % 2]
 
-        sr, hn, xn, sz = bank_ring("sr"), bank_ring("hn"), bank_ring("xn"), bank_ring("sz")
-        reset, keep_gate = ring("reset", 2), ring("keep_gate", 4)
-        cand, moved, updated = ring("cand", 3, first_on="w_raw_z"), ring("moved", 1), ring("updated", 2)
+        sr, hn, xn, sz = bank_ring("sr", slot), bank_ring("hn", slot), bank_ring("xn", slot), bank_ring("sz", int)
+        keep_gate, later_cand = ring("keep_gate", 4), ring("cand", 2)
+        later_updated = ring("updated", 2)
+        first_updated = held("first_updated", [P, HALF], F32)
+        placed_late = {}
+        first_cand = held("first_cand", [P, HALF], F32)
+        early_moved = [held("early_moved_0", [P, HALF], F32)]
+        reset_pair = shared.tile([P, 2, HALF], F32, name="reset_pair", align_bytes=64, offset=0)
+        x_grouped.append(shared.tile([P, HALF * PACK], BF16, name="x_grouped_1", align_bytes=64, offset=4096))
+        second_sum = []
 
-        def products(u):
+        def updated(u):
+            return first_updated[:] if u == 0 else later_updated(u)
+
+        def scaled(u):
+            return placed_late["moved"][:] if u == 1 else moved(u)
+
+        def moved(u):
+            return early_moved[u][:] if u < 2 else placed_late["moved"][:]
+
+        def cand(u):
+            return first_cand[:] if u == 0 else later_cand(u)
+
+        def summed(u):
+            return second_sum[0][:] if u == 1 else cand(u)
+
+        def reset(u):
+            return reset_pair[:, slot(u) % 2, :]
+
+        def reset_gate(u):
             t, c = units[u]
             state_pass(sr(u), "r", t, c, True, False)
             message_pass(sr(u), "r", t, c, False, True)
+            nc.scalar.activation(reset(u), sr(u)[:], ACT.Sigmoid, bias=bias["r"][:, t : t + 1])
+
+        def products(u):
+            t, c = units[u]
             state_pass(hn(u), "n", t, c, True, True)
             message_pass(xn(u), "n", t, c, True, True)
-            nc.scalar.activation(reset(u), sr(u)[:], ACT.Sigmoid, bias=bias["r"][:, t : t + 1])
 
         def update_gate(u):
             t, c = units[u]
@@ -213,22 +269,18 @@ def tile_list_tgn_gruP_kernel(
             nc.scalar.activation(keep_gate(u), sz(u)[:], ACT.Sigmoid, bias=minus_bias_z[:, t : t + 1], scale=-1.0)
 
         def reset_state(u):
-            nc.vector.tensor_tensor(cand(u), hn(u)[:], reset(u), ALU.mult)
+            nc.vector.tensor_tensor(summed(u), hn(u)[:], reset(u), ALU.mult)
 
         def candidate(u):
             t, c = units[u]
-            nc.vector.tensor_tensor(cand(u), xn(u)[:], cand(u), ALU.add)
-            nc.scalar.activation(cand(u), cand(u), ACT.Tanh, bias=bias["n"][:, t : t + 1])
-
-        def looked_up(u):
-            t, c = units[u]
-            return state[t][:].indirect(listed(c))
+            nc.vector.tensor_tensor(summed(u), xn(u)[:], summed(u), ALU.add)
+            nc.scalar.activation(cand(u), summed(u), ACT.Tanh, bias=bias["n"][:, t : t + 1])
 
         def gate(engine, u):
-            engine.tensor_tensor(moved(u), moved(u), keep_gate(u), ALU.mult)
+            engine.tensor_tensor(scaled(u), moved(u), keep_gate(u), ALU.mult)
 
         def combine(engine, u):
-            engine.tensor_tensor(updated(u), moved(u), cand(u), ALU.add)
+            engine.tensor_tensor(updated(u), scaled(u), cand(u), ALU.add)
 
         def weigh(engine, u):
             c = units[u][1]
@@ -240,7 +292,7 @@ def tile_list_tgn_gruP_kernel(
         out_rows = out_0.rearrange("(p t) c -> p t c", t=PACK)
 
         def round_y(t, k, engine):
-            source = result[t][:, k * CHUNK : (k + 1) * CHUNK]
+            source = pages[t % PAGES][:, k * CHUNK : (k + 1) * CHUNK]
             if t == PACK - 2 and k in VECTOR_CHUNKS:
                 copy_on(engine, y_grouped[k][:, :, t : t + 2], source.unsqueeze(2).to_broadcast([P, CHUNK, 2]))
             else:
@@ -248,64 +300,78 @@ def tile_list_tgn_gruP_kernel(
 
         def place(u):
             t, c = units[u]
-            if u < len(units) - 1:
-                nc.vector.tensor_copy(result[t][:].indirect(listed(c)), updated(u))
+            page = pages[t % PAGES]
+            if u == 0:
+                nc.vector.tensor_copy(page[:].indirect(listed(c)), first_weighed[:])
+            elif u < len(units) - 1:
+                nc.vector.tensor_copy(page[:].indirect(listed(c)), updated(u))
             else:
-                nc.vector.tensor_tensor(result[t][:].indirect(listed(c)), updated(u), event_weight[c][:], ALU.mult)
+                nc.vector.tensor_tensor(page[:].indirect(listed(c)), updated(u), event_weight[c][:], ALU.mult)
             if c == HALVES - 1:
-                nc.sync.dma_start(out_rows[:, t, :], result[t][:])
-                for k in (1, 2, 0, 3):
-                    round_y(t, k, "vector" if t == PACK - 1 and k in VECTOR_CHUNKS else "scalar")
+                nc.sync.dma_start(out_rows[:, t, :], page[:])
 
         def difference(u):
-            nc.vector.tensor_tensor(moved(u), looked_up(u), cand(u), ALU.subtract)
-
-        def prepare(u):
-            products(u)
-            reset_state(u)
-            candidate(u)
+            t, c = units[u]
+            nc.vector.tensor_tensor(moved(u), state[t][:].indirect(listed(c)), cand(u), ALU.subtract)
 
         last = len(units) - 1
-        prepare(0)
-        u_mx["z"] = deal_u("z")
-        w_mx["z"] = quantise("w_z", w_grouped_z, N, on="u_scales_raw_z")
-        update_gate(0)
-        x_mx[1] = (held("x_1_codes", [P, HALF], U32), held("x_1_scales", [P, HALF], U8))
-        quarter = HALF // 2
-        x_parts = []
-        for i in range(2):
-            part = reused.tile([P, quarter * PACK], BF16, name="x_part_%d" % i, align_bytes=64, offset=i * T * 4)
-            nc.vector.tensor_copy(
-                part[:].rearrange("p (c i j) -> p c j i", i=4, j=PACK),
-                x_raw[1][:, :, i * quarter : (i + 1) * quarter].rearrange("p j (c i) -> p c j i", i=4),
-            )
-            x_parts.append(part)
-        for i in range(2):
-            cols = slice(i * quarter, (i + 1) * quarter)
-            nc.vector.quantize_mx(out=x_mx[1][0][:, cols].bitcast(FP8X4), scales=x_mx[1][1][:, cols], in_=x_parts[i][:])
-        for i in range(2):
-            result.append(reused.tile([P, T], F32, name="result_%d" % (2 + i), align_bytes=64, offset=i * T * 4))
-            nc.gpsimd.memset(result[2 + i][:].bitcast(I32), 0)
+        reset_gate(0)
+        round_x(x_grouped[1], 1, "scalar", slice(0, P // 2))
+        round_x(x_grouped[1], 1, "vector", slice(P // 2, P))
+        reset_gate(2)
+        products(0)
+        products(2)
+        reset_state(0)
+        x_mx[1] = quantise("x_1", x_grouped[1][:], HALF)
+        candidate(0)
+        reset_gate(1)
+        reset_state(2)
+        candidate(2)
+        products(1)
         difference(0)
-        for u in range(1, 3):
-            prepare(u)
-            update_gate(u)
-        for u in range(last + 1):
-            engine = nc.vector if u == 0 else nc.gpsimd
-            gate(engine, u)
-            combine(engine, u)
+        u_words["z"] = deal_words("z", on=6144)
+        u_scales["z"] = deal_scales("z")
+        second_sum.append(placed("second_sum", [P, HALF], F32, 8192))
+        reset_state(1)
+        candidate(1)
+        round_w("z", 0, "scalar")
+        quantise_w("z", 0, on=10240)
+        early_moved.append(held("early_moved_1", [P, HALF], F32, on="w_grouped_z0"))
+        update_gate(0)
+        update_gate(1)
+        round_w("z", 1, "scalar")
+        difference(1)
+        gate(nc.vector, 0)
+        combine(nc.vector, 0)
+        quantise_w("z", 1)
+        first_weighed = placed("first_weighed", [P, HALF], F32, 8192)
+        nc.vector.tensor_tensor(first_weighed[:], updated(0), event_weight[0][:], ALU.mult)
+        placed_late["moved"] = held("moved", [P, HALF], F32, on="first_updated")
+        update_gate(2)
+        reset_gate(3)
+        products(3)
+        update_gate(3)
+        place(0)
+        for u in range(1, last + 1):
+            gate(nc.gpsimd, u)
+            combine(nc.gpsimd, u)
             if u < last:
                 weigh(nc.gpsimd, u)
-            ahead = u + 3
-            if ahead <= last:
-                products(ahead)
-                update_gate(ahead)
-                reset_state(ahead)
+            if u + 2 <= last:
+                reset_state(u + 2)
             if u + 1 <= last:
                 difference(u + 1)
-            if ahead <= last:
-                candidate(ahead)
+            if u + 2 <= last:
+                candidate(u + 2)
+            if u + 3 <= last:
+                reset_gate(u + 3)
+                products(u + 3)
+                update_gate(u + 3)
+            for t, k in ROUNDS.get(u, []):
+                round_y(t, k, "scalar")
             place(u)
+        for k in (1, 2, 0, 3):
+            round_y(PACK - 1, k, "vector" if k in VECTOR_CHUNKS else "scalar")
 
         out_words = out_1[0].rearrange("p c i -> p (c i)").bitcast(I32)
         for k in range(CHUNKS):

@@ -1,6 +1,7 @@
 from contextlib import ExitStack
 
 import concourse.mybir as mybir
+from concourse.masks import make_identity
 
 K, M, N, T, J = 512, 512, 512, 2048, 1024
 FLOPS = 6 * 2 * 512 * N * J
@@ -20,11 +21,10 @@ P = 128
 PACK = 4
 HALF = 512
 HALVES = J // HALF
-CHUNK = 512
-CHUNKS = T // CHUNK
-VECTOR_CHUNKS = (1, 2)
-PAGES = 2
-ROUNDS = {4: [(0, 0), (0, 1), (0, 2), (0, 3)], 6: [(1, 0), (1, 1), (1, 2), (1, 3)], 7: [(2, 1), (2, 2), (2, 0), (2, 3)]}
+BLOCKS = N // P
+SPAN = 2 * P
+QUARTER = T // 4
+PAGES = 3
 
 
 def tile_list_tgn_gruP_kernel(
@@ -43,6 +43,9 @@ def tile_list_tgn_gruP_kernel(
         def placed(name, shape, dtype, offset):
             return shared.tile(shape, dtype, name=name, align_bytes=64, offset=offset)
 
+        def bank(name, on=None):
+            return psum.tile([P, HALF], F32, name=name, tag=on or name)
+
         offsets = keep.tile([P, J // 16], U16, name="offsets")
         table_words = held("table_words", [P, T], I32)
         table_scales = held("table_scales", [P, T], U8)
@@ -51,16 +54,18 @@ def tile_list_tgn_gruP_kernel(
         u_words_dram = {"r": ur_words, "n": un_words, "z": uz_words}
         u_scales_dram = {"r": ur_scales, "n": un_scales, "z": uz_scales}
         bias_dram = {"r": br, "n": bn, "z": bz}
-        w_raw = {g: held("w_raw_" + g, [P, PACK, N], F32) for g in gates}
-        u_words_raw = {g: held("u_words_raw_" + g, [P, 2 * N], U8) for g in gates}
-        u_scales_raw = {g: held("u_scales_raw_" + g, [P, N], U8) for g in ("r",)}
-        u_scales_raw["n"] = placed("u_scales_raw_n", [P, N], U8, 12800 - 256)
-        u_scales_raw["z"] = placed("u_scales_raw_z", [P, N], U8, 10240 - 256)
-        bias = {g: held("bias_" + g, [P, PACK], F32) for g in gates}
+        w_raw = {
+            (g, s): held("w_raw_%s%d" % (g, s), [P, PACK, SPAN], F32) for g in gates for s in range(2) if (g, s) != ("n", 0)
+        }
+        w_raw["n", 0] = placed("w_raw_n0", [P, PACK, SPAN], F32, 12288)
+        u_words = {g: held("u_words_" + g, [P, 2 * N], U8) for g in gates}
+        u_scales = {g: held("u_scales_" + g, [P, N], U8) for g in gates}
+        bias = {g: held("bias_" + g, [P, BLOCKS], F32) for g in gates}
         x_raw = [held("x_raw_%d" % c, [P, PACK, HALF], F32) for c in range(HALVES)]
-        state = [held("state_%d" % t, [P, T], F32) for t in range(PACK)]
+        state = [held("state_%d" % b, [P, T], F32) for b in range(BLOCKS)]
         event_weight = [held("event_weight_%d" % c, [P, HALF], F32) for c in range(HALVES)]
         pages = [held("page_%d" % i, [P, T], F32) for i in range(PAGES)]
+        identity = held("identity", [P, P], F32)
 
         warm = held("warm", [P, 8], F32)
         warm_out = held("warm_out", [P, 8], F32)
@@ -68,9 +73,11 @@ def tile_list_tgn_gruP_kernel(
         nc.scalar.activation(warm_out[:], warm[:], ACT.Sigmoid)
         nc.gpsimd.memset(table_scales[:].bitcast(I32), 0)
         for g in gates:
-            nc.gpsimd.memset(u_scales_raw[g][:].bitcast(I32), 0)
-        for page in pages:
+            nc.gpsimd.memset(u_scales[g][:].bitcast(I32), 0)
+        make_identity(nc, identity[:])
+        for page in pages[:2]:
             nc.vector.memset(page[:].bitcast(I32), 0)
+        nc.gpsimd.memset(pages[2][:].bitcast(I32), 0)
 
         def load_scale_rows(tile, dram):
             for q in range(4):
@@ -79,47 +86,52 @@ def tile_list_tgn_gruP_kernel(
         def load_rows(tile, dram):
             nc.sync.dma_start(tile[:], dram.rearrange("(p j) c -> p j c", j=PACK))
 
+        def load_w(g, s):
+            load_rows(w_raw[g, s], w_dram[g][:, s * SPAN : (s + 1) * SPAN])
+
         def load_u_words(g):
-            nc.sync.dma_start(u_words_raw[g][:].bitcast(I32), u_words_dram[g][0].bitcast(I32))
+            nc.sync.dma_start(u_words[g][:].bitcast(I32), u_words_dram[g][0].bitcast(I32))
 
         def load_bias(g):
-            nc.sync.dma_start(bias[g][:], bias_dram[g].rearrange("(p t) -> p t", t=PACK))
+            with nc.allow_non_contiguous_dma(reason="one bias value a partition and row block"):
+                nc.sync.dma_start(bias[g][:], bias_dram[g].rearrange("(b q) -> q b", q=P))
 
-        def load_state(t):
-            nc.sync.dma_start(state[t][:], hT.rearrange("(p t) c -> p t c", t=PACK)[:, t, :])
+        def load_state(b):
+            nc.sync.dma_start(state[b][:], hT[b * P : (b + 1) * P, :])
 
         nc.sync.dma_start(offsets[:], offs)
         nc.sync.dma_start(table_words[:], tab_words[0].rearrange("p c i -> p (c i)").bitcast(I32))
-        load_u_words("r")
-        load_u_words("n")
-        for g in gates:
-            load_bias(g)
         load_rows(x_raw[0], x[:, 0:HALF])
         load_scale_rows(table_scales, tab_scales)
-        load_rows(w_raw["r"], wr)
-        load_scale_rows(u_scales_raw["r"], ur_scales)
-        load_rows(w_raw["n"], wn)
-        load_scale_rows(u_scales_raw["n"], un_scales)
+        load_w("r", 0)
+        load_u_words("r")
+        load_w("n", 0)
+        load_scale_rows(u_scales["r"], ur_scales)
         load_rows(x_raw[1], x[:, HALF:J])
+        load_u_words("n")
+        load_scale_rows(u_scales["n"], un_scales)
+        load_bias("r")
         load_state(0)
+        load_bias("n")
+        load_w("z", 0)
         load_u_words("z")
-        load_scale_rows(u_scales_raw["z"], uz_scales)
-        load_rows(w_raw["z"], wz)
-        nc.sync.dma_start(event_weight[0][:], wgo[:, 0:HALF])
-        nc.sync.dma_start(event_weight[1][:], wgo[:, HALF:J])
-        for t in range(1, PACK):
-            load_state(t)
+        load_scale_rows(u_scales["z"], uz_scales)
+        load_bias("z")
+        for g in gates:
+            load_w(g, 1)
+        for c in range(HALVES):
+            nc.sync.dma_start(event_weight[c][:], wgo[:, c * HALF : (c + 1) * HALF])
+        for b in range(1, BLOCKS):
+            load_state(b)
 
         def listed(c):
             return offsets[:, c * (HALF // 16) : (c + 1) * (HALF // 16)]
 
         picked_words = [held("picked_words_%d" % c, [P, HALF], U32) for c in range(HALVES)]
         picked_scales = [held("picked_scales_%d" % c, [P, HALF], U8) for c in range(HALVES)]
-
-        def pick_words(c):
+        for c in range(HALVES):
             nc.vector.tensor_copy(picked_words[c][:], table_words[:].bitcast(U32).indirect(listed(c)))
-
-        def pick_scales(c):
+        for c in range(HALVES):
             nc.vector.tensor_copy(picked_scales[c][:], table_scales[:].indirect(listed(c)))
 
         def copy_on(engine, out, in_):
@@ -128,153 +140,138 @@ def tile_list_tgn_gruP_kernel(
             else:
                 nc.vector.tensor_copy(out, in_)
 
+        def round_rows(grouped, raw, engine):
+            copy_on(
+                engine,
+                grouped.rearrange("p (c i j) -> p c j i", i=4, j=PACK),
+                raw.rearrange("p j (c i) -> p c j i", i=4),
+            )
+
         def quantise(name, grouped, width, on=None):
             codes = held(name + "_codes", [P, width], U32)
-            scales = placed(name + "_scales", [P, width], U8, on) if isinstance(on, int) else held(name + "_scales", [P, width], U8, on)
+            scales = held(name + "_scales", [P, width], U8, on)
             nc.vector.quantize_mx(out=codes[:].bitcast(FP8X4), scales=scales[:], in_=grouped)
             return codes, scales
 
-        def round_x(grouped, c, engine, part):
-            copy_on(
-                engine,
-                grouped[:].rearrange("p (c i j) -> p c j i", i=4, j=PACK)[:, part],
-                x_raw[c][:].rearrange("p j (c i) -> p c j i", i=4)[:, part],
-            )
-
-        def round_w(g, pair, engine):
-            copy_on(
-                engine,
-                w_grouped[g, pair][:].rearrange("p (t m j) -> p m j t", t=2, j=PACK),
-                w_raw[g][:].rearrange("p j (m t) -> p m j t", t=PACK)[:, :, :, 2 * pair : 2 * pair + 2],
-            )
-
-        def deal_words(g, on=None):
-            words = placed("u_words_z", [P, 2 * N], U8, on) if on else held("u_words_" + g, [P, 2 * N], U8)
-            nc.vector.tensor_copy(
-                words[:].bitcast(U16).rearrange("p (t m) -> p t m", t=PACK),
-                u_words_raw[g][:].bitcast(U16).rearrange("p (m t) -> p t m", t=PACK),
-            )
-            return words
-
-        def deal_scales(g, on=None):
-            scales = held("u_scales_" + g, [P, N], U8, on)
-            nc.vector.tensor_copy(
-                scales[:].rearrange("p (t m) -> p t m", t=PACK),
-                u_scales_raw[g][:].rearrange("p (m t) -> p t m", t=PACK),
-            )
-            return scales
-
-        x_mx, w_mx, u_words, u_scales = {}, {}, {}, {}
-        minus_bias_z = held("minus_bias_z", [P, PACK], F32)
+        x_mx, w_mx = {}, {}
         x_grouped = [held("x_grouped_0", [P, HALF * PACK], BF16)]
-        w_grouped = {key: held("w_grouped_%s%d" % key, [P, 2 * P * PACK], BF16) for key in (("r", 0), ("r", 1), ("z", 0), ("z", 1))}
-        w_grouped["n", 0] = shared.tile([P, 2 * P * PACK], BF16, name="w_grouped_n0", align_bytes=64, offset=3072)
+        w_grouped = {g: held("w_grouped_" + g, [P, SPAN * PACK], BF16) for g in ("r", "n")}
 
-        def quantise_w(g, pair, on=None):
-            codes, scales = quantise("w_%s%d" % (g, pair), w_grouped[g, pair][:], 2 * P, on)
-            for t in range(2):
-                w_mx[g, 2 * pair + t] = (codes[:, t * P : (t + 1) * P], scales[:, t * P : (t + 1) * P])
+        def quantise_w(g, on=None):
+            codes, scales = quantise("w_" + g, w_grouped[g][:], SPAN, on)
+            for b in range(2):
+                w_mx[g, b] = (codes[:, b * P : (b + 1) * P], scales[:, b * P : (b + 1) * P])
 
-        round_x(x_grouped[0], 0, "scalar", slice(0, P))
-        round_w("r", 0, "scalar")
-        round_w("r", 1, "scalar")
-        pick_words(0)
-        u_words["r"] = deal_words("r")
-        u_words["n"] = deal_words("n")
-        pick_words(1)
-        nc.vector.tensor_scalar(minus_bias_z[:], bias["z"][:], -1.0, None, ALU.mult)
-        pick_scales(0)
-        pick_scales(1)
+        across = [bank("across_%d" % i) for i in range(2)]
+        back = [bank("back_%d" % i) for i in range(2)]
+        minus_bias_z = held("minus_bias_z", [P, BLOCKS], F32)
+
+        round_rows(x_grouped[0][:], x_raw[0][:], "scalar")
+        round_rows(w_grouped["r"][:], w_raw["r", 0][:], "scalar")
+        round_rows(w_grouped["n"][:], w_raw["n", 0][:], "scalar")
         x_mx[0] = quantise("x_0", x_grouped[0][:], HALF, on="table_scales")
-        u_scales["r"] = deal_scales("r")
-        quantise_w("r", 0, on="u_scales_raw_r")
-        quantise_w("r", 1, on="w_grouped_r0")
-        round_w("n", 0, "scalar")
-        u_scales["n"] = deal_scales("n")
-        w_grouped["n", 1] = placed("w_grouped_n1", [P, 2 * P * PACK], BF16, 10752)
-        round_w("n", 1, "vector")
-        quantise_w("n", 0, on=12800)
-        quantise_w("n", 1)
+        quantise_w("r", on="x_grouped_0")
+        quantise_w("n", on="w_grouped_r")
 
-        def message_pass(acc, g, t, c, start, stop):
+        def message_pass(acc, g, b, c, start, stop):
             nc.tensor.matmul_mx(
-                out=acc[:], lhsT=w_mx[g, t][0].bitcast(FP8X4), lhsT_scale=w_mx[g, t][1],
+                out=acc[:], lhsT=w_mx[g, b][0].bitcast(FP8X4), lhsT_scale=w_mx[g, b][1],
                 rhs=x_mx[c][0][:].bitcast(FP8X4), rhs_scale=x_mx[c][1][:], start=start, stop=stop,
             )
 
-        def state_pass(acc, g, t, c, start, stop):
+        def state_pass(acc, g, b, c, start, stop):
             nc.tensor.matmul_mx(
-                out=acc[:], lhsT=u_words[g][:, 2 * t * P : 2 * (t + 1) * P].bitcast(FP4X4),
-                lhsT_scale=u_scales[g][:, t * P : (t + 1) * P],
+                out=acc[:], lhsT=u_words[g][:, 2 * b * P : 2 * (b + 1) * P].bitcast(FP4X4),
+                lhsT_scale=u_scales[g][:, b * P : (b + 1) * P],
                 rhs=picked_words[c][:].bitcast(FP8X4), rhs_scale=picked_scales[c][:], start=start, stop=stop,
             )
 
-        units = [(t, c) for t in range(PACK) for c in range(HALVES)]
+        units = [(b, c) for b in range(BLOCKS) for c in range(HALVES)]
 
         def slot(u):
             return {1: 2, 2: 1}.get(u, u)
 
-        def ring(name, count, first_on=None):
-            tiles = [held("%s_%d" % (name, i), [P, HALF], F32, first_on if i == 0 else None) for i in range(count)]
+        def ring(name, count):
+            tiles = [held("%s_%d" % (name, i), [P, HALF], F32) for i in range(count)]
             return lambda u: tiles[u % count][:]
 
-        def bank_ring(name, turn):
-            tiles = [psum.tile([P, HALF], F32, name="%s_%d" % (name, i)) for i in range(2)]
-            return lambda u: tiles[turn(u) % 2]
+        reset_bank, update_bank = bank("reset_bank"), bank("update_bank")
+        state_bank, message_bank = bank("state_bank"), bank("message_bank")
 
-        sr, hn, xn, sz = bank_ring("sr", slot), bank_ring("hn", slot), bank_ring("xn", slot), bank_ring("sz", int)
-        keep_gate, later_cand = ring("keep_gate", 4), ring("cand", 2)
-        later_updated = ring("updated", 2)
-        first_updated = held("first_updated", [P, HALF], F32)
-        placed_late = {}
+        def sr(u):
+            return message_bank if u == 2 else reset_bank
+
+        def hn(u):
+            return across[0] if u == 2 else state_bank
+
+        def xn(u):
+            return reset_bank if u == 0 else message_bank
+
+        def sz(u):
+            return update_bank
+
+        later_keep_gate, later_updated = ring("keep_gate", 3), ring("updated", 2)
+        later_reset = ring("reset", 2)
+        own_reset = {
+            0: placed("first_reset", [P, HALF], F32, 12288), 2: placed("third_reset", [P, HALF], F32, 14336),
+        }
         first_cand = held("first_cand", [P, HALF], F32)
-        early_moved = [held("early_moved_0", [P, HALF], F32)]
-        reset_pair = shared.tile([P, 2, HALF], F32, name="reset_pair", align_bytes=64, offset=0)
-        x_grouped.append(shared.tile([P, HALF * PACK], BF16, name="x_grouped_1", align_bytes=64, offset=4096))
-        second_sum = []
+        first_moved = held("first_moved", [P, HALF], F32)
+        first_updated = held("first_updated", [P, HALF], F32)
+        early_sum = {0: held("first_sum", [P, HALF], F32), 1: placed("second_sum", [P, HALF], F32, 1024), 2: held("third_sum", [P, HALF], F32)}
+        later = {}
+
+        def reset(u):
+            return own_reset[u][:] if u in own_reset else later_reset(u)
+
+        def keep_gate(u):
+            return later["keep_gate"][:] if u == 0 else later_keep_gate(u)
+
+        def cand(u):
+            return first_cand[:] if u == 0 else later["cand"][:, u % 2, :]
+
+        def summed(u):
+            return early_sum[u][:] if u in early_sum else cand(u)
+
+        def moved(u):
+            return first_moved[:] if u == 0 else later["second_moved"][:] if u == 1 else later["moved"][:]
+
+        def scaled(u):
+            return later["moved"][:] if u == 1 else moved(u)
 
         def updated(u):
             return first_updated[:] if u == 0 else later_updated(u)
 
-        def scaled(u):
-            return placed_late["moved"][:] if u == 1 else moved(u)
-
-        def moved(u):
-            return early_moved[u][:] if u < 2 else placed_late["moved"][:]
-
-        def cand(u):
-            return first_cand[:] if u == 0 else later_cand(u)
-
-        def summed(u):
-            return second_sum[0][:] if u == 1 else cand(u)
-
-        def reset(u):
-            return reset_pair[:, slot(u) % 2, :]
-
         def reset_gate(u):
-            t, c = units[u]
-            state_pass(sr(u), "r", t, c, True, False)
-            message_pass(sr(u), "r", t, c, False, True)
-            nc.scalar.activation(reset(u), sr(u)[:], ACT.Sigmoid, bias=bias["r"][:, t : t + 1])
+            b, c = units[u]
+            state_pass(sr(u), "r", b, c, True, False)
+            message_pass(sr(u), "r", b, c, False, True)
+            nc.scalar.activation(reset(u), sr(u)[:], ACT.Sigmoid, bias=bias["r"][:, b : b + 1])
 
         def products(u):
-            t, c = units[u]
-            state_pass(hn(u), "n", t, c, True, True)
-            message_pass(xn(u), "n", t, c, True, True)
+            b, c = units[u]
+            state_pass(hn(u), "n", b, c, True, True)
+            message_pass(xn(u), "n", b, c, True, True)
 
         def update_gate(u):
-            t, c = units[u]
-            state_pass(sz(u), "z", t, c, True, False)
-            message_pass(sz(u), "z", t, c, False, True)
-            nc.scalar.activation(keep_gate(u), sz(u)[:], ACT.Sigmoid, bias=minus_bias_z[:, t : t + 1], scale=-1.0)
+            b, c = units[u]
+            state_pass(sz(u), "z", b, c, True, False)
+            message_pass(sz(u), "z", b, c, False, True)
+            nc.scalar.activation(keep_gate(u), sz(u)[:], ACT.Sigmoid, bias=minus_bias_z[:, b : b + 1], scale=-1.0)
 
         def reset_state(u):
             nc.vector.tensor_tensor(summed(u), hn(u)[:], reset(u), ALU.mult)
 
-        def candidate(u):
-            t, c = units[u]
+        def candidate_sum(u):
             nc.vector.tensor_tensor(summed(u), xn(u)[:], summed(u), ALU.add)
-            nc.scalar.activation(cand(u), summed(u), ACT.Tanh, bias=bias["n"][:, t : t + 1])
+
+        def candidate_tanh(u):
+            b = units[u][0]
+            nc.scalar.activation(cand(u), summed(u), ACT.Tanh, bias=bias["n"][:, b : b + 1])
+
+        def difference(u):
+            b, c = units[u]
+            nc.vector.tensor_tensor(moved(u), state[b][:].indirect(listed(c)), cand(u), ALU.subtract)
 
         def gate(engine, u):
             engine.tensor_tensor(scaled(u), moved(u), keep_gate(u), ALU.mult)
@@ -282,104 +279,164 @@ def tile_list_tgn_gruP_kernel(
         def combine(engine, u):
             engine.tensor_tensor(updated(u), scaled(u), cand(u), ALU.add)
 
-        def weigh(engine, u):
-            c = units[u][1]
-            engine.tensor_tensor(updated(u), updated(u), event_weight[c][:], ALU.mult)
-
-        y_grouped = [held("y_grouped_%d" % k, [P, CHUNK, PACK], BF16) for k in range(CHUNKS)]
-        y_codes = [held("y_codes_%d" % k, [P, CHUNK], U32) for k in range(CHUNKS)]
-        y_scales = held("y_scales", [P, T], U8)
-        out_rows = out_0.rearrange("(p t) c -> p t c", t=PACK)
-
-        def round_y(t, k, engine):
-            source = pages[t % PAGES][:, k * CHUNK : (k + 1) * CHUNK]
-            if t == PACK - 2 and k in VECTOR_CHUNKS:
-                copy_on(engine, y_grouped[k][:, :, t : t + 2], source.unsqueeze(2).to_broadcast([P, CHUNK, 2]))
-            else:
-                copy_on(engine, y_grouped[k][:, :, t], source)
+        def weigh(u):
+            nc.gpsimd.tensor_tensor(updated(u), updated(u), event_weight[units[u][1]][:], ALU.mult)
 
         def place(u):
-            t, c = units[u]
-            page = pages[t % PAGES]
+            b, c = units[u]
+            page = pages[b % PAGES]
             if u == 0:
-                nc.vector.tensor_copy(page[:].indirect(listed(c)), first_weighed[:])
+                nc.vector.tensor_copy(page[:].indirect(listed(c)), later["weighed"][:])
             elif u < len(units) - 1:
                 nc.vector.tensor_copy(page[:].indirect(listed(c)), updated(u))
             else:
                 nc.vector.tensor_tensor(page[:].indirect(listed(c)), updated(u), event_weight[c][:], ALU.mult)
             if c == HALVES - 1:
-                nc.sync.dma_start(out_rows[:, t, :], page[:])
+                nc.sync.dma_start(out_0[b * P : (b + 1) * P, :], page[:])
 
-        def difference(u):
-            t, c = units[u]
-            nc.vector.tensor_tensor(moved(u), state[t][:].indirect(listed(c)), cand(u), ALU.subtract)
+        y_pairs = [held("y_pairs_%d" % i, [P, HALF], BF16) for i in range(4)]
+        y_grouped = held("y_grouped", [P, BLOCKS, QUARTER * PACK], BF16)
+        out_words = out_1[0].rearrange("p c i -> p (c i)").bitcast(I32)
+
+        def turn_out(b, s, across, engine):
+            page = pages[b % PAGES]
+            for a in range(4):
+                first = a * QUARTER + s * P
+                nc.tensor.transpose(across[:, a * P : (a + 1) * P], page[:, first : first + P], identity[:])
+            copy_on(
+                engine,
+                y_pairs[s][:].rearrange("t (u r e) -> t u r e", u=2, e=2),
+                across[:].rearrange("t (r u e) -> t u r e", u=2, e=2),
+            )
+
+        def turn_back(s, target):
+            words = y_pairs[s][:].bitcast(F32)
+            for u in range(2):
+                first = (2 * (s % 2) + u) * P
+                nc.tensor.transpose(target[:, first : first + P], words[:, u * P : (u + 1) * P], identity[:])
+
+        def weave(b, pair, source, engine):
+            copy_on(
+                engine,
+                y_grouped[:, b, :].bitcast(F32)[:, pair * HALF : (pair + 1) * HALF].rearrange("r (s t u) -> r s t u", s=2, u=2),
+                source[:].rearrange("r (s u t) -> r s t u", s=2, u=2),
+            )
+
+        def regroup(b):
+            for s in range(4):
+                turn_out(b, s, across[s % 2], "scalar")
+            for pair in range(2):
+                turn_back(2 * pair, back[pair])
+                turn_back(2 * pair + 1, back[pair])
+                weave(b, pair, back[pair], "scalar")
+
+        y_scales = held("y_scales", [P, BLOCKS, QUARTER], U8)
 
         last = len(units) - 1
+        x_grouped.append(held("x_grouped_1", [P, HALF * PACK], BF16, on="w_grouped_n"))
+        round_rows(x_grouped[1][:], x_raw[1][:], "vector")
+        x_mx[1] = quantise("x_1", x_grouped[1][:], HALF)
         reset_gate(0)
-        round_x(x_grouped[1], 1, "scalar", slice(0, P // 2))
-        round_x(x_grouped[1], 1, "vector", slice(P // 2, P))
         reset_gate(2)
         products(0)
         products(2)
         reset_state(0)
-        x_mx[1] = quantise("x_1", x_grouped[1][:], HALF)
-        candidate(0)
-        reset_gate(1)
         reset_state(2)
-        candidate(2)
+        candidate_sum(0)
+        candidate_tanh(0)
+        w_grouped["z"] = held("w_grouped_z", [P, SPAN * PACK], BF16, on="first_sum")
+        round_rows(w_grouped["z"][:], w_raw["z", 0][:], "scalar")
+        reset_gate(1)
+        candidate_sum(2)
         products(1)
         difference(0)
-        u_words["z"] = deal_words("z", on=6144)
-        u_scales["z"] = deal_scales("z")
-        second_sum.append(placed("second_sum", [P, HALF], F32, 8192))
         reset_state(1)
-        candidate(1)
-        round_w("z", 0, "scalar")
-        quantise_w("z", 0, on=10240)
-        early_moved.append(held("early_moved_1", [P, HALF], F32, on="w_grouped_z0"))
+        candidate_sum(1)
+        later["cand"] = held("cand", [P, 2, HALF], F32, on="w_raw_z0")
+        candidate_tanh(1)
+        nc.vector.tensor_scalar(minus_bias_z[:], bias["z"][:], -1.0, None, ALU.mult)
+        quantise_w("z")
+        later["second_moved"] = held("second_moved", [P, HALF], F32, on="first_sum")
+        later["keep_gate"] = placed("first_keep_gate", [P, HALF], F32, 0)
         update_gate(0)
+        late_r = placed("late_r", [P, SPAN * PACK], BF16, 6144)
+        late_nz = placed("late_nz", [P, 2, SPAN * PACK], BF16, 2048)
+        round_rows(late_r[:], w_raw["r", 1][:], "scalar")
+        round_rows(late_nz[:, 0, :], w_raw["n", 1][:], "scalar")
+        round_rows(late_nz[:, 1, :], w_raw["z", 1][:], "scalar")
         update_gate(1)
-        round_w("z", 1, "scalar")
         difference(1)
         gate(nc.vector, 0)
+        codes_r, scales_r = quantise("late_r", late_r[:], SPAN)
         combine(nc.vector, 0)
-        quantise_w("z", 1)
-        first_weighed = placed("first_weighed", [P, HALF], F32, 8192)
-        nc.vector.tensor_tensor(first_weighed[:], updated(0), event_weight[0][:], ALU.mult)
-        placed_late["moved"] = held("moved", [P, HALF], F32, on="first_updated")
-        update_gate(2)
+        codes_nz, scales_nz = quantise("late_nz", late_nz[:].rearrange("p g c -> p (g c)"), 2 * SPAN)
+        for b in range(2):
+            cols = slice(b * P, (b + 1) * P)
+            w_mx["r", 2 + b] = (codes_r[:, cols], scales_r[:, cols])
+            w_mx["n", 2 + b] = (codes_nz[:, cols], scales_nz[:, cols])
+            cols = slice(SPAN + b * P, SPAN + (b + 1) * P)
+            w_mx["z", 2 + b] = (codes_nz[:, cols], scales_nz[:, cols])
+        later["weighed"] = placed("first_weighed", [P, HALF], F32, 5120)
+        nc.vector.tensor_tensor(later["weighed"][:], updated(0), event_weight[0][:], ALU.mult)
+        later["moved"] = held("moved", [P, HALF], F32, on="first_updated")
+        own_reset[3] = placed("fourth_reset", [P, HALF], F32, 0)
         reset_gate(3)
+        candidate_tanh(2)
         products(3)
+        update_gate(2)
         update_gate(3)
         place(0)
         for u in range(1, last + 1):
             gate(nc.gpsimd, u)
             combine(nc.gpsimd, u)
             if u < last:
-                weigh(nc.gpsimd, u)
+                weigh(u)
             if u + 2 <= last:
                 reset_state(u + 2)
             if u + 1 <= last:
                 difference(u + 1)
             if u + 2 <= last:
-                candidate(u + 2)
+                candidate_sum(u + 2)
+                candidate_tanh(u + 2)
             if u + 3 <= last:
                 reset_gate(u + 3)
                 products(u + 3)
                 update_gate(u + 3)
-            for t, k in ROUNDS.get(u, []):
-                round_y(t, k, "scalar")
+            if u == PAGES * HALVES:
+                regroup(0)
             place(u)
-        for k in (1, 2, 0, 3):
-            round_y(PACK - 1, k, "vector" if k in VECTOR_CHUNKS else "scalar")
 
-        out_words = out_1[0].rearrange("p c i -> p (c i)").bitcast(I32)
-        for k in range(CHUNKS):
-            cols = slice(k * CHUNK, (k + 1) * CHUNK)
+        final = BLOCKS - 1
+        for b in range(1, final):
+            regroup(b)
+        free_banks = [bank("final_%d" % s, on) for s, on in enumerate(("reset_bank", "update_bank", "state_bank", "message_bank"))]
+        engines = ("scalar", "vector")
+        for s in range(4):
+            turn_out(final, s, free_banks[s], engines[s % 2])
+        codes = held("y_codes", [P, final, QUARTER], U32, on="updated_%d" % (last % 2))
+        for blocks in (slice(0, 2), slice(2, 3)):
             nc.vector.quantize_mx(
-                out=y_codes[k][:].bitcast(FP8X4), scales=y_scales[:, cols],
-                in_=y_grouped[k][:].rearrange("p c i -> p (c i)"),
+                out=codes[:, blocks, :].rearrange("r b c -> r (b c)").bitcast(FP8X4),
+                scales=y_scales[:, blocks, :].rearrange("r b c -> r (b c)"),
+                in_=y_grouped[:, blocks, :].rearrange("r b c -> r (b c)"),
             )
-            nc.sync.dma_start(out_words[:, cols], y_codes[k][:].bitcast(I32))
-        for q in range(4):
-            nc.sync.dma_start(out_2[0, 4 * q : 4 * q + 4, :].bitcast(I32), y_scales[32 * q : 32 * q + 4, :].bitcast(I32))
+            for b in range(blocks.start, blocks.stop):
+                nc.sync.dma_start(
+                    out_words[32 * b : 32 * (b + 1), :].rearrange("p (a c) -> a p c", a=4), codes[:, b, :].bitcast(I32)
+                )
+        final_codes = [held("final_codes_%d" % pair, [P, SPAN], U32) for pair in range(2)]
+        final_words = out_words[32 * final : 32 * (final + 1), :].rearrange("p (a h c) -> h a p c", a=4, h=2)
+        for pair in range(2):
+            turn_back(2 * pair, back[pair])
+            turn_back(2 * pair + 1, back[pair])
+            weave(final, pair, back[pair], engines[pair])
+            nc.vector.quantize_mx(
+                out=final_codes[pair][:].bitcast(FP8X4), scales=y_scales[:, final, pair * SPAN : (pair + 1) * SPAN],
+                in_=y_grouped[:, final, pair * SPAN * PACK : (pair + 1) * SPAN * PACK],
+            )
+            nc.sync.dma_start(final_words[pair], final_codes[pair][:].bitcast(I32))
+        scale_rows = out_2[0].rearrange("(b r) t -> r b t", r=4)
+        for a in range(4):
+            nc.sync.dma_start(
+                scale_rows[:, :, a * QUARTER : (a + 1) * QUARTER].bitcast(I32), y_scales[32 * a : 32 * a + 4].bitcast(I32)
+            )

@@ -60,7 +60,7 @@ def tile_list_tgn_gruP_kernel(
         w_raw["n", 0] = placed("w_raw_n0", [P, PACK, SPAN], F32, 12288)
         u_words = {g: held("u_words_" + g, [P, 2 * N], U8) for g in gates}
         u_scales = {g: held("u_scales_" + g, [P, N], U8) for g in gates}
-        bias = {g: held("bias_" + g, [P, BLOCKS], F32) for g in gates}
+        bias_rows = held("bias_rows", [P, P], F32)
         x_raw = [held("x_raw_%d" % c, [P, PACK, HALF], F32) for c in range(HALVES)]
         state = [held("state_%d" % b, [P, T], F32) for b in range(BLOCKS)]
         event_weight = [held("event_weight_%d" % c, [P, HALF], F32) for c in range(HALVES)]
@@ -71,13 +71,13 @@ def tile_list_tgn_gruP_kernel(
         warm_out = held("warm_out", [P, 8], F32)
         nc.vector.memset(warm[:], 0.0)
         nc.scalar.activation(warm_out[:], warm[:], ACT.Sigmoid)
+        nc.gpsimd.memset(bias_rows[:], 0.0)
         nc.gpsimd.memset(table_scales[:].bitcast(I32), 0)
         for g in gates:
             nc.gpsimd.memset(u_scales[g][:].bitcast(I32), 0)
         make_identity(nc, identity[:])
-        for page in pages[:2]:
+        for page in pages:
             nc.vector.memset(page[:].bitcast(I32), 0)
-        nc.gpsimd.memset(pages[2][:].bitcast(I32), 0)
 
         def load_scale_rows(tile, dram):
             for q in range(4):
@@ -92,15 +92,13 @@ def tile_list_tgn_gruP_kernel(
         def load_u_words(g):
             nc.sync.dma_start(u_words[g][:].bitcast(I32), u_words_dram[g][0].bitcast(I32))
 
-        def load_bias(g):
-            with nc.allow_non_contiguous_dma(reason="one bias value a partition and row block"):
-                nc.sync.dma_start(bias[g][:], bias_dram[g].rearrange("(b q) -> q b", q=P))
-
         def load_state(b):
             nc.sync.dma_start(state[b][:], hT[b * P : (b + 1) * P, :])
 
         nc.sync.dma_start(offsets[:], offs)
         nc.sync.dma_start(table_words[:], tab_words[0].rearrange("p c i -> p (c i)").bitcast(I32))
+        for i, g in enumerate(gates):
+            nc.sync.dma_start(bias_rows[32 * i : 32 * i + BLOCKS, :], bias_dram[g].rearrange("(b q) -> b q", q=P))
         load_rows(x_raw[0], x[:, 0:HALF])
         load_scale_rows(table_scales, tab_scales)
         load_w("r", 0)
@@ -110,15 +108,13 @@ def tile_list_tgn_gruP_kernel(
         load_rows(x_raw[1], x[:, HALF:J])
         load_u_words("n")
         load_scale_rows(u_scales["n"], un_scales)
-        load_bias("r")
+        load_w("r", 1)
+        load_w("n", 1)
         load_state(0)
-        load_bias("n")
         load_w("z", 0)
         load_u_words("z")
         load_scale_rows(u_scales["z"], uz_scales)
-        load_bias("z")
-        for g in gates:
-            load_w(g, 1)
+        load_w("z", 1)
         for c in range(HALVES):
             nc.sync.dma_start(event_weight[c][:], wgo[:, c * HALF : (c + 1) * HALF])
         for b in range(1, BLOCKS):
@@ -164,7 +160,11 @@ def tile_list_tgn_gruP_kernel(
 
         across = [bank("across_%d" % i) for i in range(2)]
         back = [bank("back_%d" % i) for i in range(2)]
+        bias = held("bias", [P, 2 * BLOCKS], F32)
         minus_bias_z = held("minus_bias_z", [P, BLOCKS], F32)
+        nc.tensor.transpose(back[1][:, 0:P], bias_rows[:], identity[:])
+        nc.scalar.copy(bias[:].rearrange("q (g b) -> q g b", g=2), back[1][:, 0:64].rearrange("q (g b) -> q g b", g=2)[:, :, 0:BLOCKS])
+        nc.scalar.activation(minus_bias_z[:], back[1][:, 64 : 64 + BLOCKS], ACT.Copy, scale=-1.0)
 
         round_rows(x_grouped[0][:], x_raw[0][:], "scalar")
         round_rows(w_grouped["r"][:], w_raw["r", 0][:], "scalar")
@@ -218,8 +218,8 @@ def tile_list_tgn_gruP_kernel(
         first_cand = held("first_cand", [P, HALF], F32)
         first_moved = held("first_moved", [P, HALF], F32)
         first_updated = held("first_updated", [P, HALF], F32)
-        early_sum = {0: held("first_sum", [P, HALF], F32), 1: placed("second_sum", [P, HALF], F32, 1024), 2: held("third_sum", [P, HALF], F32)}
-        later = {}
+        early_sum = {0: held("first_sum", [P, HALF], F32), 1: placed("second_sum", [P, HALF], F32, 1024)}
+        later = {("cand", 0): held("cand_0", [P, HALF], F32)}
 
         def reset(u):
             return own_reset[u][:] if u in own_reset else later_reset(u)
@@ -228,7 +228,7 @@ def tile_list_tgn_gruP_kernel(
             return later["keep_gate"][:] if u == 0 else later_keep_gate(u)
 
         def cand(u):
-            return first_cand[:] if u == 0 else later["cand"][:, u % 2, :]
+            return first_cand[:] if u == 0 else later["cand", u % 2][:]
 
         def summed(u):
             return early_sum[u][:] if u in early_sum else cand(u)
@@ -246,7 +246,7 @@ def tile_list_tgn_gruP_kernel(
             b, c = units[u]
             state_pass(sr(u), "r", b, c, True, False)
             message_pass(sr(u), "r", b, c, False, True)
-            nc.scalar.activation(reset(u), sr(u)[:], ACT.Sigmoid, bias=bias["r"][:, b : b + 1])
+            nc.scalar.activation(reset(u), sr(u)[:], ACT.Sigmoid, bias=bias[:, b : b + 1])
 
         def products(u):
             b, c = units[u]
@@ -267,7 +267,7 @@ def tile_list_tgn_gruP_kernel(
 
         def candidate_tanh(u):
             b = units[u][0]
-            nc.scalar.activation(cand(u), summed(u), ACT.Tanh, bias=bias["n"][:, b : b + 1])
+            nc.scalar.activation(cand(u), summed(u), ACT.Tanh, bias=bias[:, BLOCKS + b : BLOCKS + b + 1])
 
         def difference(u):
             b, c = units[u]
@@ -338,6 +338,9 @@ def tile_list_tgn_gruP_kernel(
         x_mx[1] = quantise("x_1", x_grouped[1][:], HALF)
         reset_gate(0)
         reset_gate(2)
+        late_rn = placed("late_rn", [P, 2, SPAN * PACK], BF16, 5120)
+        round_rows(late_rn[:, 0, :], w_raw["r", 1][:], "scalar")
+        round_rows(late_rn[:, 1, :], w_raw["n", 1][:], "scalar")
         products(0)
         products(2)
         reset_state(0)
@@ -348,40 +351,38 @@ def tile_list_tgn_gruP_kernel(
         round_rows(w_grouped["z"][:], w_raw["z", 0][:], "scalar")
         reset_gate(1)
         candidate_sum(2)
+        candidate_tanh(2)
+        codes_rn = held("late_rn_codes", [P, 2 * SPAN], U32)
+        scales_rn = placed("late_rn_scales", [P, 2 * SPAN], U8, 14336)
+        nc.vector.quantize_mx(out=codes_rn[:].bitcast(FP8X4), scales=scales_rn[:], in_=late_rn[:].rearrange("p g c -> p (g c)"))
         products(1)
         difference(0)
         reset_state(1)
         candidate_sum(1)
-        later["cand"] = held("cand", [P, 2, HALF], F32, on="w_raw_z0")
+        later["cand", 1] = held("cand_1", [P, HALF], F32, on="w_raw_z0")
         candidate_tanh(1)
-        nc.vector.tensor_scalar(minus_bias_z[:], bias["z"][:], -1.0, None, ALU.mult)
         quantise_w("z")
         later["second_moved"] = held("second_moved", [P, HALF], F32, on="first_sum")
         later["keep_gate"] = placed("first_keep_gate", [P, HALF], F32, 0)
         update_gate(0)
-        late_r = placed("late_r", [P, SPAN * PACK], BF16, 6144)
-        late_nz = placed("late_nz", [P, 2, SPAN * PACK], BF16, 2048)
-        round_rows(late_r[:], w_raw["r", 1][:], "scalar")
-        round_rows(late_nz[:, 0, :], w_raw["n", 1][:], "scalar")
-        round_rows(late_nz[:, 1, :], w_raw["z", 1][:], "scalar")
+        late_z = placed("late_z", [P, SPAN * PACK], BF16, 3072)
+        round_rows(late_z[:], w_raw["z", 1][:], "scalar")
         update_gate(1)
         difference(1)
         gate(nc.vector, 0)
-        codes_r, scales_r = quantise("late_r", late_r[:], SPAN)
+        codes_z, scales_z = quantise("late_z", late_z[:], SPAN)
         combine(nc.vector, 0)
-        codes_nz, scales_nz = quantise("late_nz", late_nz[:].rearrange("p g c -> p (g c)"), 2 * SPAN)
         for b in range(2):
             cols = slice(b * P, (b + 1) * P)
-            w_mx["r", 2 + b] = (codes_r[:, cols], scales_r[:, cols])
-            w_mx["n", 2 + b] = (codes_nz[:, cols], scales_nz[:, cols])
+            w_mx["r", 2 + b] = (codes_rn[:, cols], scales_rn[:, cols])
+            w_mx["z", 2 + b] = (codes_z[:, cols], scales_z[:, cols])
             cols = slice(SPAN + b * P, SPAN + (b + 1) * P)
-            w_mx["z", 2 + b] = (codes_nz[:, cols], scales_nz[:, cols])
-        later["weighed"] = placed("first_weighed", [P, HALF], F32, 5120)
+            w_mx["n", 2 + b] = (codes_rn[:, cols], scales_rn[:, cols])
+        later["weighed"] = placed("first_weighed", [P, HALF], F32, 4096)
         nc.vector.tensor_tensor(later["weighed"][:], updated(0), event_weight[0][:], ALU.mult)
         later["moved"] = held("moved", [P, HALF], F32, on="first_updated")
         own_reset[3] = placed("fourth_reset", [P, HALF], F32, 0)
         reset_gate(3)
-        candidate_tanh(2)
         products(3)
         update_gate(2)
         update_gate(3)
@@ -420,21 +421,21 @@ def tile_list_tgn_gruP_kernel(
                 scales=y_scales[:, blocks, :].rearrange("r b c -> r (b c)"),
                 in_=y_grouped[:, blocks, :].rearrange("r b c -> r (b c)"),
             )
-            for b in range(blocks.start, blocks.stop):
-                nc.sync.dma_start(
-                    out_words[32 * b : 32 * (b + 1), :].rearrange("p (a c) -> a p c", a=4), codes[:, b, :].bitcast(I32)
-                )
-        final_codes = [held("final_codes_%d" % pair, [P, SPAN], U32) for pair in range(2)]
-        final_words = out_words[32 * final : 32 * (final + 1), :].rearrange("p (a h c) -> h a p c", a=4, h=2)
+        rows = out_words.rearrange("(b p) t -> p b t", p=32)
+        for a in range(4):
+            nc.sync.dma_start(rows[:, 0:final, a * QUARTER : (a + 1) * QUARTER], codes[32 * a : 32 * (a + 1)].bitcast(I32))
+        final_codes = held("final_codes", [P, QUARTER], U32)
         for pair in range(2):
             turn_back(2 * pair, back[pair])
             turn_back(2 * pair + 1, back[pair])
             weave(final, pair, back[pair], engines[pair])
+            cols = slice(pair * SPAN, (pair + 1) * SPAN)
             nc.vector.quantize_mx(
-                out=final_codes[pair][:].bitcast(FP8X4), scales=y_scales[:, final, pair * SPAN : (pair + 1) * SPAN],
-                in_=y_grouped[:, final, pair * SPAN * PACK : (pair + 1) * SPAN * PACK],
+                out=final_codes[:, cols].bitcast(FP8X4), scales=y_scales[:, final, cols],
+                in_=y_grouped[:, final, PACK * cols.start : PACK * cols.stop],
             )
-            nc.sync.dma_start(final_words[pair], final_codes[pair][:].bitcast(I32))
+        for a in range(4):
+            nc.sync.dma_start(rows[:, final, a * QUARTER : (a + 1) * QUARTER], final_codes[32 * a : 32 * (a + 1), :].bitcast(I32))
         scale_rows = out_2[0].rearrange("(b r) t -> r b t", r=4)
         for a in range(4):
             nc.sync.dma_start(

@@ -55,8 +55,9 @@ def tile_list_tgn_gruP_kernel(
         u_scales_dram = {"r": ur_scales, "n": un_scales, "z": uz_scales}
         bias_dram = {"r": br, "n": bn, "z": bz}
         w_raw = {
-            (g, s): held("w_raw_%s%d" % (g, s), [P, PACK, SPAN], F32) for g in gates for s in range(2) if (g, s) != ("n", 0)
+            (g, s): held("w_raw_%s%d" % (g, s), [P, PACK, SPAN], F32) for g in gates for s in range(2) if g != "n"
         }
+        w_raw["n", 1] = placed("w_raw_n1", [P, PACK, SPAN], F32, 21504)
         w_raw["n", 0] = placed("w_raw_n0", [P, PACK, SPAN], F32, 12288)
         u_words = {g: held("u_words_" + g, [P, 2 * N], U8) for g in gates}
         u_scales = {g: held("u_scales_" + g, [P, N], U8) for g in gates}
@@ -110,8 +111,8 @@ def tile_list_tgn_gruP_kernel(
         load_scale_rows(u_scales["n"], un_scales)
         load_w("r", 1)
         load_w("n", 1)
-        load_state(0)
         load_w("z", 0)
+        load_state(0)
         load_u_words("z")
         load_scale_rows(u_scales["z"], uz_scales)
         load_w("z", 1)
@@ -199,13 +200,13 @@ def tile_list_tgn_gruP_kernel(
         state_bank, message_bank = bank("state_bank"), bank("message_bank")
 
         def sr(u):
-            return message_bank if u == 2 else reset_bank
+            return message_bank if u == 2 else state_bank if u == 1 else reset_bank
 
         def hn(u):
-            return across[0] if u == 2 else state_bank
+            return across[0] if u == 2 else message_bank if u == 1 else state_bank
 
         def xn(u):
-            return reset_bank if u == 0 else message_bank
+            return across[0] if u == 2 else reset_bank if u < 2 else message_bank
 
         def sz(u):
             return update_bank
@@ -215,11 +216,12 @@ def tile_list_tgn_gruP_kernel(
         own_reset = {
             0: placed("first_reset", [P, HALF], F32, 12288), 2: placed("third_reset", [P, HALF], F32, 14336),
         }
-        first_cand = held("first_cand", [P, HALF], F32)
-        first_moved = held("first_moved", [P, HALF], F32)
+        second_gated = placed("second_gated", [P, HALF], F32, 16384)
+        third_gated = held("third_gated", [P, HALF], F32)
         first_updated = held("first_updated", [P, HALF], F32)
-        early_sum = {0: held("first_sum", [P, HALF], F32), 1: placed("second_sum", [P, HALF], F32, 1024)}
-        later = {("cand", 0): held("cand_0", [P, HALF], F32)}
+        early_sum = {0: placed("first_sum", [P, HALF], F32, 18432), 1: placed("second_sum", [P, HALF], F32, 1024)}
+        early_sum[2] = held("third_sum", [P, HALF], F32)
+        later = {}
 
         def reset(u):
             return own_reset[u][:] if u in own_reset else later_reset(u)
@@ -228,13 +230,16 @@ def tile_list_tgn_gruP_kernel(
             return later["keep_gate"][:] if u == 0 else later_keep_gate(u)
 
         def cand(u):
-            return first_cand[:] if u == 0 else later["cand", u % 2][:]
+            return later["first_cand"][:] if u == 0 else later["cand", u % 2][:]
 
         def summed(u):
             return early_sum[u][:] if u in early_sum else cand(u)
 
+        def gated(u):
+            return second_gated[:] if u == 1 else third_gated[:] if u == 2 else summed(u)
+
         def moved(u):
-            return first_moved[:] if u == 0 else later["second_moved"][:] if u == 1 else later["moved"][:]
+            return later["first_moved"][:] if u == 0 else later["second_moved"][:] if u == 1 else later["moved"][:]
 
         def scaled(u):
             return later["moved"][:] if u == 1 else moved(u)
@@ -248,10 +253,17 @@ def tile_list_tgn_gruP_kernel(
             message_pass(sr(u), "r", b, c, False, True)
             nc.scalar.activation(reset(u), sr(u)[:], ACT.Sigmoid, bias=bias[:, b : b + 1])
 
-        def products(u):
+        def state_product(u):
             b, c = units[u]
             state_pass(hn(u), "n", b, c, True, True)
+
+        def message_product(u):
+            b, c = units[u]
             message_pass(xn(u), "n", b, c, True, True)
+
+        def products(u):
+            state_product(u)
+            message_product(u)
 
         def update_gate(u):
             b, c = units[u]
@@ -260,10 +272,10 @@ def tile_list_tgn_gruP_kernel(
             nc.scalar.activation(keep_gate(u), sz(u)[:], ACT.Sigmoid, bias=minus_bias_z[:, b : b + 1], scale=-1.0)
 
         def reset_state(u):
-            nc.vector.tensor_tensor(summed(u), hn(u)[:], reset(u), ALU.mult)
+            nc.vector.tensor_tensor(gated(u), hn(u)[:], reset(u), ALU.mult)
 
         def candidate_sum(u):
-            nc.vector.tensor_tensor(summed(u), xn(u)[:], summed(u), ALU.add)
+            nc.vector.tensor_tensor(summed(u), xn(u)[:], gated(u), ALU.add)
 
         def candidate_tanh(u):
             b = units[u][0]
@@ -341,37 +353,41 @@ def tile_list_tgn_gruP_kernel(
         late_rn = placed("late_rn", [P, 2, SPAN * PACK], BF16, 5120)
         round_rows(late_rn[:, 0, :], w_raw["r", 1][:], "scalar")
         round_rows(late_rn[:, 1, :], w_raw["n", 1][:], "scalar")
+        later["first_cand"] = placed("first_cand", [P, HALF], F32, 21504)
+        own_reset[1] = placed("second_reset", [P, HALF], F32, 23552)
         products(0)
-        products(2)
+        state_product(2)
         reset_state(0)
         reset_state(2)
+        message_product(2)
         candidate_sum(0)
         candidate_tanh(0)
-        w_grouped["z"] = held("w_grouped_z", [P, SPAN * PACK], BF16, on="first_sum")
+        w_grouped["z"] = placed("w_grouped_z", [P, SPAN * PACK], BF16, 18432)
         round_rows(w_grouped["z"][:], w_raw["z", 0][:], "scalar")
         reset_gate(1)
         candidate_sum(2)
-        candidate_tanh(2)
         codes_rn = held("late_rn_codes", [P, 2 * SPAN], U32)
-        scales_rn = placed("late_rn_scales", [P, 2 * SPAN], U8, 14336)
+        scales_rn = held("late_rn_scales", [P, 2 * SPAN], U8, on="third_gated")
         nc.vector.quantize_mx(out=codes_rn[:].bitcast(FP8X4), scales=scales_rn[:], in_=late_rn[:].rearrange("p g c -> p (g c)"))
         products(1)
-        difference(0)
         reset_state(1)
         candidate_sum(1)
+        quantise_w("z")
+        later["first_moved"] = placed("first_moved", [P, HALF], F32, 17408)
+        difference(0)
         later["cand", 1] = held("cand_1", [P, HALF], F32, on="w_raw_z0")
         candidate_tanh(1)
-        quantise_w("z")
-        later["second_moved"] = held("second_moved", [P, HALF], F32, on="first_sum")
+        later["second_moved"] = placed("second_moved", [P, HALF], F32, 19456)
         later["keep_gate"] = placed("first_keep_gate", [P, HALF], F32, 0)
         update_gate(0)
         late_z = placed("late_z", [P, SPAN * PACK], BF16, 3072)
         round_rows(late_z[:], w_raw["z", 1][:], "scalar")
+        later["cand", 0] = held("cand_0", [P, HALF], F32, on="w_raw_z1")
         update_gate(1)
-        difference(1)
         gate(nc.vector, 0)
-        codes_z, scales_z = quantise("late_z", late_z[:], SPAN)
+        difference(1)
         combine(nc.vector, 0)
+        codes_z, scales_z = quantise("late_z", late_z[:], SPAN)
         for b in range(2):
             cols = slice(b * P, (b + 1) * P)
             w_mx["r", 2 + b] = (codes_rn[:, cols], scales_rn[:, cols])
@@ -383,6 +399,7 @@ def tile_list_tgn_gruP_kernel(
         later["moved"] = held("moved", [P, HALF], F32, on="first_updated")
         own_reset[3] = placed("fourth_reset", [P, HALF], F32, 0)
         reset_gate(3)
+        candidate_tanh(2)
         products(3)
         update_gate(2)
         update_gate(3)
@@ -425,15 +442,21 @@ def tile_list_tgn_gruP_kernel(
         for a in range(4):
             nc.sync.dma_start(rows[:, 0:final, a * QUARTER : (a + 1) * QUARTER], codes[32 * a : 32 * (a + 1)].bitcast(I32))
         final_codes = held("final_codes", [P, QUARTER], U32)
-        for pair in range(2):
-            turn_back(2 * pair, back[pair])
-            turn_back(2 * pair + 1, back[pair])
-            weave(final, pair, back[pair], engines[pair])
-            cols = slice(pair * SPAN, (pair + 1) * SPAN)
-            nc.vector.quantize_mx(
-                out=final_codes[:, cols].bitcast(FP8X4), scales=y_scales[:, final, cols],
-                in_=y_grouped[:, final, PACK * cols.start : PACK * cols.stop],
+        for s, target in enumerate(back + across):
+            words = y_pairs[s][:].bitcast(F32)
+            for u in range(2):
+                nc.tensor.transpose(target[:, u * P : (u + 1) * P], words[:, u * P : (u + 1) * P], identity[:])
+            copy_on(
+                engines[s % 2],
+                y_grouped[:, final, :].bitcast(F32)[:, s * SPAN : (s + 1) * SPAN].rearrange("r (t u) -> r t u", u=2),
+                target[:, 0:SPAN].rearrange("r (u t) -> r t u", u=2),
             )
+            if s % 2 == 1:
+                cols = slice((s - 1) * P, (s + 1) * P)
+                nc.vector.quantize_mx(
+                    out=final_codes[:, cols].bitcast(FP8X4), scales=y_scales[:, final, cols],
+                    in_=y_grouped[:, final, PACK * cols.start : PACK * cols.stop],
+                )
         for a in range(4):
             nc.sync.dma_start(rows[:, final, a * QUARTER : (a + 1) * QUARTER], final_codes[32 * a : 32 * (a + 1), :].bitcast(I32))
         scale_rows = out_2[0].rearrange("(b r) t -> r b t", r=4)

@@ -3,8 +3,8 @@ from contextlib import ExitStack
 import concourse.mybir as mybir
 from concourse.masks import make_identity
 
-K, M, N, T, J = 512, 512, 512, 2048, 1024
-FLOPS = 6 * 2 * 512 * N * J
+K, N, T, J = 512, 512, 2048, 1024
+FLOPS = 6 * 2 * K * N * J
 
 F32 = mybir.dt.float32
 BF16 = mybir.dt.bfloat16
@@ -19,12 +19,15 @@ ACT = mybir.ActivationFunctionType
 
 P = 128
 PACK = 4
+QUADRANT = 32
 HALF = 512
 HALVES = J // HALF
 BLOCKS = N // P
 SPAN = 2 * P
 QUARTER = T // 4
+SLICES = QUARTER // P
 PAGES = 3
+STEP = 1024
 
 
 def tile_list_tgn_gruP_kernel(
@@ -40,25 +43,32 @@ def tile_list_tgn_gruP_kernel(
         def held(name, shape, dtype, on=None):
             return keep.tile(shape, dtype, name=name, tag=on or name, align_bytes=64)
 
-        def placed(name, shape, dtype, offset):
-            return shared.tile(shape, dtype, name=name, align_bytes=64, offset=offset)
+        def placed(name, shape, dtype, steps):
+            return shared.tile(shape, dtype, name=name, align_bytes=64, offset=steps * STEP)
 
-        def bank(name, on=None):
-            return psum.tile([P, HALF], F32, name=name, tag=on or name)
+        def unit_tile(name, on=None):
+            return held(name, [P, HALF], F32, on)[:]
 
-        offsets = keep.tile([P, J // 16], U16, name="offsets")
-        table_words = held("table_words", [P, T], I32)
-        table_scales = held("table_scales", [P, T], U8)
+        def placed_unit_tile(name, steps):
+            return placed(name, [P, HALF], F32, steps)[:]
+
+        def bank(name):
+            return psum.tile([P, HALF], F32, name=name)
+
         gates = ("r", "n", "z")
         w_dram = {"r": wr, "n": wn, "z": wz}
         u_words_dram = {"r": ur_words, "n": un_words, "z": uz_words}
         u_scales_dram = {"r": ur_scales, "n": un_scales, "z": uz_scales}
         bias_dram = {"r": br, "n": bn, "z": bz}
+
+        offsets = keep.tile([P, J // 16], U16, name="offsets")
+        table_words = held("table_words", [P, T], I32)
+        table_scales = held("table_scales", [P, T], U8)
         w_raw = {
-            (g, s): held("w_raw_%s%d" % (g, s), [P, PACK, SPAN], F32) for g in gates for s in range(2) if g != "n"
+            (g, span): held("w_raw_%s%d" % (g, span), [P, PACK, SPAN], F32) for g in ("r", "z") for span in range(2)
         }
-        w_raw["n", 1] = placed("w_raw_n1", [P, PACK, SPAN], F32, 21504)
-        w_raw["n", 0] = placed("w_raw_n0", [P, PACK, SPAN], F32, 12288)
+        w_raw["n", 1] = placed("w_raw_n1", [P, PACK, SPAN], F32, 21)
+        w_raw["n", 0] = placed("w_raw_n0", [P, PACK, SPAN], F32, 12)
         u_words = {g: held("u_words_" + g, [P, 2 * N], U8) for g in gates}
         u_scales = {g: held("u_scales_" + g, [P, N], U8) for g in gates}
         bias_rows = held("bias_rows", [P, P], F32)
@@ -68,10 +78,6 @@ def tile_list_tgn_gruP_kernel(
         pages = [held("page_%d" % i, [P, T], F32) for i in range(PAGES)]
         identity = held("identity", [P, P], F32)
 
-        warm = held("warm", [P, 8], F32)
-        warm_out = held("warm_out", [P, 8], F32)
-        nc.vector.memset(warm[:], 0.0)
-        nc.scalar.activation(warm_out[:], warm[:], ACT.Sigmoid)
         nc.gpsimd.memset(bias_rows[:], 0.0)
         nc.gpsimd.memset(table_scales[:].bitcast(I32), 0)
         for g in gates:
@@ -80,15 +86,19 @@ def tile_list_tgn_gruP_kernel(
         for page in pages:
             nc.vector.memset(page[:].bitcast(I32), 0)
 
+        warm_out = held("warm_out", [P, 8], F32)
+        nc.scalar.activation(warm_out[:], identity[:, 0:8], ACT.Sigmoid)
+
         def load_scale_rows(tile, dram):
             for q in range(4):
-                nc.sync.dma_start(tile[32 * q : 32 * q + 4, :].bitcast(I32), dram[0, 4 * q : 4 * q + 4, :].bitcast(I32))
+                rows = tile[QUADRANT * q : QUADRANT * q + 4, :]
+                nc.sync.dma_start(rows.bitcast(I32), dram[0, 4 * q : 4 * q + 4, :].bitcast(I32))
 
         def load_rows(tile, dram):
-            nc.sync.dma_start(tile[:], dram.rearrange("(p j) c -> p j c", j=PACK))
+            nc.sync.dma_start(tile[:], dram.rearrange("(p i) c -> p i c", i=PACK))
 
-        def load_w(g, s):
-            load_rows(w_raw[g, s], w_dram[g][:, s * SPAN : (s + 1) * SPAN])
+        def load_w(g, span):
+            load_rows(w_raw[g, span], w_dram[g][:, span * SPAN : (span + 1) * SPAN])
 
         def load_u_words(g):
             nc.sync.dma_start(u_words[g][:].bitcast(I32), u_words_dram[g][0].bitcast(I32))
@@ -99,7 +109,8 @@ def tile_list_tgn_gruP_kernel(
         nc.sync.dma_start(offsets[:], offs)
         nc.sync.dma_start(table_words[:], tab_words[0].rearrange("p c i -> p (c i)").bitcast(I32))
         for i, g in enumerate(gates):
-            nc.sync.dma_start(bias_rows[32 * i : 32 * i + BLOCKS, :], bias_dram[g].rearrange("(b q) -> b q", q=P))
+            rows = bias_rows[QUADRANT * i : QUADRANT * i + BLOCKS, :]
+            nc.sync.dma_start(rows, bias_dram[g].rearrange("(b q) -> b q", q=P))
         load_rows(x_raw[0], x[:, 0:HALF])
         load_scale_rows(table_scales, tab_scales)
         load_w("r", 0)
@@ -140,8 +151,8 @@ def tile_list_tgn_gruP_kernel(
         def round_rows(grouped, raw, engine):
             copy_on(
                 engine,
-                grouped.rearrange("p (c i j) -> p c j i", i=4, j=PACK),
-                raw.rearrange("p j (c i) -> p c j i", i=4),
+                grouped.rearrange("p (c d i) -> p c i d", d=4, i=PACK),
+                raw.rearrange("p i (c d) -> p c i d", d=4),
             )
 
         def quantise(name, grouped, width, on=None):
@@ -151,264 +162,237 @@ def tile_list_tgn_gruP_kernel(
             return codes, scales
 
         x_mx, w_mx = {}, {}
-        x_grouped = [held("x_grouped_0", [P, HALF * PACK], BF16)]
-        w_grouped = {g: held("w_grouped_" + g, [P, SPAN * PACK], BF16) for g in ("r", "n")}
 
-        def quantise_w(g, on=None):
-            codes, scales = quantise("w_" + g, w_grouped[g][:], SPAN, on)
-            for b in range(2):
-                w_mx[g, b] = (codes[:, b * P : (b + 1) * P], scales[:, b * P : (b + 1) * P])
+        def quantise_w(name, grouped, parts, on=None):
+            codes, scales = quantise(name, grouped, len(parts) * SPAN, on)
+            for i, (g, span) in enumerate(parts):
+                for b in range(2):
+                    cols = slice(i * SPAN + b * P, i * SPAN + (b + 1) * P)
+                    w_mx[g, 2 * span + b] = (codes[:, cols], scales[:, cols])
+
+        x_grouped_0 = held("x_grouped_0", [P, HALF * PACK], BF16)
+        w_grouped_r = held("w_grouped_r", [P, SPAN * PACK], BF16)
+        w_grouped_n = held("w_grouped_n", [P, SPAN * PACK], BF16)
 
         across = [bank("across_%d" % i) for i in range(2)]
         back = [bank("back_%d" % i) for i in range(2)]
-        bias = held("bias", [P, 2 * BLOCKS], F32)
+
+        bias = held("bias", [P, 2, BLOCKS], F32)
         minus_bias_z = held("minus_bias_z", [P, BLOCKS], F32)
         nc.tensor.transpose(back[1][:, 0:P], bias_rows[:], identity[:])
-        nc.scalar.copy(bias[:].rearrange("q (g b) -> q g b", g=2), back[1][:, 0:64].rearrange("q (g b) -> q g b", g=2)[:, :, 0:BLOCKS])
-        nc.scalar.activation(minus_bias_z[:], back[1][:, 64 : 64 + BLOCKS], ACT.Copy, scale=-1.0)
+        turned_bias = back[1][:, 0 : 2 * QUADRANT].rearrange("q (g b) -> q g b", g=2)
+        nc.scalar.copy(bias[:], turned_bias[:, :, 0:BLOCKS])
+        nc.scalar.activation(minus_bias_z[:], back[1][:, 2 * QUADRANT : 2 * QUADRANT + BLOCKS], ACT.Copy, scale=-1.0)
 
-        round_rows(x_grouped[0][:], x_raw[0][:], "scalar")
-        round_rows(w_grouped["r"][:], w_raw["r", 0][:], "scalar")
-        round_rows(w_grouped["n"][:], w_raw["n", 0][:], "scalar")
-        x_mx[0] = quantise("x_0", x_grouped[0][:], HALF, on="table_scales")
-        quantise_w("r", on="x_grouped_0")
-        quantise_w("n", on="w_grouped_r")
+        round_rows(x_grouped_0[:], x_raw[0][:], "scalar")
+        round_rows(w_grouped_r[:], w_raw["r", 0][:], "scalar")
+        round_rows(w_grouped_n[:], w_raw["n", 0][:], "scalar")
+        x_mx[0] = quantise("x_0", x_grouped_0[:], HALF, on="table_scales")
+        quantise_w("w_r", w_grouped_r[:], [("r", 0)], on="x_grouped_0")
+        quantise_w("w_n", w_grouped_n[:], [("n", 0)], on="w_grouped_r")
 
-        def message_pass(acc, g, b, c, start, stop):
+        units = [(b, c) for b in range(BLOCKS) for c in range(HALVES)]
+        last = len(units) - 1
+
+        def message_pass(acc, g, u, start, stop):
+            b, c = units[u]
             nc.tensor.matmul_mx(
                 out=acc[:], lhsT=w_mx[g, b][0].bitcast(FP8X4), lhsT_scale=w_mx[g, b][1],
                 rhs=x_mx[c][0][:].bitcast(FP8X4), rhs_scale=x_mx[c][1][:], start=start, stop=stop,
             )
 
-        def state_pass(acc, g, b, c, start, stop):
+        def state_pass(acc, g, u, start, stop):
+            b, c = units[u]
             nc.tensor.matmul_mx(
                 out=acc[:], lhsT=u_words[g][:, 2 * b * P : 2 * (b + 1) * P].bitcast(FP4X4),
                 lhsT_scale=u_scales[g][:, b * P : (b + 1) * P],
                 rhs=picked_words[c][:].bitcast(FP8X4), rhs_scale=picked_scales[c][:], start=start, stop=stop,
             )
 
-        units = [(b, c) for b in range(BLOCKS) for c in range(HALVES)]
-
-        def slot(u):
-            return {1: 2, 2: 1}.get(u, u)
-
-        def ring(name, count):
-            tiles = [held("%s_%d" % (name, i), [P, HALF], F32) for i in range(count)]
-            return lambda u: tiles[u % count][:]
+        def ring(name, count, first):
+            tiles = [unit_tile("%s_%d" % (name, i)) for i in range(count)]
+            return {u: tiles[u % count] for u in range(first, last + 1)}
 
         reset_bank, update_bank = bank("reset_bank"), bank("update_bank")
         state_bank, message_bank = bank("state_bank"), bank("message_bank")
+        sr = {u: reset_bank for u in range(last + 1)}
+        hn = {u: state_bank for u in range(last + 1)}
+        xn = {u: message_bank for u in range(last + 1)}
+        sr[2], hn[2], xn[2] = message_bank, across[0], across[0]
+        sr[1], hn[1], xn[1] = state_bank, message_bank, reset_bank
+        xn[0] = reset_bank
 
-        def sr(u):
-            return message_bank if u == 2 else state_bank if u == 1 else reset_bank
-
-        def hn(u):
-            return across[0] if u == 2 else message_bank if u == 1 else state_bank
-
-        def xn(u):
-            return across[0] if u == 2 else reset_bank if u < 2 else message_bank
-
-        def sz(u):
-            return update_bank
-
-        later_keep_gate, later_updated = ring("keep_gate", 3), ring("updated", 2)
-        later_reset = ring("reset", 2)
-        own_reset = {
-            0: placed("first_reset", [P, HALF], F32, 12288), 2: placed("third_reset", [P, HALF], F32, 14336),
-        }
-        second_gated = placed("second_gated", [P, HALF], F32, 16384)
-        third_gated = held("third_gated", [P, HALF], F32)
-        first_updated = held("first_updated", [P, HALF], F32)
-        early_sum = {0: placed("first_sum", [P, HALF], F32, 18432), 1: placed("second_sum", [P, HALF], F32, 1024)}
-        early_sum[2] = held("third_sum", [P, HALF], F32)
-        later = {}
-
-        def reset(u):
-            return own_reset[u][:] if u in own_reset else later_reset(u)
-
-        def keep_gate(u):
-            return later["keep_gate"][:] if u == 0 else later_keep_gate(u)
-
-        def cand(u):
-            return later["first_cand"][:] if u == 0 else later["cand", u % 2][:]
-
-        def summed(u):
-            return early_sum[u][:] if u in early_sum else cand(u)
-
-        def gated(u):
-            return second_gated[:] if u == 1 else third_gated[:] if u == 2 else summed(u)
-
-        def moved(u):
-            return later["first_moved"][:] if u == 0 else later["second_moved"][:] if u == 1 else later["moved"][:]
-
-        def scaled(u):
-            return later["moved"][:] if u == 1 else moved(u)
-
-        def updated(u):
-            return first_updated[:] if u == 0 else later_updated(u)
+        keep_gate = ring("keep_gate", 3, first=1)
+        updated = ring("updated", 2, first=1)
+        reset = ring("reset", 2, first=4)
+        reset[0] = placed_unit_tile("reset_of_0", 12)
+        reset[2] = placed_unit_tile("reset_of_2", 14)
+        gated = {1: placed_unit_tile("gated_of_1", 16), 2: unit_tile("gated_of_2")}
+        updated[0] = unit_tile("updated_of_0")
+        summed = {0: placed_unit_tile("summed_of_0", 18), 1: placed_unit_tile("summed_of_1", 1)}
+        summed[2] = unit_tile("summed_of_2")
+        gated[0] = summed[0]
+        cand, moved, scaled = {}, {}, {}
 
         def reset_gate(u):
-            b, c = units[u]
-            state_pass(sr(u), "r", b, c, True, False)
-            message_pass(sr(u), "r", b, c, False, True)
-            nc.scalar.activation(reset(u), sr(u)[:], ACT.Sigmoid, bias=bias[:, b : b + 1])
+            b = units[u][0]
+            state_pass(sr[u], "r", u, True, False)
+            message_pass(sr[u], "r", u, False, True)
+            nc.scalar.activation(reset[u], sr[u][:], ACT.Sigmoid, bias=bias[:, 0, b : b + 1])
 
         def state_product(u):
-            b, c = units[u]
-            state_pass(hn(u), "n", b, c, True, True)
+            state_pass(hn[u], "n", u, True, True)
 
         def message_product(u):
-            b, c = units[u]
-            message_pass(xn(u), "n", b, c, True, True)
-
-        def products(u):
-            state_product(u)
-            message_product(u)
+            message_pass(xn[u], "n", u, True, True)
 
         def update_gate(u):
-            b, c = units[u]
-            state_pass(sz(u), "z", b, c, True, False)
-            message_pass(sz(u), "z", b, c, False, True)
-            nc.scalar.activation(keep_gate(u), sz(u)[:], ACT.Sigmoid, bias=minus_bias_z[:, b : b + 1], scale=-1.0)
+            b = units[u][0]
+            state_pass(update_bank, "z", u, True, False)
+            message_pass(update_bank, "z", u, False, True)
+            nc.scalar.activation(keep_gate[u], update_bank[:], ACT.Sigmoid, bias=minus_bias_z[:, b : b + 1], scale=-1.0)
 
         def reset_state(u):
-            nc.vector.tensor_tensor(gated(u), hn(u)[:], reset(u), ALU.mult)
+            nc.vector.tensor_tensor(gated[u], hn[u][:], reset[u], ALU.mult)
 
         def candidate_sum(u):
-            nc.vector.tensor_tensor(summed(u), xn(u)[:], gated(u), ALU.add)
+            nc.vector.tensor_tensor(summed[u], xn[u][:], gated[u], ALU.add)
 
         def candidate_tanh(u):
             b = units[u][0]
-            nc.scalar.activation(cand(u), summed(u), ACT.Tanh, bias=bias[:, BLOCKS + b : BLOCKS + b + 1])
+            nc.scalar.activation(cand[u], summed[u], ACT.Tanh, bias=bias[:, 1, b : b + 1])
 
         def difference(u):
             b, c = units[u]
-            nc.vector.tensor_tensor(moved(u), state[b][:].indirect(listed(c)), cand(u), ALU.subtract)
+            nc.vector.tensor_tensor(moved[u], state[b][:].indirect(listed(c)), cand[u], ALU.subtract)
 
-        def gate(engine, u):
-            engine.tensor_tensor(scaled(u), moved(u), keep_gate(u), ALU.mult)
+        def scale_by_keep(engine, u):
+            engine.tensor_tensor(scaled[u], moved[u], keep_gate[u], ALU.mult)
 
-        def combine(engine, u):
-            engine.tensor_tensor(updated(u), scaled(u), cand(u), ALU.add)
+        def add_candidate(engine, u):
+            engine.tensor_tensor(updated[u], scaled[u], cand[u], ALU.add)
 
-        def weigh(u):
-            nc.gpsimd.tensor_tensor(updated(u), updated(u), event_weight[units[u][1]][:], ALU.mult)
+        def weigh(engine, out, u):
+            engine.tensor_tensor(out, updated[u], event_weight[units[u][1]][:], ALU.mult)
 
-        def place(u):
+        def window(u):
             b, c = units[u]
-            page = pages[b % PAGES]
-            if u == 0:
-                nc.vector.tensor_copy(page[:].indirect(listed(c)), later["weighed"][:])
-            elif u < len(units) - 1:
-                nc.vector.tensor_copy(page[:].indirect(listed(c)), updated(u))
-            else:
-                nc.vector.tensor_tensor(page[:].indirect(listed(c)), updated(u), event_weight[c][:], ALU.mult)
+            return pages[b % PAGES][:].indirect(listed(c))
+
+        def store_if_finished(u):
+            b, c = units[u]
             if c == HALVES - 1:
-                nc.sync.dma_start(out_0[b * P : (b + 1) * P, :], page[:])
+                nc.sync.dma_start(out_0[b * P : (b + 1) * P, :], pages[b % PAGES][:])
 
-        y_pairs = [held("y_pairs_%d" % i, [P, HALF], BF16) for i in range(4)]
+        y_pairs = [held("y_pairs_%d" % s, [P, HALF], BF16) for s in range(SLICES)]
         y_grouped = held("y_grouped", [P, BLOCKS, QUARTER * PACK], BF16)
-        out_words = out_1[0].rearrange("p c i -> p (c i)").bitcast(I32)
 
-        def turn_out(b, s, across, engine):
-            page = pages[b % PAGES]
-            for a in range(4):
+        def turn_out(b, s, target, engine, quarters=range(4)):
+            for i, a in enumerate(quarters):
                 first = a * QUARTER + s * P
-                nc.tensor.transpose(across[:, a * P : (a + 1) * P], page[:, first : first + P], identity[:])
+                nc.tensor.transpose(target[:, i * P : (i + 1) * P], pages[b % PAGES][:, first : first + P], identity[:])
+            words = slice(QUADRANT * quarters[0], QUADRANT * (quarters[-1] + 1))
             copy_on(
                 engine,
-                y_pairs[s][:].rearrange("t (u r e) -> t u r e", u=2, e=2),
-                across[:].rearrange("t (r u e) -> t u r e", u=2, e=2),
+                y_pairs[s][:].rearrange("t (h r e) -> t h r e", h=2, e=2)[:, :, words, :],
+                target[:, 0 : len(quarters) * P].rearrange("t (r h e) -> t h r e", h=2, e=2),
             )
 
-        def turn_back(s, target):
+        def turn_back(s, target, first):
             words = y_pairs[s][:].bitcast(F32)
-            for u in range(2):
-                first = (2 * (s % 2) + u) * P
-                nc.tensor.transpose(target[:, first : first + P], words[:, u * P : (u + 1) * P], identity[:])
+            for h in range(2):
+                nc.tensor.transpose(
+                    target[:, first + h * P : first + (h + 1) * P], words[:, h * P : (h + 1) * P], identity[:]
+                )
 
-        def weave(b, pair, source, engine):
+        def weave(b, first, count, source, engine):
+            words = y_grouped[:, b, :].bitcast(F32)[:, first * 2 * P : (first + count) * 2 * P]
             copy_on(
                 engine,
-                y_grouped[:, b, :].bitcast(F32)[:, pair * HALF : (pair + 1) * HALF].rearrange("r (s t u) -> r s t u", s=2, u=2),
-                source[:].rearrange("r (s u t) -> r s t u", s=2, u=2),
+                words.rearrange("r (s t h) -> r s t h", s=count, h=2),
+                source[:, 0 : count * 2 * P].rearrange("r (s h t) -> r s t h", s=count, h=2),
             )
 
-        def regroup(b):
-            for s in range(4):
-                turn_out(b, s, across[s % 2], "scalar")
-            for pair in range(2):
-                turn_back(2 * pair, back[pair])
-                turn_back(2 * pair + 1, back[pair])
-                weave(b, pair, back[pair], "scalar")
+        def regroup(b, targets):
+            for s in range(SLICES):
+                turn_out(b, s, targets[s % len(targets)], "scalar")
+            for pair in range(SLICES // 2):
+                turn_back(2 * pair, back[pair], 0)
+                turn_back(2 * pair + 1, back[pair], 2 * P)
+                weave(b, 2 * pair, 2, back[pair], "scalar")
 
         y_scales = held("y_scales", [P, BLOCKS, QUARTER], U8)
 
-        last = len(units) - 1
-        x_grouped.append(held("x_grouped_1", [P, HALF * PACK], BF16, on="w_grouped_n"))
-        round_rows(x_grouped[1][:], x_raw[1][:], "vector")
-        x_mx[1] = quantise("x_1", x_grouped[1][:], HALF)
+        x_grouped_1 = held("x_grouped_1", [P, HALF * PACK], BF16, on="w_grouped_n")
+        round_rows(x_grouped_1[:], x_raw[1][:], "vector")
+        x_mx[1] = quantise("x_1", x_grouped_1[:], HALF)
         reset_gate(0)
         reset_gate(2)
-        late_rn = placed("late_rn", [P, 2, SPAN * PACK], BF16, 5120)
+        late_rn = placed("late_rn", [P, 2, SPAN * PACK], BF16, 5)
         round_rows(late_rn[:, 0, :], w_raw["r", 1][:], "scalar")
         round_rows(late_rn[:, 1, :], w_raw["n", 1][:], "scalar")
-        later["first_cand"] = placed("first_cand", [P, HALF], F32, 21504)
-        own_reset[1] = placed("second_reset", [P, HALF], F32, 23552)
-        products(0)
+        cand[0] = placed_unit_tile("cand_of_0", 21)
+        reset[1] = placed_unit_tile("reset_of_1", 23)
+        state_product(0)
+        message_product(0)
         state_product(2)
         reset_state(0)
         reset_state(2)
         message_product(2)
         candidate_sum(0)
         candidate_tanh(0)
-        w_grouped["z"] = placed("w_grouped_z", [P, SPAN * PACK], BF16, 18432)
-        round_rows(w_grouped["z"][:], w_raw["z", 0][:], "scalar")
+        w_grouped_z = placed("w_grouped_z", [P, SPAN * PACK], BF16, 18)
+        round_rows(w_grouped_z[:], w_raw["z", 0][:], "scalar")
         reset_gate(1)
         candidate_sum(2)
-        codes_rn = held("late_rn_codes", [P, 2 * SPAN], U32)
-        scales_rn = held("late_rn_scales", [P, 2 * SPAN], U8, on="third_gated")
-        nc.vector.quantize_mx(out=codes_rn[:].bitcast(FP8X4), scales=scales_rn[:], in_=late_rn[:].rearrange("p g c -> p (g c)"))
-        products(1)
+        quantise_w("late_rn", late_rn[:].rearrange("p g c -> p (g c)"), [("r", 1), ("n", 1)], on="gated_of_2")
+        state_product(1)
+        message_product(1)
         reset_state(1)
         candidate_sum(1)
-        quantise_w("z")
-        later["first_moved"] = placed("first_moved", [P, HALF], F32, 17408)
+        quantise_w("w_z", w_grouped_z[:], [("z", 0)])
+        moved[0] = placed_unit_tile("moved_of_0", 17)
+        scaled[0] = moved[0]
         difference(0)
-        later["cand", 1] = held("cand_1", [P, HALF], F32, on="w_raw_z0")
+        odd_cand = unit_tile("odd_cand", on="w_raw_z0")
+        cand[1] = odd_cand
         candidate_tanh(1)
-        later["second_moved"] = placed("second_moved", [P, HALF], F32, 19456)
-        later["keep_gate"] = placed("first_keep_gate", [P, HALF], F32, 0)
+        moved[1] = placed_unit_tile("moved_of_1", 19)
+        keep_gate[0] = placed_unit_tile("keep_gate_of_0", 0)
         update_gate(0)
-        late_z = placed("late_z", [P, SPAN * PACK], BF16, 3072)
+        late_z = placed("late_z", [P, SPAN * PACK], BF16, 3)
         round_rows(late_z[:], w_raw["z", 1][:], "scalar")
-        later["cand", 0] = held("cand_0", [P, HALF], F32, on="w_raw_z1")
+        even_cand = unit_tile("even_cand", on="w_raw_z1")
+        for u in range(2, last + 1):
+            cand[u] = odd_cand if u % 2 else even_cand
+        for u in range(3, last + 1):
+            gated[u] = summed[u] = cand[u]
         update_gate(1)
-        gate(nc.vector, 0)
+        scale_by_keep(nc.vector, 0)
         difference(1)
-        combine(nc.vector, 0)
-        codes_z, scales_z = quantise("late_z", late_z[:], SPAN)
-        for b in range(2):
-            cols = slice(b * P, (b + 1) * P)
-            w_mx["r", 2 + b] = (codes_rn[:, cols], scales_rn[:, cols])
-            w_mx["z", 2 + b] = (codes_z[:, cols], scales_z[:, cols])
-            cols = slice(SPAN + b * P, SPAN + (b + 1) * P)
-            w_mx["n", 2 + b] = (codes_rn[:, cols], scales_rn[:, cols])
-        later["weighed"] = placed("first_weighed", [P, HALF], F32, 4096)
-        nc.vector.tensor_tensor(later["weighed"][:], updated(0), event_weight[0][:], ALU.mult)
-        later["moved"] = held("moved", [P, HALF], F32, on="first_updated")
-        own_reset[3] = placed("fourth_reset", [P, HALF], F32, 0)
+        add_candidate(nc.vector, 0)
+        quantise_w("late_z", late_z[:], [("z", 1)])
+        weighed_of_0 = placed_unit_tile("weighed_of_0", 4)
+        weigh(nc.vector, weighed_of_0, 0)
+        moved_later = unit_tile("moved_later", on="updated_of_0")
+        for u in range(1, last + 1):
+            scaled[u] = moved_later
+        for u in range(2, last + 1):
+            moved[u] = moved_later
+        reset[3] = placed_unit_tile("reset_of_3", 0)
         reset_gate(3)
         candidate_tanh(2)
-        products(3)
+        state_product(3)
+        message_product(3)
         update_gate(2)
         update_gate(3)
-        place(0)
+        nc.vector.tensor_copy(window(0), weighed_of_0)
+
         for u in range(1, last + 1):
-            gate(nc.gpsimd, u)
-            combine(nc.gpsimd, u)
+            scale_by_keep(nc.gpsimd, u)
+            add_candidate(nc.gpsimd, u)
             if u < last:
-                weigh(u)
+                weigh(nc.gpsimd, updated[u], u)
             if u + 2 <= last:
                 reset_state(u + 2)
             if u + 1 <= last:
@@ -418,49 +402,57 @@ def tile_list_tgn_gruP_kernel(
                 candidate_tanh(u + 2)
             if u + 3 <= last:
                 reset_gate(u + 3)
-                products(u + 3)
+                state_product(u + 3)
+                message_product(u + 3)
                 update_gate(u + 3)
             if u == PAGES * HALVES:
-                regroup(0)
-            place(u)
+                regroup(0, across)
+            if u < last:
+                nc.vector.tensor_copy(window(u), updated[u])
+            else:
+                weigh(nc.vector, window(u), u)
+            store_if_finished(u)
 
         final = BLOCKS - 1
-        for b in range(1, final):
-            regroup(b)
-        free_banks = [bank("final_%d" % s, on) for s, on in enumerate(("reset_bank", "update_bank", "state_bank", "message_bank"))]
-        engines = ("scalar", "vector")
-        for s in range(4):
-            turn_out(final, s, free_banks[s], engines[s % 2])
+        sum_banks = (reset_bank, update_bank, state_bank, message_bank)
+        regroup(1, across)
+        regroup(2, sum_banks)
+        for s, engine in enumerate(("scalar", "vector", "scalar")):
+            turn_out(final, s, sum_banks[s], engine)
+        turn_out(final, SLICES - 1, message_bank, "scalar", range(0, 2))
+        turn_out(final, SLICES - 1, across[1], "vector", range(2, 4))
         codes = held("y_codes", [P, final, QUARTER], U32, on="updated_%d" % (last % 2))
-        for blocks in (slice(0, 2), slice(2, 3)):
+        for blocks in (slice(0, 2), slice(2, final)):
             nc.vector.quantize_mx(
                 out=codes[:, blocks, :].rearrange("r b c -> r (b c)").bitcast(FP8X4),
                 scales=y_scales[:, blocks, :].rearrange("r b c -> r (b c)"),
                 in_=y_grouped[:, blocks, :].rearrange("r b c -> r (b c)"),
             )
-        rows = out_words.rearrange("(b p) t -> p b t", p=32)
+        word_rows = out_1[0].rearrange("p c i -> p (c i)").bitcast(I32).rearrange("(b r) t -> r b t", r=QUADRANT)
         for a in range(4):
-            nc.sync.dma_start(rows[:, 0:final, a * QUARTER : (a + 1) * QUARTER], codes[32 * a : 32 * (a + 1)].bitcast(I32))
+            source = codes[QUADRANT * a : QUADRANT * (a + 1)]
+            nc.sync.dma_start(word_rows[:, 0:final, a * QUARTER : (a + 1) * QUARTER], source.bitcast(I32))
         final_codes = held("final_codes", [P, QUARTER], U32)
-        for s, target in enumerate(back + across):
-            words = y_pairs[s][:].bitcast(F32)
-            for u in range(2):
-                nc.tensor.transpose(target[:, u * P : (u + 1) * P], words[:, u * P : (u + 1) * P], identity[:])
-            copy_on(
-                engines[s % 2],
-                y_grouped[:, final, :].bitcast(F32)[:, s * SPAN : (s + 1) * SPAN].rearrange("r (t u) -> r t u", u=2),
-                target[:, 0:SPAN].rearrange("r (u t) -> r t u", u=2),
+
+        def quantise_final(first, end):
+            cols = slice(first * P, end * P)
+            nc.vector.quantize_mx(
+                out=final_codes[:, cols].bitcast(FP8X4), scales=y_scales[:, final, cols],
+                in_=y_grouped[:, final, PACK * cols.start : PACK * cols.stop],
             )
-            if s % 2 == 1:
-                cols = slice((s - 1) * P, (s + 1) * P)
-                nc.vector.quantize_mx(
-                    out=final_codes[:, cols].bitcast(FP8X4), scales=y_scales[:, final, cols],
-                    in_=y_grouped[:, final, PACK * cols.start : PACK * cols.stop],
-                )
+
+        for s, target, engine in ((0, back[0], "scalar"), (1, back[1], "vector")):
+            turn_back(s, target, 0)
+            weave(final, s, 1, target, engine)
+        quantise_final(0, 2)
+        for s, target, engine in ((2, across[0], "vector"), (3, reset_bank, "scalar")):
+            turn_back(s, target, 0)
+            weave(final, s, 1, target, engine)
+            quantise_final(s, s + 1)
         for a in range(4):
-            nc.sync.dma_start(rows[:, final, a * QUARTER : (a + 1) * QUARTER], final_codes[32 * a : 32 * (a + 1), :].bitcast(I32))
-        scale_rows = out_2[0].rearrange("(b r) t -> r b t", r=4)
+            source = final_codes[QUADRANT * a : QUADRANT * (a + 1), :]
+            nc.sync.dma_start(word_rows[:, final, a * QUARTER : (a + 1) * QUARTER], source.bitcast(I32))
+        scale_rows = out_2[0].rearrange("(b s) t -> s b t", s=4)
         for a in range(4):
-            nc.sync.dma_start(
-                scale_rows[:, :, a * QUARTER : (a + 1) * QUARTER].bitcast(I32), y_scales[32 * a : 32 * a + 4].bitcast(I32)
-            )
+            source = y_scales[QUADRANT * a : QUADRANT * a + 4]
+            nc.sync.dma_start(scale_rows[:, :, a * QUARTER : (a + 1) * QUARTER].bitcast(I32), source.bitcast(I32))

@@ -24,10 +24,31 @@ HALF = 512
 HALVES = J // HALF
 BLOCKS = N // P
 SPAN = 2 * P
-QUARTER = T // 4
+QUARTERS = P // QUADRANT
+QUARTER = T // QUARTERS
 SLICES = QUARTER // P
 PAGES = 3
 STEP = 1024
+
+PLACES = {
+    "summed_of_1": 1,
+    "keep_gate_of_0": 0,
+    "reset_of_3": 0,
+    "late_z": 3,
+    "late_rn": 5,
+    "weighed_of_0": 4,
+    "w_raw_n0": 12,
+    "reset_of_0": 12,
+    "reset_of_2": 14,
+    "gated_of_1": 16,
+    "summed_of_0": 18,
+    "w_grouped_z": 18,
+    "moved_of_0": 17,
+    "moved_of_1": 19,
+    "w_raw_n1": 21,
+    "cand_of_0": 21,
+    "reset_of_1": 23,
+}
 
 
 def tile_list_tgn_gruP_kernel(
@@ -43,14 +64,14 @@ def tile_list_tgn_gruP_kernel(
         def held(name, shape, dtype, on=None):
             return keep.tile(shape, dtype, name=name, tag=on or name, align_bytes=64)
 
-        def placed(name, shape, dtype, steps):
-            return shared.tile(shape, dtype, name=name, align_bytes=64, offset=steps * STEP)
+        def placed(name, shape, dtype):
+            return shared.tile(shape, dtype, name=name, align_bytes=64, offset=PLACES[name] * STEP)
 
         def unit_tile(name, on=None):
             return held(name, [P, HALF], F32, on)[:]
 
-        def placed_unit_tile(name, steps):
-            return placed(name, [P, HALF], F32, steps)[:]
+        def placed_unit_tile(name):
+            return placed(name, [P, HALF], F32)[:]
 
         def bank(name):
             return psum.tile([P, HALF], F32, name=name)
@@ -67,8 +88,8 @@ def tile_list_tgn_gruP_kernel(
         w_raw = {
             (g, span): held("w_raw_%s%d" % (g, span), [P, PACK, SPAN], F32) for g in ("r", "z") for span in range(2)
         }
-        w_raw["n", 1] = placed("w_raw_n1", [P, PACK, SPAN], F32, 21)
-        w_raw["n", 0] = placed("w_raw_n0", [P, PACK, SPAN], F32, 12)
+        w_raw["n", 1] = placed("w_raw_n1", [P, PACK, SPAN], F32)
+        w_raw["n", 0] = placed("w_raw_n0", [P, PACK, SPAN], F32)
         u_words = {g: held("u_words_" + g, [P, 2 * N], U8) for g in gates}
         u_scales = {g: held("u_scales_" + g, [P, N], U8) for g in gates}
         bias_rows = held("bias_rows", [P, P], F32)
@@ -78,6 +99,11 @@ def tile_list_tgn_gruP_kernel(
         pages = [held("page_%d" % i, [P, T], F32) for i in range(PAGES)]
         identity = held("identity", [P, P], F32)
 
+        warm_in = held("warm_in", [P, 8], F32)
+        warm_out = held("warm_out", [P, 8], F32)
+        nc.vector.memset(warm_in[:], 0.0)
+        nc.scalar.activation(warm_out[:], warm_in[:], ACT.Sigmoid)
+
         nc.gpsimd.memset(bias_rows[:], 0.0)
         nc.gpsimd.memset(table_scales[:].bitcast(I32), 0)
         for g in gates:
@@ -85,9 +111,6 @@ def tile_list_tgn_gruP_kernel(
         make_identity(nc, identity[:])
         for page in pages:
             nc.vector.memset(page[:].bitcast(I32), 0)
-
-        warm_out = held("warm_out", [P, 8], F32)
-        nc.scalar.activation(warm_out[:], identity[:, 0:8], ACT.Sigmoid)
 
         def load_scale_rows(tile, dram):
             for q in range(4):
@@ -225,11 +248,11 @@ def tile_list_tgn_gruP_kernel(
         keep_gate = ring("keep_gate", 3, first=1)
         updated = ring("updated", 2, first=1)
         reset = ring("reset", 2, first=4)
-        reset[0] = placed_unit_tile("reset_of_0", 12)
-        reset[2] = placed_unit_tile("reset_of_2", 14)
-        gated = {1: placed_unit_tile("gated_of_1", 16), 2: unit_tile("gated_of_2")}
+        reset[0] = placed_unit_tile("reset_of_0")
+        reset[2] = placed_unit_tile("reset_of_2")
+        gated = {1: placed_unit_tile("gated_of_1"), 2: unit_tile("gated_of_2")}
         updated[0] = unit_tile("updated_of_0")
-        summed = {0: placed_unit_tile("summed_of_0", 18), 1: placed_unit_tile("summed_of_1", 1)}
+        summed = {0: placed_unit_tile("summed_of_0"), 1: placed_unit_tile("summed_of_1")}
         summed[2] = unit_tile("summed_of_2")
         gated[0] = summed[0]
         cand, moved, scaled = {}, {}, {}
@@ -287,7 +310,7 @@ def tile_list_tgn_gruP_kernel(
         y_pairs = [held("y_pairs_%d" % s, [P, HALF], BF16) for s in range(SLICES)]
         y_grouped = held("y_grouped", [P, BLOCKS, QUARTER * PACK], BF16)
 
-        def turn_out(b, s, target, engine, quarters=range(4)):
+        def turn_out(b, s, target, engine, quarters=range(QUARTERS)):
             for i, a in enumerate(quarters):
                 first = a * QUARTER + s * P
                 nc.tensor.transpose(target[:, i * P : (i + 1) * P], pages[b % PAGES][:, first : first + P], identity[:])
@@ -328,11 +351,11 @@ def tile_list_tgn_gruP_kernel(
         x_mx[1] = quantise("x_1", x_grouped_1[:], HALF)
         reset_gate(0)
         reset_gate(2)
-        late_rn = placed("late_rn", [P, 2, SPAN * PACK], BF16, 5)
+        late_rn = placed("late_rn", [P, 2, SPAN * PACK], BF16)
         round_rows(late_rn[:, 0, :], w_raw["r", 1][:], "scalar")
         round_rows(late_rn[:, 1, :], w_raw["n", 1][:], "scalar")
-        cand[0] = placed_unit_tile("cand_of_0", 21)
-        reset[1] = placed_unit_tile("reset_of_1", 23)
+        cand[0] = placed_unit_tile("cand_of_0")
+        reset[1] = placed_unit_tile("reset_of_1")
         state_product(0)
         message_product(0)
         state_product(2)
@@ -341,7 +364,7 @@ def tile_list_tgn_gruP_kernel(
         message_product(2)
         candidate_sum(0)
         candidate_tanh(0)
-        w_grouped_z = placed("w_grouped_z", [P, SPAN * PACK], BF16, 18)
+        w_grouped_z = placed("w_grouped_z", [P, SPAN * PACK], BF16)
         round_rows(w_grouped_z[:], w_raw["z", 0][:], "scalar")
         reset_gate(1)
         candidate_sum(2)
@@ -351,16 +374,16 @@ def tile_list_tgn_gruP_kernel(
         reset_state(1)
         candidate_sum(1)
         quantise_w("w_z", w_grouped_z[:], [("z", 0)])
-        moved[0] = placed_unit_tile("moved_of_0", 17)
+        moved[0] = placed_unit_tile("moved_of_0")
         scaled[0] = moved[0]
         difference(0)
         odd_cand = unit_tile("odd_cand", on="w_raw_z0")
         cand[1] = odd_cand
         candidate_tanh(1)
-        moved[1] = placed_unit_tile("moved_of_1", 19)
-        keep_gate[0] = placed_unit_tile("keep_gate_of_0", 0)
+        moved[1] = placed_unit_tile("moved_of_1")
+        keep_gate[0] = placed_unit_tile("keep_gate_of_0")
         update_gate(0)
-        late_z = placed("late_z", [P, SPAN * PACK], BF16, 3)
+        late_z = placed("late_z", [P, SPAN * PACK], BF16)
         round_rows(late_z[:], w_raw["z", 1][:], "scalar")
         even_cand = unit_tile("even_cand", on="w_raw_z1")
         for u in range(2, last + 1):
@@ -372,14 +395,14 @@ def tile_list_tgn_gruP_kernel(
         difference(1)
         add_candidate(nc.vector, 0)
         quantise_w("late_z", late_z[:], [("z", 1)])
-        weighed_of_0 = placed_unit_tile("weighed_of_0", 4)
+        weighed_of_0 = placed_unit_tile("weighed_of_0")
         weigh(nc.vector, weighed_of_0, 0)
         moved_later = unit_tile("moved_later", on="updated_of_0")
         for u in range(1, last + 1):
             scaled[u] = moved_later
         for u in range(2, last + 1):
             moved[u] = moved_later
-        reset[3] = placed_unit_tile("reset_of_3", 0)
+        reset[3] = placed_unit_tile("reset_of_3")
         reset_gate(3)
         candidate_tanh(2)
         state_product(3)
@@ -421,38 +444,36 @@ def tile_list_tgn_gruP_kernel(
             turn_out(final, s, sum_banks[s], engine)
         turn_out(final, SLICES - 1, message_bank, "scalar", range(0, 2))
         turn_out(final, SLICES - 1, across[1], "vector", range(2, 4))
-        codes = held("y_codes", [P, final, QUARTER], U32, on="updated_%d" % (last % 2))
-        for blocks in (slice(0, 2), slice(2, final)):
+        y_codes = held("y_codes", [P, BLOCKS, QUARTER], U32, on="updated_%d" % (last % 2))
+
+        def quantise_y(blocks, slices):
+            cols = slice(slices.start * P, slices.stop * P)
             nc.vector.quantize_mx(
-                out=codes[:, blocks, :].rearrange("r b c -> r (b c)").bitcast(FP8X4),
-                scales=y_scales[:, blocks, :].rearrange("r b c -> r (b c)"),
-                in_=y_grouped[:, blocks, :].rearrange("r b c -> r (b c)"),
+                out=y_codes[:, blocks, cols].rearrange("r b c -> r (b c)").bitcast(FP8X4),
+                scales=y_scales[:, blocks, cols].rearrange("r b c -> r (b c)"),
+                in_=y_grouped[:, blocks, PACK * cols.start : PACK * cols.stop].rearrange("r b c -> r (b c)"),
             )
+
         word_rows = out_1[0].rearrange("p c i -> p (c i)").bitcast(I32).rearrange("(b r) t -> r b t", r=QUADRANT)
-        for a in range(4):
-            source = codes[QUADRANT * a : QUADRANT * (a + 1)]
-            nc.sync.dma_start(word_rows[:, 0:final, a * QUARTER : (a + 1) * QUARTER], source.bitcast(I32))
-        final_codes = held("final_codes", [P, QUARTER], U32)
 
-        def quantise_final(first, end):
-            cols = slice(first * P, end * P)
-            nc.vector.quantize_mx(
-                out=final_codes[:, cols].bitcast(FP8X4), scales=y_scales[:, final, cols],
-                in_=y_grouped[:, final, PACK * cols.start : PACK * cols.stop],
-            )
+        def store_words(blocks):
+            for a in range(QUARTERS):
+                source = y_codes[QUADRANT * a : QUADRANT * (a + 1), blocks, :]
+                nc.sync.dma_start(word_rows[:, blocks, a * QUARTER : (a + 1) * QUARTER], source.bitcast(I32))
 
+        quantise_y(slice(0, 2), slice(0, SLICES))
+        store_words(slice(0, 2))
+        quantise_y(slice(2, final), slice(0, SLICES))
         for s, target, engine in ((0, back[0], "scalar"), (1, back[1], "vector")):
             turn_back(s, target, 0)
             weave(final, s, 1, target, engine)
-        quantise_final(0, 2)
+        quantise_y(slice(final, BLOCKS), slice(0, 2))
         for s, target, engine in ((2, across[0], "vector"), (3, reset_bank, "scalar")):
             turn_back(s, target, 0)
             weave(final, s, 1, target, engine)
-            quantise_final(s, s + 1)
-        for a in range(4):
-            source = final_codes[QUADRANT * a : QUADRANT * (a + 1), :]
-            nc.sync.dma_start(word_rows[:, final, a * QUARTER : (a + 1) * QUARTER], source.bitcast(I32))
-        scale_rows = out_2[0].rearrange("(b s) t -> s b t", s=4)
-        for a in range(4):
+            quantise_y(slice(final, BLOCKS), slice(s, s + 1))
+        store_words(slice(2, BLOCKS))
+        scale_rows = out_2[0].rearrange("(b j) t -> j b t", j=4)
+        for a in range(QUARTERS):
             source = y_scales[QUADRANT * a : QUADRANT * a + 4]
             nc.sync.dma_start(scale_rows[:, :, a * QUARTER : (a + 1) * QUARTER].bitcast(I32), source.bitcast(I32))

@@ -386,8 +386,9 @@ def tile_list_tgn_gruP_kernel(
         late_z = placed("late_z", [P, SPAN * PACK], BF16)
         round_rows(late_z[:], w_raw["z", 1][:], "scalar")
         even_cand = unit_tile("even_cand", on="w_raw_z1")
+        cand_ring = [unit_tile("third_cand"), odd_cand, even_cand]
         for u in range(2, last + 1):
-            cand[u] = odd_cand if u % 2 else even_cand
+            cand[u] = cand_ring[u % 3]
         for u in range(3, last + 1):
             gated[u] = summed[u] = cand[u]
         update_gate(1)
@@ -398,10 +399,10 @@ def tile_list_tgn_gruP_kernel(
         weighed_of_0 = placed_unit_tile("weighed_of_0")
         weigh(nc.vector, weighed_of_0, 0)
         moved_later = unit_tile("moved_later", on="updated_of_0")
-        for u in range(1, last + 1):
-            scaled[u] = moved_later
+        scaled[1] = moved_later
+        picked = ring("picked", 3, first=2)
         for u in range(2, last + 1):
-            moved[u] = moved_later
+            scaled[u] = picked[u]
         reset[3] = placed_unit_tile("reset_of_3")
         reset_gate(3)
         candidate_tanh(2)
@@ -411,23 +412,51 @@ def tile_list_tgn_gruP_kernel(
         update_gate(3)
         nc.vector.tensor_copy(window(0), weighed_of_0)
 
+        def pick(u):
+            b, c = units[u]
+            nc.vector.tensor_copy(picked[u], state[b][:].indirect(listed(c)))
+
+        pick(2)
+
+        def prepare(u):
+            reset_state(u)
+            pick(u)
+            candidate_sum(u)
+            candidate_tanh(u)
+
+        def products(u):
+            reset_gate(u)
+            state_product(u)
+            message_product(u)
+            update_gate(u)
+
+        prepare(3)
+        scale_by_keep(nc.gpsimd, 1)
+        products(4)
+        unweighed = unit_tile("unweighed")
+        for u in range(2, last + 1):
+            moved[u] = unweighed
+
+        def subtract(u):
+            nc.gpsimd.tensor_tensor(moved[u], picked[u], cand[u], ALU.subtract)
+
         for u in range(1, last + 1):
-            scale_by_keep(nc.gpsimd, u)
-            add_candidate(nc.gpsimd, u)
-            if u < last:
+            if u in (1, last - 1):
+                nc.gpsimd.tensor_tensor(unweighed, scaled[u], cand[u], ALU.add)
+                nc.gpsimd.tensor_tensor(updated[u], unweighed, event_weight[units[u][1]][:], ALU.mult)
+                subtract(u + 1)
+                scale_by_keep(nc.gpsimd, u + 1)
+            elif u < last:
+                subtract(u + 1)
+                add_candidate(nc.gpsimd, u)
+                scale_by_keep(nc.gpsimd, u + 1)
                 weigh(nc.gpsimd, updated[u], u)
-            if u + 2 <= last:
-                reset_state(u + 2)
-            if u + 1 <= last:
-                difference(u + 1)
-            if u + 2 <= last:
-                candidate_sum(u + 2)
-                candidate_tanh(u + 2)
+            else:
+                add_candidate(nc.gpsimd, u)
             if u + 3 <= last:
-                reset_gate(u + 3)
-                state_product(u + 3)
-                message_product(u + 3)
-                update_gate(u + 3)
+                prepare(u + 3)
+            if u + 4 <= last:
+                products(u + 4)
             if u == PAGES * HALVES:
                 regroup(0, across)
             if u < last:

@@ -31,23 +31,28 @@ PAGES = 3
 STEP = 1024
 
 PLACES = {
-    "summed_of_1": 1,
-    "keep_gate_of_0": 0,
-    "reset_of_3": 0,
-    "late_z": 3,
-    "late_rn": 5,
-    "weighed_of_0": 4,
-    "w_raw_n0": 12,
-    "reset_of_0": 12,
-    "reset_of_2": 14,
-    "gated_of_1": 16,
-    "summed_of_0": 18,
-    "w_grouped_z": 18,
-    "moved_of_0": 17,
-    "moved_of_1": 19,
-    "w_raw_n1": 21,
-    "cand_of_0": 21,
-    "reset_of_1": 23,
+    "x_raw_1": 0,
+    "cand_of_0": 0,
+    "cand_of_2": 2,
+    "late_rn": 4,
+    "late_z": 8,
+    "updated_odd": 7,
+    "picked_of_3": 4,
+    "moved_of_0": 12,
+    "cand_of_1": 11,
+    "summed_of_3": 13,
+    "w_raw_n0": 15,
+    "reset_of_0": 15,
+    "reset_of_2": 17,
+    "x_raw_0": 19,
+    "w_grouped_r": 27,
+    "page_2": 20,
+    "gated_of_2": 33,
+    "w_z_scales": 33,
+    "first_spare": 35,
+    "picked_of_1": 37,
+    "spare": 36,
+    "unweighed_of_2": 38,
 }
 
 
@@ -79,24 +84,22 @@ def tile_list_tgn_gruP_kernel(
         gates = ("r", "n", "z")
         w_dram = {"r": wr, "n": wn, "z": wz}
         u_words_dram = {"r": ur_words, "n": un_words, "z": uz_words}
-        u_scales_dram = {"r": ur_scales, "n": un_scales, "z": uz_scales}
-        bias_dram = {"r": br, "n": bn, "z": bz}
 
         offsets = keep.tile([P, J // 16], U16, name="offsets")
         table_words = held("table_words", [P, T], I32)
         table_scales = held("table_scales", [P, T], U8)
-        w_raw = {
-            (g, span): held("w_raw_%s%d" % (g, span), [P, PACK, SPAN], F32) for g in ("r", "z") for span in range(2)
-        }
-        w_raw["n", 1] = placed("w_raw_n1", [P, PACK, SPAN], F32)
+        w_raw = {(g, 1): held("w_raw_%s1" % g, [P, PACK, SPAN], F32) for g in gates}
+        w_raw["r", 0] = held("w_raw_r0", [P, PACK, SPAN], F32)
         w_raw["n", 0] = placed("w_raw_n0", [P, PACK, SPAN], F32)
+        w_raw["z", 0] = held("w_raw_z0", [P, PACK, SPAN], F32)
         u_words = {g: held("u_words_" + g, [P, 2 * N], U8) for g in gates}
         u_scales = {g: held("u_scales_" + g, [P, N], U8) for g in gates}
-        bias_rows = held("bias_rows", [P, P], F32)
-        x_raw = [held("x_raw_%d" % c, [P, PACK, HALF], F32) for c in range(HALVES)]
+        bias_dram = {"r": br, "n": bn, "z": bz}
+        bias_rows = {g: held("bias_rows_" + g, [P, P], F32) for g in gates}
+        x_raw = [placed("x_raw_0", [P, PACK, HALF], F32), placed("x_raw_1", [P, PACK, HALF], F32)]
         state = [held("state_%d" % b, [P, T], F32) for b in range(BLOCKS)]
-        event_weight = [held("event_weight_%d" % c, [P, HALF], F32) for c in range(HALVES)]
-        pages = [held("page_%d" % i, [P, T], F32) for i in range(PAGES)]
+        event_weight = [unit_tile("event_weight_%d" % c) for c in range(HALVES)]
+        pages = [held("page_%d" % i, [P, T], F32) for i in range(PAGES - 1)]
         identity = held("identity", [P, P], F32)
 
         warm_in = held("warm_in", [P, 8], F32)
@@ -104,10 +107,11 @@ def tile_list_tgn_gruP_kernel(
         nc.vector.memset(warm_in[:], 0.0)
         nc.scalar.activation(warm_out[:], warm_in[:], ACT.Sigmoid)
 
-        nc.gpsimd.memset(bias_rows[:], 0.0)
-        nc.gpsimd.memset(table_scales[:].bitcast(I32), 0)
+        nc.vector.memset(table_scales[:].bitcast(I32), 0)
         for g in gates:
-            nc.gpsimd.memset(u_scales[g][:].bitcast(I32), 0)
+            nc.vector.memset(u_scales[g][:].bitcast(I32), 0)
+        for g in gates:
+            nc.vector.memset(bias_rows[g][:], 0.0)
         make_identity(nc, identity[:])
         for page in pages:
             nc.vector.memset(page[:].bitcast(I32), 0)
@@ -126,34 +130,37 @@ def tile_list_tgn_gruP_kernel(
         def load_u_words(g):
             nc.sync.dma_start(u_words[g][:].bitcast(I32), u_words_dram[g][0].bitcast(I32))
 
+        def load_bias(g):
+            nc.sync.dma_start(bias_rows[g][0:BLOCKS, :], bias_dram[g].rearrange("(b q) -> b q", q=P))
+
         def load_state(b):
             nc.sync.dma_start(state[b][:], hT[b * P : (b + 1) * P, :])
 
         nc.sync.dma_start(offsets[:], offs)
         nc.sync.dma_start(table_words[:], tab_words[0].rearrange("p c i -> p (c i)").bitcast(I32))
-        for i, g in enumerate(gates):
-            rows = bias_rows[QUADRANT * i : QUADRANT * i + BLOCKS, :]
-            nc.sync.dma_start(rows, bias_dram[g].rearrange("(b q) -> b q", q=P))
-        load_rows(x_raw[0], x[:, 0:HALF])
         load_scale_rows(table_scales, tab_scales)
+        load_rows(x_raw[0], x[:, 0:HALF])
         load_w("r", 0)
+        load_bias("r")
         load_u_words("r")
-        load_w("n", 0)
         load_scale_rows(u_scales["r"], ur_scales)
-        load_rows(x_raw[1], x[:, HALF:J])
+        load_w("n", 0)
         load_u_words("n")
-        load_scale_rows(u_scales["n"], un_scales)
-        load_w("r", 1)
-        load_w("n", 1)
         load_w("z", 0)
-        load_state(0)
+        load_bias("n")
+        load_scale_rows(u_scales["n"], un_scales)
+        load_rows(x_raw[1], x[:, HALF:J])
+        load_bias("z")
         load_u_words("z")
         load_scale_rows(u_scales["z"], uz_scales)
-        load_w("z", 1)
-        for c in range(HALVES):
-            nc.sync.dma_start(event_weight[c][:], wgo[:, c * HALF : (c + 1) * HALF])
-        for b in range(1, BLOCKS):
-            load_state(b)
+        load_state(0)
+        load_state(1)
+        nc.sync.dma_start(event_weight[0], wgo[:, 0:HALF])
+        for g in gates:
+            load_w(g, 1)
+        load_state(2)
+        nc.sync.dma_start(event_weight[1], wgo[:, HALF:J])
+        load_state(3)
 
         def listed(c):
             return offsets[:, c * (HALF // 16) : (c + 1) * (HALF // 16)]
@@ -162,25 +169,29 @@ def tile_list_tgn_gruP_kernel(
         picked_scales = [held("picked_scales_%d" % c, [P, HALF], U8) for c in range(HALVES)]
         for c in range(HALVES):
             nc.vector.tensor_copy(picked_words[c][:], table_words[:].bitcast(U32).indirect(listed(c)))
-        for c in range(HALVES):
-            nc.vector.tensor_copy(picked_scales[c][:], table_scales[:].indirect(listed(c)))
+        nc.vector.tensor_copy(picked_scales[0][:], table_scales[:].indirect(listed(0)))
 
         def copy_on(engine, out, in_):
             if engine == "scalar":
                 nc.scalar.copy(out, in_)
+            elif engine == "gpsimd":
+                nc.gpsimd.tensor_scalar(out, in_, 1.0, 0.0, ALU.mult, ALU.add)
             else:
                 nc.vector.tensor_copy(out, in_)
 
         def round_rows(grouped, raw, engine):
-            copy_on(
-                engine,
-                grouped.rearrange("p (c d i) -> p c i d", d=4, i=PACK),
-                raw.rearrange("p i (c d) -> p c i d", d=4),
-            )
+            if engine == "gpsimd":
+                copy_on(engine, grouped.rearrange("p (c i) -> p c i", i=PACK), raw.rearrange("p i c -> p c i"))
+            else:
+                copy_on(
+                    engine,
+                    grouped.rearrange("p (c d i) -> p c i d", d=4, i=PACK),
+                    raw.rearrange("p i (c d) -> p c i d", d=4),
+                )
 
         def quantise(name, grouped, width, on=None):
             codes = held(name + "_codes", [P, width], U32)
-            scales = held(name + "_scales", [P, width], U8, on)
+            scales = (placed if name + "_scales" in PLACES else held)(name + "_scales", [P, width], U8)
             nc.vector.quantize_mx(out=codes[:].bitcast(FP8X4), scales=scales[:], in_=grouped)
             return codes, scales
 
@@ -194,25 +205,34 @@ def tile_list_tgn_gruP_kernel(
                     w_mx[g, 2 * span + b] = (codes[:, cols], scales[:, cols])
 
         x_grouped_0 = held("x_grouped_0", [P, HALF * PACK], BF16)
-        w_grouped_r = held("w_grouped_r", [P, SPAN * PACK], BF16)
+        w_grouped_r = placed("w_grouped_r", [P, SPAN * PACK], BF16)
         w_grouped_n = held("w_grouped_n", [P, SPAN * PACK], BF16)
 
         across = [bank("across_%d" % i) for i in range(2)]
         back = [bank("back_%d" % i) for i in range(2)]
 
-        bias = held("bias", [P, 2, BLOCKS], F32)
-        minus_bias_z = held("minus_bias_z", [P, BLOCKS], F32)
-        nc.tensor.transpose(back[1][:, 0:P], bias_rows[:], identity[:])
-        turned_bias = back[1][:, 0 : 2 * QUADRANT].rearrange("q (g b) -> q g b", g=2)
-        nc.scalar.copy(bias[:], turned_bias[:, :, 0:BLOCKS])
-        nc.scalar.activation(minus_bias_z[:], back[1][:, 2 * QUADRANT : 2 * QUADRANT + BLOCKS], ACT.Copy, scale=-1.0)
+        bias = {g: held("bias_" + g, [P, BLOCKS], F32) for g in gates}
 
-        round_rows(x_grouped_0[:], x_raw[0][:], "scalar")
+        def turn_bias(g, target, sign):
+            nc.tensor.transpose(target[:, 0:P], bias_rows[g][:], identity[:])
+            nc.scalar.activation(bias[g][:], target[:, 0:BLOCKS], ACT.Copy, scale=sign)
+
+        def round_x(grouped, c, engines):
+            share = HALF // len(engines)
+            for i, engine in enumerate(engines):
+                cols = slice(i * share, (i + 1) * share)
+                round_rows(grouped[:, PACK * cols.start : PACK * cols.stop], x_raw[c][:, :, cols], engine)
+
+        round_x(x_grouped_0, 0, ("scalar", "gpsimd"))
         round_rows(w_grouped_r[:], w_raw["r", 0][:], "scalar")
+        turn_bias("r", back[1], 1.0)
         round_rows(w_grouped_n[:], w_raw["n", 0][:], "scalar")
-        x_mx[0] = quantise("x_0", x_grouped_0[:], HALF, on="table_scales")
-        quantise_w("w_r", w_grouped_r[:], [("r", 0)], on="x_grouped_0")
-        quantise_w("w_n", w_grouped_n[:], [("n", 0)], on="w_grouped_r")
+        x_mx[0] = quantise("x_0", x_grouped_0[:], HALF)
+        quantise_w("w_r", w_grouped_r[:], [("r", 0)])
+        nc.vector.tensor_copy(picked_scales[1][:], table_scales[:].indirect(listed(1)))
+        quantise_w("w_n", w_grouped_n[:], [("n", 0)])
+        pages.append(placed("page_2", [P, T], F32))
+        nc.vector.memset(pages[2][:].bitcast(I32), 0)
 
         units = [(b, c) for b in range(BLOCKS) for c in range(HALVES)]
         last = len(units) - 1
@@ -241,27 +261,31 @@ def tile_list_tgn_gruP_kernel(
         sr = {u: reset_bank for u in range(last + 1)}
         hn = {u: state_bank for u in range(last + 1)}
         xn = {u: message_bank for u in range(last + 1)}
-        sr[2], hn[2], xn[2] = message_bank, across[0], across[0]
-        sr[1], hn[1], xn[1] = state_bank, message_bank, reset_bank
-        xn[0] = reset_bank
+        sr[2], sr[1] = across[0], update_bank
+        hn[2] = hn[3] = across[1]
+        for u in range(4):
+            xn[u] = hn[u]
+        sz = {u: update_bank for u in range(last + 1)}
+        sz[1] = reset_bank
 
-        keep_gate = ring("keep_gate", 3, first=1)
-        updated = ring("updated", 2, first=1)
-        reset = ring("reset", 2, first=4)
-        reset[0] = placed_unit_tile("reset_of_0")
-        reset[2] = placed_unit_tile("reset_of_2")
-        gated = {1: placed_unit_tile("gated_of_1"), 2: unit_tile("gated_of_2")}
-        updated[0] = unit_tile("updated_of_0")
-        summed = {0: placed_unit_tile("summed_of_0"), 1: placed_unit_tile("summed_of_1")}
-        summed[2] = unit_tile("summed_of_2")
-        gated[0] = summed[0]
-        cand, moved, scaled = {}, {}, {}
+        keep_gate = ring("keep_gate", 2, first=0)
+        reset = ring("reset", 2, first=1)
+        reset[0], reset[2] = placed_unit_tile("reset_of_0"), placed_unit_tile("reset_of_2")
+        reset[3] = unit_tile("reset_of_3")
+        picked = ring("picked", 2, first=2)
+        picked[1] = placed_unit_tile("picked_of_1")
+        summed = {u: unit_tile("summed_of_%d" % u) for u in (0, 2)}
+        gated = {0: summed[0], 2: placed_unit_tile("gated_of_2")}
+        cand, moved, scaled, updated = {}, {}, {}, {}
+
+        def reset_sigmoid(u):
+            b = units[u][0]
+            nc.scalar.activation(reset[u], sr[u][:], ACT.Sigmoid, bias=bias["r"][:, b : b + 1])
 
         def reset_gate(u):
-            b = units[u][0]
-            state_pass(sr[u], "r", u, True, False)
-            message_pass(sr[u], "r", u, False, True)
-            nc.scalar.activation(reset[u], sr[u][:], ACT.Sigmoid, bias=bias[:, 0, b : b + 1])
+            message_pass(sr[u], "r", u, True, False)
+            state_pass(sr[u], "r", u, False, True)
+            reset_sigmoid(u)
 
         def state_product(u):
             state_pass(hn[u], "n", u, True, True)
@@ -271,9 +295,10 @@ def tile_list_tgn_gruP_kernel(
 
         def update_gate(u):
             b = units[u][0]
-            state_pass(update_bank, "z", u, True, False)
-            message_pass(update_bank, "z", u, False, True)
-            nc.scalar.activation(keep_gate[u], update_bank[:], ACT.Sigmoid, bias=minus_bias_z[:, b : b + 1], scale=-1.0)
+            first, second = (state_pass, message_pass) if u < 2 else (message_pass, state_pass)
+            first(sz[u], "z", u, True, False)
+            second(sz[u], "z", u, False, True)
+            nc.scalar.activation(keep_gate[u], sz[u][:], ACT.Sigmoid, bias=bias["z"][:, b : b + 1], scale=-1.0)
 
         def reset_state(u):
             nc.vector.tensor_tensor(gated[u], hn[u][:], reset[u], ALU.mult)
@@ -283,7 +308,7 @@ def tile_list_tgn_gruP_kernel(
 
         def candidate_tanh(u):
             b = units[u][0]
-            nc.scalar.activation(cand[u], summed[u], ACT.Tanh, bias=bias[:, 1, b : b + 1])
+            nc.scalar.activation(cand[u], summed[u], ACT.Tanh, bias=bias["n"][:, b : b + 1])
 
         def difference(u):
             b, c = units[u]
@@ -296,7 +321,7 @@ def tile_list_tgn_gruP_kernel(
             engine.tensor_tensor(updated[u], scaled[u], cand[u], ALU.add)
 
         def weigh(engine, out, u):
-            engine.tensor_tensor(out, updated[u], event_weight[units[u][1]][:], ALU.mult)
+            engine.tensor_tensor(out, updated[u], event_weight[units[u][1]], ALU.mult)
 
         def window(u):
             b, c = units[u]
@@ -346,115 +371,127 @@ def tile_list_tgn_gruP_kernel(
 
         y_scales = held("y_scales", [P, BLOCKS, QUARTER], U8)
 
-        x_grouped_1 = held("x_grouped_1", [P, HALF * PACK], BF16, on="w_grouped_n")
-        round_rows(x_grouped_1[:], x_raw[1][:], "vector")
-        x_mx[1] = quantise("x_1", x_grouped_1[:], HALF)
-        reset_gate(0)
-        reset_gate(2)
-        late_rn = placed("late_rn", [P, 2, SPAN * PACK], BF16)
-        round_rows(late_rn[:, 0, :], w_raw["r", 1][:], "scalar")
-        round_rows(late_rn[:, 1, :], w_raw["n", 1][:], "scalar")
-        cand[0] = placed_unit_tile("cand_of_0")
-        reset[1] = placed_unit_tile("reset_of_1")
-        state_product(0)
-        message_product(0)
-        state_product(2)
-        reset_state(0)
-        reset_state(2)
-        message_product(2)
-        candidate_sum(0)
-        candidate_tanh(0)
-        w_grouped_z = placed("w_grouped_z", [P, SPAN * PACK], BF16)
-        round_rows(w_grouped_z[:], w_raw["z", 0][:], "scalar")
-        reset_gate(1)
-        candidate_sum(2)
-        quantise_w("late_rn", late_rn[:].rearrange("p g c -> p (g c)"), [("r", 1), ("n", 1)], on="gated_of_2")
-        state_product(1)
-        message_product(1)
-        reset_state(1)
-        candidate_sum(1)
-        quantise_w("w_z", w_grouped_z[:], [("z", 0)])
-        moved[0] = placed_unit_tile("moved_of_0")
-        scaled[0] = moved[0]
-        difference(0)
-        odd_cand = unit_tile("odd_cand", on="w_raw_z0")
-        cand[1] = odd_cand
-        candidate_tanh(1)
-        moved[1] = placed_unit_tile("moved_of_1")
-        keep_gate[0] = placed_unit_tile("keep_gate_of_0")
-        update_gate(0)
-        late_z = placed("late_z", [P, SPAN * PACK], BF16)
-        round_rows(late_z[:], w_raw["z", 1][:], "scalar")
-        even_cand = unit_tile("even_cand", on="w_raw_z1")
-        cand_ring = [unit_tile("third_cand"), odd_cand, even_cand]
-        for u in range(2, last + 1):
-            cand[u] = cand_ring[u % 3]
-        for u in range(3, last + 1):
-            gated[u] = summed[u] = cand[u]
-        update_gate(1)
-        scale_by_keep(nc.vector, 0)
-        difference(1)
-        add_candidate(nc.vector, 0)
-        quantise_w("late_z", late_z[:], [("z", 1)])
-        weighed_of_0 = placed_unit_tile("weighed_of_0")
-        weigh(nc.vector, weighed_of_0, 0)
-        moved_later = unit_tile("moved_later", on="updated_of_0")
-        scaled[1] = moved_later
-        picked = ring("picked", 3, first=2)
-        for u in range(2, last + 1):
-            scaled[u] = picked[u]
-        reset[3] = placed_unit_tile("reset_of_3")
-        reset_gate(3)
-        candidate_tanh(2)
-        state_product(3)
-        message_product(3)
-        update_gate(2)
-        update_gate(3)
-        nc.vector.tensor_copy(window(0), weighed_of_0)
-
         def pick(u):
             b, c = units[u]
             nc.vector.tensor_copy(picked[u], state[b][:].indirect(listed(c)))
 
-        pick(2)
-
-        def prepare(u):
-            reset_state(u)
-            pick(u)
-            candidate_sum(u)
-            candidate_tanh(u)
+        def subtract(u):
+            nc.gpsimd.tensor_tensor(moved[u], picked[u], cand[u], ALU.subtract)
 
         def products(u):
             reset_gate(u)
             state_product(u)
             message_product(u)
-            update_gate(u)
 
-        prepare(3)
+        for u in (0, 2):
+            state_pass(sr[u], "r", u, True, False)
+        for u in (0, 2):
+            message_pass(sr[u], "r", u, False, True)
+            reset_sigmoid(u)
+            state_product(u)
+        turn_bias("n", back[0], 1.0)
+        w_grouped_z = held("w_grouped_z", [P, SPAN * PACK], BF16)
+        round_rows(w_grouped_z[:], w_raw["z", 0][:], "scalar")
+        for step in (reset_state, message_product, candidate_sum):
+            for u in (0, 2):
+                step(u)
+        quantise_w("w_z", w_grouped_z[:], [("z", 0)])
+        x_grouped_1 = held("x_grouped_1", [P, HALF * PACK], BF16)
+        round_x(x_grouped_1, 1, ("gpsimd", "scalar"))
+        x_mx[1] = quantise("x_1", x_grouped_1[:], HALF)
+        turn_bias("z", back[1], -1.0)
+        cand[0], cand[2] = placed_unit_tile("cand_of_0"), placed_unit_tile("cand_of_2")
+        candidate_tanh(0)
+        update_gate(0)
+        moved[0] = placed_unit_tile("moved_of_0")
+        difference(0)
+        pick(1)
+        scaled[0] = summed[0]
+        scale_by_keep(nc.gpsimd, 0)
+        cand[1] = gated[1] = summed[1] = placed_unit_tile("cand_of_1")
+        gated[3] = summed[3] = placed_unit_tile("summed_of_3")
+        reset_gate(1)
+        update_gate(1)
+        reset_gate(3)
+        for u in (1, 3):
+            state_product(u)
+        candidate_tanh(2)
+        for step in (reset_state, message_product, candidate_sum):
+            for u in (1, 3):
+                step(u)
+        candidate_tanh(1)
+        update_gate(2)
+        pick(2)
+
+        late_rn = placed("late_rn", [P, 2, SPAN * PACK], BF16)
+        late_z = placed("late_z", [P, SPAN * PACK], BF16)
+        round_rows(late_rn[:, 0, :], w_raw["r", 1][:], "scalar")
+        round_rows(late_rn[:, 1, :], w_raw["n", 1][:], "scalar")
+        cand[3] = unit_tile("cand_of_3", on="w_raw_n1")
+        candidate_tanh(3)
+        for u in range(4, last + 1):
+            cand[u] = gated[u] = summed[u] = cand[u - 3]
+        round_rows(late_z[:], w_raw["z", 1][:], "scalar")
+
+        first_spare = placed_unit_tile("first_spare")
+        updated_even = unit_tile("updated_even")
+        for u in range(1, last + 1):
+            scaled[u] = picked[u]
+        moved[1] = moved[2] = first_spare
+
+        def add_into(out, u):
+            nc.gpsimd.tensor_tensor(out, scaled[u], cand[u], ALU.add)
+
+        def weigh_from(source, u):
+            nc.gpsimd.tensor_tensor(updated[u], source, event_weight[units[u][1]], ALU.mult)
+
+        updated[0] = updated_even
+        add_into(first_spare, 0)
+        weigh_from(first_spare, 0)
+        subtract(1)
         scale_by_keep(nc.gpsimd, 1)
+        keep_gate[3] = unit_tile("keep_gate_of_3", on="w_raw_z1")
+        update_gate(3)
+        nc.vector.tensor_copy(window(0), updated_even)
+        quantise_w("late_rn", late_rn[:].rearrange("p g c -> p (g c)"), [("r", 1), ("n", 1)])
+        quantise_w("late_z", late_z[:], [("z", 1)])
+        picked[3] = scaled[3] = picked[6] = scaled[6] = placed_unit_tile("picked_of_3")
+        picked[4] = scaled[4] = picked[7] = scaled[7] = picked[1 + HALVES * 2 + 2]
+        picked[5] = scaled[5] = picked[2]
+        pick(3)
+        updated_odd = placed_unit_tile("updated_odd")
+        for u in range(last + 1):
+            updated[u] = updated_odd if u % 2 else updated_even
         products(4)
-        unweighed = unit_tile("unweighed")
-        for u in range(2, last + 1):
-            moved[u] = unweighed
-
-        def subtract(u):
-            nc.gpsimd.tensor_tensor(moved[u], picked[u], cand[u], ALU.subtract)
 
         for u in range(1, last + 1):
-            if u in (1, last - 1):
-                nc.gpsimd.tensor_tensor(unweighed, scaled[u], cand[u], ALU.add)
-                nc.gpsimd.tensor_tensor(updated[u], unweighed, event_weight[units[u][1]][:], ALU.mult)
+            if u == 2:
+                spare = placed_unit_tile("spare")
+                for later in range(3, last + 1):
+                    moved[later] = spare
+            unweighed = updated[u]
+            if u == 1:
+                unweighed = scaled[u]
+            if u == 2:
+                unweighed = placed_unit_tile("unweighed_of_2")
+            if u == last - 1:
+                add_into(spare, u)
+                weigh_from(spare, u)
                 subtract(u + 1)
                 scale_by_keep(nc.gpsimd, u + 1)
             elif u < last:
                 subtract(u + 1)
-                add_candidate(nc.gpsimd, u)
+                add_into(unweighed, u)
                 scale_by_keep(nc.gpsimd, u + 1)
-                weigh(nc.gpsimd, updated[u], u)
+                weigh_from(unweighed, u)
             else:
-                add_candidate(nc.gpsimd, u)
+                add_into(unweighed, u)
             if u + 3 <= last:
-                prepare(u + 3)
+                update_gate(u + 3)
+                reset_state(u + 3)
+                pick(u + 3)
+                candidate_sum(u + 3)
+                candidate_tanh(u + 3)
             if u + 4 <= last:
                 products(u + 4)
             if u == PAGES * HALVES:
@@ -473,7 +510,7 @@ def tile_list_tgn_gruP_kernel(
             turn_out(final, s, sum_banks[s], engine)
         turn_out(final, SLICES - 1, message_bank, "scalar", range(0, 2))
         turn_out(final, SLICES - 1, across[1], "vector", range(2, 4))
-        y_codes = held("y_codes", [P, BLOCKS, QUARTER], U32, on="updated_%d" % (last % 2))
+        y_codes = held("y_codes", [P, BLOCKS, QUARTER], U32, on="picked_1")
 
         def quantise_y(blocks, slices):
             cols = slice(slices.start * P, slices.stop * P)
@@ -485,13 +522,14 @@ def tile_list_tgn_gruP_kernel(
 
         word_rows = out_1[0].rearrange("p c i -> p (c i)").bitcast(I32).rearrange("(b r) t -> r b t", r=QUADRANT)
 
-        def store_words(blocks):
+        def store_words(blocks, queues):
             for a in range(QUARTERS):
                 source = y_codes[QUADRANT * a : QUADRANT * (a + 1), blocks, :]
-                nc.sync.dma_start(word_rows[:, blocks, a * QUARTER : (a + 1) * QUARTER], source.bitcast(I32))
+                target = word_rows[:, blocks, a * QUARTER : (a + 1) * QUARTER]
+                queues[a % len(queues)].dma_start(target, source.bitcast(I32))
 
         quantise_y(slice(0, 2), slice(0, SLICES))
-        store_words(slice(0, 2))
+        store_words(slice(0, 2), [nc.sync])
         quantise_y(slice(2, final), slice(0, SLICES))
         for s, target, engine in ((0, back[0], "scalar"), (1, back[1], "vector")):
             turn_back(s, target, 0)
@@ -501,7 +539,7 @@ def tile_list_tgn_gruP_kernel(
             turn_back(s, target, 0)
             weave(final, s, 1, target, engine)
             quantise_y(slice(final, BLOCKS), slice(s, s + 1))
-        store_words(slice(2, BLOCKS))
+        store_words(slice(2, BLOCKS), [nc.sync])
         scale_rows = out_2[0].rearrange("(b j) t -> j b t", j=4)
         for a in range(QUARTERS):
             source = y_scales[QUADRANT * a : QUADRANT * a + 4]

@@ -33,26 +33,30 @@ STEP = 1024
 PLACES = {
     "x_raw_1": 0,
     "cand_of_0": 0,
-    "cand_of_2": 2,
-    "late_rn": 4,
-    "late_z": 8,
-    "updated_odd": 7,
-    "picked_of_3": 4,
-    "moved_of_0": 12,
-    "cand_of_1": 11,
-    "summed_of_3": 13,
-    "w_raw_n0": 15,
-    "reset_of_0": 15,
-    "reset_of_2": 17,
-    "x_raw_0": 19,
-    "w_grouped_r": 27,
-    "page_2": 20,
-    "gated_of_2": 33,
-    "w_z_scales": 33,
-    "first_spare": 35,
-    "picked_of_1": 37,
-    "spare": 36,
-    "unweighed_of_2": 38,
+    "cand_of_block_1": 2,
+    "late_rn": 9,
+    "late_z": 13,
+    "picked_of_block_2": 6,
+    "unweighed_of_1": 12,
+    "updated_of_1": 14,
+    "scaled_of_block_1": 10,
+    "moved_of_0": 42,
+    "gated_of_3": 41,
+    "gated_of_1": 43,
+    "picked_of_block_1": 44,
+    "gated_of_5": 48,
+    "picked_of_block_3": 48,
+    "w_raw_n0": 18,
+    "reset_of_0": 18,
+    "reset_of_2": 20,
+    "x_raw_0": 22,
+    "w_grouped_r": 30,
+    "page_2": 23,
+    "gated_of_2": 32,
+    "w_z_scales": 32,
+    "spare": 34,
+    "wide_spare": 34,
+    "y_codes": 37,
 }
 
 
@@ -98,7 +102,8 @@ def tile_list_tgn_gruP_kernel(
         bias_rows = {g: held("bias_rows_" + g, [P, P], F32) for g in gates}
         x_raw = [placed("x_raw_0", [P, PACK, HALF], F32), placed("x_raw_1", [P, PACK, HALF], F32)]
         state = [held("state_%d" % b, [P, T], F32) for b in range(BLOCKS)]
-        event_weight = [unit_tile("event_weight_%d" % c) for c in range(HALVES)]
+        both_weights = held("event_weight", [P, J], F32)
+        event_weight = [both_weights[:, c * HALF : (c + 1) * HALF] for c in range(HALVES)]
         pages = [held("page_%d" % i, [P, T], F32) for i in range(PAGES - 1)]
         identity = held("identity", [P, P], F32)
 
@@ -156,20 +161,21 @@ def tile_list_tgn_gruP_kernel(
         load_state(0)
         load_state(1)
         nc.sync.dma_start(event_weight[0], wgo[:, 0:HALF])
-        for g in gates:
-            load_w(g, 1)
         load_state(2)
+        for g in ("z", "r", "n"):
+            load_w(g, 1)
         nc.sync.dma_start(event_weight[1], wgo[:, HALF:J])
         load_state(3)
 
         def listed(c):
             return offsets[:, c * (HALF // 16) : (c + 1) * (HALF // 16)]
 
-        picked_words = [held("picked_words_%d" % c, [P, HALF], U32) for c in range(HALVES)]
-        picked_scales = [held("picked_scales_%d" % c, [P, HALF], U8) for c in range(HALVES)]
-        for c in range(HALVES):
-            nc.vector.tensor_copy(picked_words[c][:], table_words[:].bitcast(U32).indirect(listed(c)))
-        nc.vector.tensor_copy(picked_scales[0][:], table_scales[:].indirect(listed(0)))
+        all_words = held("picked_words", [P, J], U32)
+        all_scales = held("picked_scales", [P, J], U8)
+        nc.vector.tensor_copy(all_words[:], table_words[:].bitcast(U32).indirect(offsets[:]))
+        nc.vector.tensor_copy(all_scales[:], table_scales[:].indirect(offsets[:]))
+        picked_words = [all_words[:, c * HALF : (c + 1) * HALF] for c in range(HALVES)]
+        picked_scales = [all_scales[:, c * HALF : (c + 1) * HALF] for c in range(HALVES)]
 
         def copy_on(engine, out, in_):
             if engine == "scalar":
@@ -191,7 +197,7 @@ def tile_list_tgn_gruP_kernel(
 
         def quantise(name, grouped, width, on=None):
             codes = held(name + "_codes", [P, width], U32)
-            scales = (placed if name + "_scales" in PLACES else held)(name + "_scales", [P, width], U8)
+            scales = placed(name + "_scales", [P, width], U8) if name + "_scales" in PLACES else held(name + "_scales", [P, width], U8, on)
             nc.vector.quantize_mx(out=codes[:].bitcast(FP8X4), scales=scales[:], in_=grouped)
             return codes, scales
 
@@ -229,7 +235,6 @@ def tile_list_tgn_gruP_kernel(
         round_rows(w_grouped_n[:], w_raw["n", 0][:], "scalar")
         x_mx[0] = quantise("x_0", x_grouped_0[:], HALF)
         quantise_w("w_r", w_grouped_r[:], [("r", 0)])
-        nc.vector.tensor_copy(picked_scales[1][:], table_scales[:].indirect(listed(1)))
         quantise_w("w_n", w_grouped_n[:], [("n", 0)])
         pages.append(placed("page_2", [P, T], F32))
         nc.vector.memset(pages[2][:].bitcast(I32), 0)
@@ -249,7 +254,7 @@ def tile_list_tgn_gruP_kernel(
             nc.tensor.matmul_mx(
                 out=acc[:], lhsT=u_words[g][:, 2 * b * P : 2 * (b + 1) * P].bitcast(FP4X4),
                 lhsT_scale=u_scales[g][:, b * P : (b + 1) * P],
-                rhs=picked_words[c][:].bitcast(FP8X4), rhs_scale=picked_scales[c][:], start=start, stop=stop,
+                rhs=picked_words[c].bitcast(FP8X4), rhs_scale=picked_scales[c], start=start, stop=stop,
             )
 
         def ring(name, count, first):
@@ -266,14 +271,26 @@ def tile_list_tgn_gruP_kernel(
         for u in range(4):
             xn[u] = hn[u]
         sz = {u: update_bank for u in range(last + 1)}
-        sz[1] = reset_bank
+        sz[1], sz[3] = reset_bank, state_bank
+        for u in (5, 7):
+            sr[u], hn[u], xn[u] = across[0], across[1], back[1]
 
-        keep_gate = ring("keep_gate", 2, first=0)
+        def block_tile(name):
+            return held(name, [P, J], F32)
+
+        def half(tile, u):
+            return tile[:, (u % HALVES) * HALF : (u % HALVES + 1) * HALF]
+
+        block_keep = {1: block_tile("keep_odd"), 2: block_tile("keep_even")}
+        block_keep[3] = block_keep[1]
+        block_picked = {}
+        keep_gate = {u: unit_tile("keep_gate_of_%d" % u) for u in range(HALVES)}
+        for u in range(HALVES, last + 1):
+            keep_gate[u] = half(block_keep[u // HALVES], u)
         reset = ring("reset", 2, first=1)
         reset[0], reset[2] = placed_unit_tile("reset_of_0"), placed_unit_tile("reset_of_2")
         reset[3] = unit_tile("reset_of_3")
-        picked = ring("picked", 2, first=2)
-        picked[1] = placed_unit_tile("picked_of_1")
+        picked = {1: unit_tile("picked_of_1")}
         summed = {u: unit_tile("summed_of_%d" % u) for u in (0, 2)}
         gated = {0: summed[0], 2: placed_unit_tile("gated_of_2")}
         cand, moved, scaled, updated = {}, {}, {}, {}
@@ -400,7 +417,11 @@ def tile_list_tgn_gruP_kernel(
         round_x(x_grouped_1, 1, ("gpsimd", "scalar"))
         x_mx[1] = quantise("x_1", x_grouped_1[:], HALF)
         turn_bias("z", back[1], -1.0)
-        cand[0], cand[2] = placed_unit_tile("cand_of_0"), placed_unit_tile("cand_of_2")
+        cand[0] = placed_unit_tile("cand_of_0")
+        block_cand = {1: placed("cand_of_block_1", [P, J], F32), 2: block_tile("cand_of_block_2")}
+        block_cand[3] = block_tile("cand_of_block_3")
+        for u in range(HALVES, last + 1):
+            cand[u] = half(block_cand[u // HALVES], u)
         candidate_tanh(0)
         update_gate(0)
         moved[0] = placed_unit_tile("moved_of_0")
@@ -408,8 +429,9 @@ def tile_list_tgn_gruP_kernel(
         pick(1)
         scaled[0] = summed[0]
         scale_by_keep(nc.gpsimd, 0)
-        cand[1] = gated[1] = summed[1] = placed_unit_tile("cand_of_1")
-        gated[3] = summed[3] = placed_unit_tile("summed_of_3")
+        cand[1] = summed[1] = unit_tile("cand_of_1")
+        gated[1] = placed_unit_tile("gated_of_1")
+        gated[3], summed[3] = placed_unit_tile("gated_of_3"), cand[3]
         reset_gate(1)
         update_gate(1)
         reset_gate(3)
@@ -420,87 +442,85 @@ def tile_list_tgn_gruP_kernel(
             for u in (1, 3):
                 step(u)
         candidate_tanh(1)
+        candidate_tanh(3)
         update_gate(2)
-        pick(2)
+        update_gate(3)
 
+        def pick_block(b):
+            block_picked[b] = placed("picked_of_block_%d" % b, [P, J], F32)
+            nc.vector.tensor_copy(block_picked[b][:], state[b][:].indirect(offsets[:]))
+
+        pick_block(1)
         late_rn = placed("late_rn", [P, 2, SPAN * PACK], BF16)
         late_z = placed("late_z", [P, SPAN * PACK], BF16)
+        round_rows(late_z[:], w_raw["z", 1][:], "scalar")
         round_rows(late_rn[:, 0, :], w_raw["r", 1][:], "scalar")
         round_rows(late_rn[:, 1, :], w_raw["n", 1][:], "scalar")
-        cand[3] = unit_tile("cand_of_3", on="w_raw_n1")
-        candidate_tanh(3)
         for u in range(4, last + 1):
-            cand[u] = gated[u] = summed[u] = cand[u - 3]
-        round_rows(late_z[:], w_raw["z", 1][:], "scalar")
+            gated[u] = summed[u] = cand[u]
+        gated[5] = placed_unit_tile("gated_of_5")
 
-        first_spare = placed_unit_tile("first_spare")
-        updated_even = unit_tile("updated_even")
-        for u in range(1, last + 1):
-            scaled[u] = picked[u]
-        moved[1] = moved[2] = first_spare
+        spare = placed_unit_tile("spare")
+        moved[1], scaled[1] = spare, picked[1]
+        updated[0] = unit_tile("updated_of_0")
 
-        def add_into(out, u):
-            nc.gpsimd.tensor_tensor(out, scaled[u], cand[u], ALU.add)
-
-        def weigh_from(source, u):
-            nc.gpsimd.tensor_tensor(updated[u], source, event_weight[units[u][1]], ALU.mult)
-
-        updated[0] = updated_even
-        add_into(first_spare, 0)
-        weigh_from(first_spare, 0)
+        nc.gpsimd.tensor_tensor(spare, scaled[0], cand[0], ALU.add)
+        nc.gpsimd.tensor_tensor(updated[0], spare, event_weight[0], ALU.mult)
         subtract(1)
         scale_by_keep(nc.gpsimd, 1)
-        keep_gate[3] = unit_tile("keep_gate_of_3", on="w_raw_z1")
-        update_gate(3)
-        nc.vector.tensor_copy(window(0), updated_even)
+        nc.vector.tensor_copy(window(0), updated[0])
+        wide_spare = placed("wide_spare", [P, J], F32)
+        nc.gpsimd.tensor_tensor(wide_spare[:], block_picked[1][:], block_cand[1][:], ALU.subtract)
+        quantise_w("late_z", late_z[:], [("z", 1)], on="w_raw_n1")
         quantise_w("late_rn", late_rn[:].rearrange("p g c -> p (g c)"), [("r", 1), ("n", 1)])
-        quantise_w("late_z", late_z[:], [("z", 1)])
-        picked[3] = scaled[3] = picked[6] = scaled[6] = placed_unit_tile("picked_of_3")
-        picked[4] = scaled[4] = picked[7] = scaled[7] = picked[1 + HALVES * 2 + 2]
-        picked[5] = scaled[5] = picked[2]
-        pick(3)
-        updated_odd = placed_unit_tile("updated_odd")
-        for u in range(last + 1):
-            updated[u] = updated_odd if u % 2 else updated_even
-        products(4)
+        unweighed, updated[1] = placed_unit_tile("unweighed_of_1"), placed_unit_tile("updated_of_1")
+        nc.gpsimd.tensor_tensor(unweighed, scaled[1], cand[1], ALU.add)
+        nc.gpsimd.tensor_tensor(updated[1], unweighed, event_weight[1], ALU.mult)
 
-        for u in range(1, last + 1):
-            if u == 2:
-                spare = placed_unit_tile("spare")
-                for later in range(3, last + 1):
-                    moved[later] = spare
-            unweighed = updated[u]
-            if u == 1:
-                unweighed = scaled[u]
-            if u == 2:
-                unweighed = placed_unit_tile("unweighed_of_2")
-            if u == last - 1:
-                add_into(spare, u)
-                weigh_from(spare, u)
-                subtract(u + 1)
-                scale_by_keep(nc.gpsimd, u + 1)
-            elif u < last:
-                subtract(u + 1)
-                add_into(unweighed, u)
-                scale_by_keep(nc.gpsimd, u + 1)
-                weigh_from(unweighed, u)
+        def prepare(b):
+            pair = (HALVES * b, HALVES * b + 1)
+            for u in pair:
+                products(u)
+            pick_block(b)
+            for u in pair:
+                reset_state(u)
+            for u in pair:
+                candidate_sum(u)
+                candidate_tanh(u)
+            for u in pair:
+                update_gate(u)
+
+        prepare(2)
+        nc.vector.tensor_copy(window(1), updated[1])
+        store_if_finished(1)
+        for b in range(1, BLOCKS - 1):
+            if b == 1:
+                values = placed("scaled_of_block_1", [P, J], F32)
             else:
-                add_into(unweighed, u)
-            if u + 3 <= last:
-                update_gate(u + 3)
-                reset_state(u + 3)
-                pick(u + 3)
-                candidate_sum(u + 3)
-                candidate_tanh(u + 3)
-            if u + 4 <= last:
-                products(u + 4)
-            if u == PAGES * HALVES:
-                regroup(0, across)
+                values = block_picked[b]
+                nc.gpsimd.tensor_tensor(wide_spare[:], values[:], block_cand[b][:], ALU.subtract)
+            nc.gpsimd.tensor_tensor(values[:], wide_spare[:], block_keep[b][:], ALU.mult)
+            nc.gpsimd.tensor_tensor(wide_spare[:], values[:], block_cand[b][:], ALU.add)
+            nc.gpsimd.tensor_tensor(values[:], wide_spare[:], both_weights[:], ALU.mult)
+            if b + 2 < BLOCKS:
+                prepare(b + 2)
+            nc.vector.tensor_copy(pages[b][:].indirect(offsets[:]), values[:])
+            store_if_finished(HALVES * b + 1)
+        regroup(0, across)
+        spare = half(wide_spare, last)
+        for u in (last - 1, last):
+            picked[u] = scaled[u] = half(block_picked[BLOCKS - 1], u)
+            moved[u] = spare
+            subtract(u)
+            scale_by_keep(nc.gpsimd, u)
+            nc.gpsimd.tensor_tensor(spare, scaled[u], cand[u], ALU.add)
             if u < last:
-                nc.vector.tensor_copy(window(u), updated[u])
+                nc.gpsimd.tensor_tensor(picked[u], spare, event_weight[0], ALU.mult)
+                nc.vector.tensor_copy(window(u), picked[u])
             else:
+                updated[u] = spare
                 weigh(nc.vector, window(u), u)
-            store_if_finished(u)
+        store_if_finished(last)
 
         final = BLOCKS - 1
         sum_banks = (reset_bank, update_bank, state_bank, message_bank)
@@ -510,7 +530,7 @@ def tile_list_tgn_gruP_kernel(
             turn_out(final, s, sum_banks[s], engine)
         turn_out(final, SLICES - 1, message_bank, "scalar", range(0, 2))
         turn_out(final, SLICES - 1, across[1], "vector", range(2, 4))
-        y_codes = held("y_codes", [P, BLOCKS, QUARTER], U32, on="picked_1")
+        y_codes = placed("y_codes", [P, BLOCKS, QUARTER], U32)
 
         def quantise_y(blocks, slices):
             cols = slice(slices.start * P, slices.stop * P)

@@ -28,6 +28,7 @@ QUARTERS = P // QUADRANT
 QUARTER = T // QUARTERS
 SLICES = QUARTER // P
 PAGES = 3
+WARM_PASSES = 4
 STEP = 1024
 
 PLACES = {
@@ -36,16 +37,16 @@ PLACES = {
     "cand_of_block_1": 2,
     "late_rn": 9,
     "late_z": 13,
-    "picked_of_block_2": 6,
-    "unweighed_of_1": 12,
-    "updated_of_1": 14,
-    "scaled_of_block_1": 10,
-    "moved_of_0": 42,
+    "unweighed_of_1": 13,
+    "picked_of_block_2": 10,
+    "scaled_of_block_1": 14,
+    "state_0": 41,
     "gated_of_3": 41,
     "gated_of_1": 43,
     "picked_of_block_1": 44,
-    "gated_of_5": 48,
-    "picked_of_block_3": 48,
+    "gated_of_5": 49,
+    "picked_of_block_3": 49,
+    "y_grouped_of_block_2": 49,
     "w_raw_n0": 18,
     "reset_of_0": 18,
     "reset_of_2": 20,
@@ -101,7 +102,7 @@ def tile_list_tgn_gruP_kernel(
         bias_dram = {"r": br, "n": bn, "z": bz}
         bias_rows = {g: held("bias_rows_" + g, [P, P], F32) for g in gates}
         x_raw = [placed("x_raw_0", [P, PACK, HALF], F32), placed("x_raw_1", [P, PACK, HALF], F32)]
-        state = [held("state_%d" % b, [P, T], F32) for b in range(BLOCKS)]
+        state = [(held if b else placed)("state_%d" % b, [P, T], F32) for b in range(BLOCKS)]
         both_weights = held("event_weight", [P, J], F32)
         event_weight = [both_weights[:, c * HALF : (c + 1) * HALF] for c in range(HALVES)]
         pages = [held("page_%d" % i, [P, T], F32) for i in range(PAGES - 1)]
@@ -160,11 +161,10 @@ def tile_list_tgn_gruP_kernel(
         load_scale_rows(u_scales["z"], uz_scales)
         load_state(0)
         load_state(1)
-        nc.sync.dma_start(event_weight[0], wgo[:, 0:HALF])
+        nc.sync.dma_start(both_weights[:], wgo)
         load_state(2)
         for g in ("z", "r", "n"):
             load_w(g, 1)
-        nc.sync.dma_start(event_weight[1], wgo[:, HALF:J])
         load_state(3)
 
         def listed(c):
@@ -350,7 +350,9 @@ def tile_list_tgn_gruP_kernel(
                 nc.sync.dma_start(out_0[b * P : (b + 1) * P, :], pages[b % PAGES][:])
 
         y_pairs = [held("y_pairs_%d" % s, [P, HALF], BF16) for s in range(SLICES)]
-        y_grouped = held("y_grouped", [P, BLOCKS, QUARTER * PACK], BF16)
+        first_grouped = held("y_grouped_of_blocks_0_1", [P, 2, QUARTER * PACK], BF16)
+        y_grouped = {b: first_grouped[:, b, :] for b in range(2)}
+        y_grouped[BLOCKS - 1] = held("y_grouped_of_block_3", [P, QUARTER * PACK], BF16)[:]
 
         def turn_out(b, s, target, engine, quarters=range(QUARTERS)):
             for i, a in enumerate(quarters):
@@ -371,7 +373,7 @@ def tile_list_tgn_gruP_kernel(
                 )
 
         def weave(b, first, count, source, engine):
-            words = y_grouped[:, b, :].bitcast(F32)[:, first * 2 * P : (first + count) * 2 * P]
+            words = y_grouped[b].bitcast(F32)[:, first * 2 * P : (first + count) * 2 * P]
             copy_on(
                 engine,
                 words.rearrange("r (s t h) -> r s t h", s=count, h=2),
@@ -424,7 +426,7 @@ def tile_list_tgn_gruP_kernel(
             cand[u] = half(block_cand[u // HALVES], u)
         candidate_tanh(0)
         update_gate(0)
-        moved[0] = placed_unit_tile("moved_of_0")
+        moved[0] = unit_tile("moved_of_0")
         difference(0)
         pick(1)
         scaled[0] = summed[0]
@@ -473,9 +475,9 @@ def tile_list_tgn_gruP_kernel(
         nc.gpsimd.tensor_tensor(wide_spare[:], block_picked[1][:], block_cand[1][:], ALU.subtract)
         quantise_w("late_z", late_z[:], [("z", 1)], on="w_raw_n1")
         quantise_w("late_rn", late_rn[:].rearrange("p g c -> p (g c)"), [("r", 1), ("n", 1)])
-        unweighed, updated[1] = placed_unit_tile("unweighed_of_1"), placed_unit_tile("updated_of_1")
-        nc.gpsimd.tensor_tensor(unweighed, scaled[1], cand[1], ALU.add)
-        nc.gpsimd.tensor_tensor(updated[1], unweighed, event_weight[1], ALU.mult)
+        unweighed, updated[1] = placed_unit_tile("unweighed_of_1"), unit_tile("updated_of_1")
+        nc.vector.tensor_tensor(unweighed, scaled[1], cand[1], ALU.add)
+        nc.vector.tensor_tensor(updated[1], unweighed, event_weight[1], ALU.mult)
 
         def prepare(b):
             pair = (HALVES * b, HALVES * b + 1)
@@ -501,10 +503,14 @@ def tile_list_tgn_gruP_kernel(
                 nc.gpsimd.tensor_tensor(wide_spare[:], values[:], block_cand[b][:], ALU.subtract)
             nc.gpsimd.tensor_tensor(values[:], wide_spare[:], block_keep[b][:], ALU.mult)
             nc.gpsimd.tensor_tensor(wide_spare[:], values[:], block_cand[b][:], ALU.add)
-            nc.gpsimd.tensor_tensor(values[:], wide_spare[:], both_weights[:], ALU.mult)
             if b + 2 < BLOCKS:
+                nc.gpsimd.tensor_tensor(values[:], wide_spare[:], both_weights[:], ALU.mult)
                 prepare(b + 2)
-            nc.vector.tensor_copy(pages[b][:].indirect(offsets[:]), values[:])
+                nc.vector.tensor_copy(pages[b][:].indirect(offsets[:]), values[:])
+            else:
+                for u in (HALVES * b, HALVES * b + 1):
+                    nc.gpsimd.tensor_tensor(half(values, u), half(wide_spare, u), event_weight[u % HALVES], ALU.mult)
+                    nc.vector.tensor_copy(window(u), half(values, u))
             store_if_finished(HALVES * b + 1)
         regroup(0, across)
         spare = half(wide_spare, last)
@@ -525,19 +531,24 @@ def tile_list_tgn_gruP_kernel(
         final = BLOCKS - 1
         sum_banks = (reset_bank, update_bank, state_bank, message_bank)
         regroup(1, across)
-        regroup(2, sum_banks)
-        for s, engine in enumerate(("scalar", "vector", "scalar")):
+        for s, target in enumerate((across[0], across[1], back[0], back[1])):
+            turn_out(2, s, target, "scalar")
+        y_grouped[2] = placed("y_grouped_of_block_2", [P, QUARTER * PACK], BF16)[:]
+        for s in range(SLICES):
+            turn_back(s, sum_banks[s], 0)
+            weave(2, s, 1, sum_banks[s], "scalar")
+        for i in range(WARM_PASSES):
+            message_pass(sum_banks[0], "z", last, i == 0, i == WARM_PASSES - 1)
+        for s, engine in enumerate(("scalar", "scalar", "scalar", "vector")):
             turn_out(final, s, sum_banks[s], engine)
-        turn_out(final, SLICES - 1, message_bank, "scalar", range(0, 2))
-        turn_out(final, SLICES - 1, across[1], "vector", range(2, 4))
         y_codes = placed("y_codes", [P, BLOCKS, QUARTER], U32)
 
-        def quantise_y(blocks, slices):
+        def quantise_y(blocks, slices, grouped):
             cols = slice(slices.start * P, slices.stop * P)
             nc.vector.quantize_mx(
                 out=y_codes[:, blocks, cols].rearrange("r b c -> r (b c)").bitcast(FP8X4),
                 scales=y_scales[:, blocks, cols].rearrange("r b c -> r (b c)"),
-                in_=y_grouped[:, blocks, PACK * cols.start : PACK * cols.stop].rearrange("r b c -> r (b c)"),
+                in_=grouped[:, PACK * cols.start : PACK * (cols.stop + (blocks.stop - blocks.start - 1) * QUARTER)],
             )
 
         word_rows = out_1[0].rearrange("p c i -> p (c i)").bitcast(I32).rearrange("(b r) t -> r b t", r=QUADRANT)
@@ -548,17 +559,14 @@ def tile_list_tgn_gruP_kernel(
                 target = word_rows[:, blocks, a * QUARTER : (a + 1) * QUARTER]
                 queues[a % len(queues)].dma_start(target, source.bitcast(I32))
 
-        quantise_y(slice(0, 2), slice(0, SLICES))
+        quantise_y(slice(0, 2), slice(0, SLICES), first_grouped[:].rearrange("r b c -> r (b c)"))
         store_words(slice(0, 2), [nc.sync])
-        quantise_y(slice(2, final), slice(0, SLICES))
-        for s, target, engine in ((0, back[0], "scalar"), (1, back[1], "vector")):
-            turn_back(s, target, 0)
-            weave(final, s, 1, target, engine)
-        quantise_y(slice(final, BLOCKS), slice(0, 2))
-        for s, target, engine in ((2, across[0], "vector"), (3, reset_bank, "scalar")):
-            turn_back(s, target, 0)
-            weave(final, s, 1, target, engine)
-            quantise_y(slice(final, BLOCKS), slice(s, s + 1))
+        quantise_y(slice(2, final), slice(0, SLICES), y_grouped[2])
+        for pair, targets in enumerate((back, across)):
+            for i, engine in enumerate(("scalar", "vector")):
+                turn_back(2 * pair + i, targets[i], 0)
+                weave(final, 2 * pair + i, 1, targets[i], engine)
+            quantise_y(slice(final, BLOCKS), slice(2 * pair, 2 * pair + 2), y_grouped[final])
         store_words(slice(2, BLOCKS), [nc.sync])
         scale_rows = out_2[0].rearrange("(b j) t -> j b t", j=4)
         for a in range(QUARTERS):

@@ -28,7 +28,6 @@ QUARTERS = P // QUADRANT
 QUARTER = T // QUARTERS
 SLICES = QUARTER // P
 PAGES = 3
-WARM_PASSES = 4
 STEP = 1024
 
 PLACES = {
@@ -67,18 +66,18 @@ def tile_list_tgn_gruP_kernel(
 ):
     nc = tc.nc
     with ExitStack() as ctx:
-        keep = ctx.enter_context(tc.tile_pool(name="keep", bufs=1))
+        own = ctx.enter_context(tc.tile_pool(name="keep", bufs=1))
         shared = ctx.enter_context(tc.tile_pool(name="shared", bufs=1))
         psum = ctx.enter_context(tc.psum_pool(name="psum", bufs=1))
 
         def held(name, shape, dtype, on=None):
-            return keep.tile(shape, dtype, name=name, tag=on or name, align_bytes=64)
+            return own.tile(shape, dtype, name=name, tag=on or name, align_bytes=64)
 
         def placed(name, shape, dtype):
             return shared.tile(shape, dtype, name=name, align_bytes=64, offset=PLACES[name] * STEP)
 
-        def unit_tile(name, on=None):
-            return held(name, [P, HALF], F32, on)[:]
+        def unit_tile(name):
+            return held(name, [P, HALF], F32)[:]
 
         def placed_unit_tile(name):
             return placed(name, [P, HALF], F32)[:]
@@ -90,7 +89,7 @@ def tile_list_tgn_gruP_kernel(
         w_dram = {"r": wr, "n": wn, "z": wz}
         u_words_dram = {"r": ur_words, "n": un_words, "z": uz_words}
 
-        offsets = keep.tile([P, J // 16], U16, name="offsets")
+        offsets = own.tile([P, J // 16], U16, name="offsets")
         table_words = held("table_words", [P, T], I32)
         table_scales = held("table_scales", [P, T], U8)
         w_raw = {(g, 1): held("w_raw_%s1" % g, [P, PACK, SPAN], F32) for g in gates}
@@ -102,7 +101,7 @@ def tile_list_tgn_gruP_kernel(
         bias_dram = {"r": br, "n": bn, "z": bz}
         bias_rows = {g: held("bias_rows_" + g, [P, P], F32) for g in gates}
         x_raw = [placed("x_raw_0", [P, PACK, HALF], F32), placed("x_raw_1", [P, PACK, HALF], F32)]
-        state = [(held if b else placed)("state_%d" % b, [P, T], F32) for b in range(BLOCKS)]
+        state = [placed("state_0", [P, T], F32)] + [held("state_%d" % b, [P, T], F32) for b in range(1, BLOCKS)]
         both_weights = held("event_weight", [P, J], F32)
         event_weight = [both_weights[:, c * HALF : (c + 1) * HALF] for c in range(HALVES)]
         pages = [held("page_%d" % i, [P, T], F32) for i in range(PAGES - 1)]
@@ -197,7 +196,10 @@ def tile_list_tgn_gruP_kernel(
 
         def quantise(name, grouped, width, on=None):
             codes = held(name + "_codes", [P, width], U32)
-            scales = placed(name + "_scales", [P, width], U8) if name + "_scales" in PLACES else held(name + "_scales", [P, width], U8, on)
+            if name + "_scales" in PLACES:
+                scales = placed(name + "_scales", [P, width], U8)
+            else:
+                scales = held(name + "_scales", [P, width], U8, on)
             nc.vector.quantize_mx(out=codes[:].bitcast(FP8X4), scales=scales[:], in_=grouped)
             return codes, scales
 
@@ -257,10 +259,6 @@ def tile_list_tgn_gruP_kernel(
                 rhs=picked_words[c].bitcast(FP8X4), rhs_scale=picked_scales[c], start=start, stop=stop,
             )
 
-        def ring(name, count, first):
-            tiles = [unit_tile("%s_%d" % (name, i)) for i in range(count)]
-            return {u: tiles[u % count] for u in range(first, last + 1)}
-
         reset_bank, update_bank = bank("reset_bank"), bank("update_bank")
         state_bank, message_bank = bank("state_bank"), bank("message_bank")
         sr = {u: reset_bank for u in range(last + 1)}
@@ -272,7 +270,7 @@ def tile_list_tgn_gruP_kernel(
             xn[u] = hn[u]
         sz = {u: update_bank for u in range(last + 1)}
         sz[1], sz[3] = reset_bank, state_bank
-        for u in (5, 7):
+        for u in range(5, last + 1, HALVES):
             sr[u], hn[u], xn[u] = across[0], across[1], back[1]
 
         def block_tile(name):
@@ -287,7 +285,8 @@ def tile_list_tgn_gruP_kernel(
         keep_gate = {u: unit_tile("keep_gate_of_%d" % u) for u in range(HALVES)}
         for u in range(HALVES, last + 1):
             keep_gate[u] = half(block_keep[u // HALVES], u)
-        reset = ring("reset", 2, first=1)
+        reset_tiles = [unit_tile("reset_%d" % c) for c in range(HALVES)]
+        reset = {u: reset_tiles[u % HALVES] for u in range(last + 1)}
         reset[0], reset[2] = placed_unit_tile("reset_of_0"), placed_unit_tile("reset_of_2")
         reset[3] = unit_tile("reset_of_3")
         picked = {1: unit_tile("picked_of_1")}
@@ -312,9 +311,9 @@ def tile_list_tgn_gruP_kernel(
 
         def update_gate(u):
             b = units[u][0]
-            first, second = (state_pass, message_pass) if u < 2 else (message_pass, state_pass)
-            first(sz[u], "z", u, True, False)
-            second(sz[u], "z", u, False, True)
+            opening, closing = (state_pass, message_pass) if b == 0 else (message_pass, state_pass)
+            opening(sz[u], "z", u, True, False)
+            closing(sz[u], "z", u, False, True)
             nc.scalar.activation(keep_gate[u], sz[u][:], ACT.Sigmoid, bias=bias["z"][:, b : b + 1], scale=-1.0)
 
         def reset_state(u):
@@ -334,35 +333,32 @@ def tile_list_tgn_gruP_kernel(
         def scale_by_keep(engine, u):
             engine.tensor_tensor(scaled[u], moved[u], keep_gate[u], ALU.mult)
 
-        def add_candidate(engine, u):
-            engine.tensor_tensor(updated[u], scaled[u], cand[u], ALU.add)
+        def add_candidate(engine, out, u):
+            engine.tensor_tensor(out, scaled[u], cand[u], ALU.add)
 
-        def weigh(engine, out, u):
-            engine.tensor_tensor(out, updated[u], event_weight[units[u][1]], ALU.mult)
+        def weigh(engine, out, unweighed, u):
+            engine.tensor_tensor(out, unweighed, event_weight[units[u][1]], ALU.mult)
 
         def window(u):
             b, c = units[u]
             return pages[b % PAGES][:].indirect(listed(c))
 
-        def store_if_finished(u):
-            b, c = units[u]
-            if c == HALVES - 1:
-                nc.sync.dma_start(out_0[b * P : (b + 1) * P, :], pages[b % PAGES][:])
+        def store_block(b):
+            nc.sync.dma_start(out_0[b * P : (b + 1) * P, :], pages[b % PAGES][:])
 
         y_pairs = [held("y_pairs_%d" % s, [P, HALF], BF16) for s in range(SLICES)]
         first_grouped = held("y_grouped_of_blocks_0_1", [P, 2, QUARTER * PACK], BF16)
         y_grouped = {b: first_grouped[:, b, :] for b in range(2)}
         y_grouped[BLOCKS - 1] = held("y_grouped_of_block_3", [P, QUARTER * PACK], BF16)[:]
 
-        def turn_out(b, s, target, engine, quarters=range(QUARTERS)):
-            for i, a in enumerate(quarters):
+        def turn_out(b, s, target, engine):
+            for a in range(QUARTERS):
                 first = a * QUARTER + s * P
-                nc.tensor.transpose(target[:, i * P : (i + 1) * P], pages[b % PAGES][:, first : first + P], identity[:])
-            words = slice(QUADRANT * quarters[0], QUADRANT * (quarters[-1] + 1))
+                nc.tensor.transpose(target[:, a * P : (a + 1) * P], pages[b % PAGES][:, first : first + P], identity[:])
             copy_on(
                 engine,
-                y_pairs[s][:].rearrange("t (h r e) -> t h r e", h=2, e=2)[:, :, words, :],
-                target[:, 0 : len(quarters) * P].rearrange("t (r h e) -> t h r e", h=2, e=2),
+                y_pairs[s][:].rearrange("t (h r e) -> t h r e", h=2, e=2),
+                target[:].rearrange("t (r h e) -> t h r e", h=2, e=2),
             )
 
         def turn_back(s, target, first):
@@ -380,9 +376,9 @@ def tile_list_tgn_gruP_kernel(
                 source[:, 0 : count * 2 * P].rearrange("r (s h t) -> r s t h", s=count, h=2),
             )
 
-        def regroup(b, targets):
+        def regroup(b):
             for s in range(SLICES):
-                turn_out(b, s, targets[s % len(targets)], "scalar")
+                turn_out(b, s, across[s % 2], "scalar")
             for pair in range(SLICES // 2):
                 turn_back(2 * pair, back[pair], 0)
                 turn_back(2 * pair + 1, back[pair], 2 * P)
@@ -396,11 +392,6 @@ def tile_list_tgn_gruP_kernel(
 
         def subtract(u):
             nc.gpsimd.tensor_tensor(moved[u], picked[u], cand[u], ALU.subtract)
-
-        def products(u):
-            reset_gate(u)
-            state_product(u)
-            message_product(u)
 
         for u in (0, 2):
             state_pass(sr[u], "r", u, True, False)
@@ -465,24 +456,26 @@ def tile_list_tgn_gruP_kernel(
         spare = placed_unit_tile("spare")
         moved[1], scaled[1] = spare, picked[1]
         updated[0] = unit_tile("updated_of_0")
-
-        nc.gpsimd.tensor_tensor(spare, scaled[0], cand[0], ALU.add)
-        nc.gpsimd.tensor_tensor(updated[0], spare, event_weight[0], ALU.mult)
+        add_candidate(nc.gpsimd, spare, 0)
+        weigh(nc.gpsimd, updated[0], spare, 0)
         subtract(1)
         scale_by_keep(nc.gpsimd, 1)
         nc.vector.tensor_copy(window(0), updated[0])
         wide_spare = placed("wide_spare", [P, J], F32)
         nc.gpsimd.tensor_tensor(wide_spare[:], block_picked[1][:], block_cand[1][:], ALU.subtract)
+
         quantise_w("late_z", late_z[:], [("z", 1)], on="w_raw_n1")
         quantise_w("late_rn", late_rn[:].rearrange("p g c -> p (g c)"), [("r", 1), ("n", 1)])
         unweighed, updated[1] = placed_unit_tile("unweighed_of_1"), unit_tile("updated_of_1")
-        nc.vector.tensor_tensor(unweighed, scaled[1], cand[1], ALU.add)
-        nc.vector.tensor_tensor(updated[1], unweighed, event_weight[1], ALU.mult)
+        add_candidate(nc.vector, unweighed, 1)
+        weigh(nc.vector, updated[1], unweighed, 1)
 
         def prepare(b):
             pair = (HALVES * b, HALVES * b + 1)
             for u in pair:
-                products(u)
+                reset_gate(u)
+                state_product(u)
+                message_product(u)
             pick_block(b)
             for u in pair:
                 reset_state(u)
@@ -492,82 +485,81 @@ def tile_list_tgn_gruP_kernel(
             for u in pair:
                 update_gate(u)
 
-        prepare(2)
-        nc.vector.tensor_copy(window(1), updated[1])
-        store_if_finished(1)
-        for b in range(1, BLOCKS - 1):
-            if b == 1:
-                values = placed("scaled_of_block_1", [P, J], F32)
-            else:
-                values = block_picked[b]
-                nc.gpsimd.tensor_tensor(wide_spare[:], values[:], block_cand[b][:], ALU.subtract)
+        def scale_and_add(b, values):
             nc.gpsimd.tensor_tensor(values[:], wide_spare[:], block_keep[b][:], ALU.mult)
             nc.gpsimd.tensor_tensor(wide_spare[:], values[:], block_cand[b][:], ALU.add)
-            if b + 2 < BLOCKS:
-                nc.gpsimd.tensor_tensor(values[:], wide_spare[:], both_weights[:], ALU.mult)
-                prepare(b + 2)
-                nc.vector.tensor_copy(pages[b][:].indirect(offsets[:]), values[:])
-            else:
-                for u in (HALVES * b, HALVES * b + 1):
-                    nc.gpsimd.tensor_tensor(half(values, u), half(wide_spare, u), event_weight[u % HALVES], ALU.mult)
-                    nc.vector.tensor_copy(window(u), half(values, u))
-            store_if_finished(HALVES * b + 1)
-        regroup(0, across)
-        spare = half(wide_spare, last)
+
+        prepare(2)
+        nc.vector.tensor_copy(window(1), updated[1])
+        store_block(0)
+
+        values = placed("scaled_of_block_1", [P, J], F32)
+        scale_and_add(1, values)
+        nc.gpsimd.tensor_tensor(values[:], wide_spare[:], both_weights[:], ALU.mult)
+        prepare(3)
+        nc.vector.tensor_copy(pages[1][:].indirect(offsets[:]), values[:])
+        store_block(1)
+
+        values = block_picked[2]
+        nc.gpsimd.tensor_tensor(wide_spare[:], values[:], block_cand[2][:], ALU.subtract)
+        scale_and_add(2, values)
+        for u in (4, 5):
+            weigh(nc.gpsimd, half(values, u), half(wide_spare, u), u)
+            nc.vector.tensor_copy(window(u), half(values, u))
+        store_block(2)
+
+        regroup(0)
+        final = BLOCKS - 1
+        last_spare = half(wide_spare, last)
         for u in (last - 1, last):
-            picked[u] = scaled[u] = half(block_picked[BLOCKS - 1], u)
-            moved[u] = spare
+            picked[u] = scaled[u] = half(block_picked[final], u)
+            moved[u] = last_spare
             subtract(u)
             scale_by_keep(nc.gpsimd, u)
-            nc.gpsimd.tensor_tensor(spare, scaled[u], cand[u], ALU.add)
+            add_candidate(nc.gpsimd, last_spare, u)
             if u < last:
-                nc.gpsimd.tensor_tensor(picked[u], spare, event_weight[0], ALU.mult)
+                weigh(nc.gpsimd, picked[u], last_spare, u)
                 nc.vector.tensor_copy(window(u), picked[u])
             else:
-                updated[u] = spare
-                weigh(nc.vector, window(u), u)
-        store_if_finished(last)
+                weigh(nc.vector, window(u), last_spare, u)
+        store_block(final)
 
-        final = BLOCKS - 1
         sum_banks = (reset_bank, update_bank, state_bank, message_bank)
-        regroup(1, across)
+        regroup(1)
         for s, target in enumerate((across[0], across[1], back[0], back[1])):
             turn_out(2, s, target, "scalar")
         y_grouped[2] = placed("y_grouped_of_block_2", [P, QUARTER * PACK], BF16)[:]
         for s in range(SLICES):
             turn_back(s, sum_banks[s], 0)
             weave(2, s, 1, sum_banks[s], "scalar")
-        for i in range(WARM_PASSES):
-            message_pass(sum_banks[0], "z", last, i == 0, i == WARM_PASSES - 1)
         for s, engine in enumerate(("scalar", "scalar", "scalar", "vector")):
             turn_out(final, s, sum_banks[s], engine)
         y_codes = placed("y_codes", [P, BLOCKS, QUARTER], U32)
 
-        def quantise_y(blocks, slices, grouped):
-            cols = slice(slices.start * P, slices.stop * P)
+        def quantise_y(blocks, cols, grouped):
             nc.vector.quantize_mx(
                 out=y_codes[:, blocks, cols].rearrange("r b c -> r (b c)").bitcast(FP8X4),
                 scales=y_scales[:, blocks, cols].rearrange("r b c -> r (b c)"),
-                in_=grouped[:, PACK * cols.start : PACK * (cols.stop + (blocks.stop - blocks.start - 1) * QUARTER)],
+                in_=grouped,
             )
 
         word_rows = out_1[0].rearrange("p c i -> p (c i)").bitcast(I32).rearrange("(b r) t -> r b t", r=QUADRANT)
 
-        def store_words(blocks, queues):
+        def store_words(blocks):
             for a in range(QUARTERS):
                 source = y_codes[QUADRANT * a : QUADRANT * (a + 1), blocks, :]
-                target = word_rows[:, blocks, a * QUARTER : (a + 1) * QUARTER]
-                queues[a % len(queues)].dma_start(target, source.bitcast(I32))
+                nc.sync.dma_start(word_rows[:, blocks, a * QUARTER : (a + 1) * QUARTER], source.bitcast(I32))
 
-        quantise_y(slice(0, 2), slice(0, SLICES), first_grouped[:].rearrange("r b c -> r (b c)"))
-        store_words(slice(0, 2), [nc.sync])
-        quantise_y(slice(2, final), slice(0, SLICES), y_grouped[2])
+        quantise_y(slice(0, 2), slice(0, QUARTER), first_grouped[:].rearrange("r b c -> r (b c)"))
+        store_words(slice(0, 2))
+        quantise_y(slice(2, final), slice(0, QUARTER), y_grouped[2])
         for pair, targets in enumerate((back, across)):
             for i, engine in enumerate(("scalar", "vector")):
                 turn_back(2 * pair + i, targets[i], 0)
                 weave(final, 2 * pair + i, 1, targets[i], engine)
-            quantise_y(slice(final, BLOCKS), slice(2 * pair, 2 * pair + 2), y_grouped[final])
-        store_words(slice(2, BLOCKS), [nc.sync])
+            cols = slice(2 * pair * P, 2 * (pair + 1) * P)
+            quantise_y(slice(final, BLOCKS), cols, y_grouped[final][:, PACK * cols.start : PACK * cols.stop])
+        store_words(slice(2, BLOCKS))
         scale_rows = out_2[0].rearrange("(b j) t -> j b t", j=4)
         for a in range(QUARTERS):
             source = y_scales[QUADRANT * a : QUADRANT * a + 4]

@@ -28,36 +28,11 @@ QUARTERS = P // QUADRANT
 QUARTER = T // QUARTERS
 SLICES = QUARTER // P
 PAGES = 3
-STEP = 1024
-
-PLACES = {
-    "x_raw_1": 0,
-    "cand_of_0": 0,
-    "cand_of_block_1": 2,
-    "late_rn": 9,
-    "late_z": 13,
-    "unweighed_of_1": 13,
-    "picked_of_block_2": 10,
-    "scaled_of_block_1": 14,
-    "state_0": 41,
-    "gated_of_3": 41,
-    "gated_of_1": 43,
-    "picked_of_block_1": 44,
-    "gated_of_5": 49,
-    "picked_of_block_3": 49,
-    "y_grouped_of_block_2": 49,
-    "w_raw_n0": 18,
-    "reset_of_0": 18,
-    "reset_of_2": 20,
-    "x_raw_0": 22,
-    "w_grouped_r": 30,
-    "page_2": 23,
-    "gated_of_2": 32,
-    "w_z_scales": 32,
-    "spare": 34,
-    "wide_spare": 34,
-    "y_codes": 37,
-}
+UNITS = [(0, 0), (1, 0), (0, 1), (1, 1), (2, 0), (2, 1), (3, 0), (3, 1)]
+LAST = len(UNITS) - 1
+ON_TENSOR = (2, 3, 4, 5)
+SUM_ON_GPSIMD = (4, 5, 6)
+X_SHARES = (("scalar", 224), ("vector", 288))
 
 
 def tile_list_tgn_gruP_kernel(
@@ -73,14 +48,8 @@ def tile_list_tgn_gruP_kernel(
         def held(name, shape, dtype, on=None):
             return own.tile(shape, dtype, name=name, tag=on or name, align_bytes=64)
 
-        def placed(name, shape, dtype):
-            return shared.tile(shape, dtype, name=name, align_bytes=64, offset=PLACES[name] * STEP)
-
-        def unit_tile(name):
-            return held(name, [P, HALF], F32)[:]
-
-        def placed_unit_tile(name):
-            return placed(name, [P, HALF], F32)[:]
+        def unit_tile(name, on=None):
+            return held(name, [P, HALF], F32, on)[:]
 
         def bank(name):
             return psum.tile([P, HALF], F32, name=name)
@@ -88,43 +57,42 @@ def tile_list_tgn_gruP_kernel(
         gates = ("r", "n", "z")
         w_dram = {"r": wr, "n": wn, "z": wz}
         u_words_dram = {"r": ur_words, "n": un_words, "z": uz_words}
+        u_scales_dram = {"r": ur_scales, "n": un_scales, "z": uz_scales}
+        bias_dram = {"r": br, "n": bn, "z": bz}
 
         offsets = own.tile([P, J // 16], U16, name="offsets")
         table_words = held("table_words", [P, T], I32)
         table_scales = held("table_scales", [P, T], U8)
-        w_raw = {(g, 1): held("w_raw_%s1" % g, [P, PACK, SPAN], F32) for g in gates}
-        w_raw["r", 0] = held("w_raw_r0", [P, PACK, SPAN], F32)
-        w_raw["n", 0] = placed("w_raw_n0", [P, PACK, SPAN], F32)
-        w_raw["z", 0] = held("w_raw_z0", [P, PACK, SPAN], F32)
+        w_raw = {(g, s): held("w_raw_%s%d" % (g, s), [P, PACK, SPAN], F32) for g in gates for s in range(2) if (g, s) != ("z", 1)}
+        w_raw["z", 1] = shared.tile([P, PACK, SPAN], F32, name="w_raw_z1", align_bytes=64, offset=0)
         u_words = {g: held("u_words_" + g, [P, 2 * N], U8) for g in gates}
-        u_scales = {g: held("u_scales_" + g, [P, N], U8) for g in gates}
-        bias_dram = {"r": br, "n": bn, "z": bz}
-        bias_rows = {g: held("bias_rows_" + g, [P, P], F32) for g in gates}
-        x_raw = [placed("x_raw_0", [P, PACK, HALF], F32), placed("x_raw_1", [P, PACK, HALF], F32)]
-        state = [placed("state_0", [P, T], F32)] + [held("state_%d" % b, [P, T], F32) for b in range(1, BLOCKS)]
-        both_weights = held("event_weight", [P, J], F32)
-        event_weight = [both_weights[:, c * HALF : (c + 1) * HALF] for c in range(HALVES)]
-        pages = [held("page_%d" % i, [P, T], F32) for i in range(PAGES - 1)]
+        all_u_scales = held("u_scales", [P, len(gates) * N], U8)
+        u_scales = {g: all_u_scales[:, i * N : (i + 1) * N] for i, g in enumerate(gates)}
+        bias_rows = {g: held("bias_rows_" + g, [P, P], F32) for g in ("r", "n")}
+        weight_rows = held("weight_rows", [P, P], F32)
+        x_raw = [held("x_raw_%d" % c, [P, PACK, HALF], F32) for c in range(HALVES)]
+        state = [held("state_%d" % b, [P, T], F32) for b in range(BLOCKS)]
+        event_weight = [unit_tile("event_weight_%d" % c) for c in range(HALVES)]
+        pages = [held("page_%d" % i, [P, T], F32) for i in range(PAGES)]
         identity = held("identity", [P, P], F32)
 
+        nc.gpsimd.memset(table_scales[:].bitcast(I32), 0)
         warm_in = held("warm_in", [P, 8], F32)
         warm_out = held("warm_out", [P, 8], F32)
         nc.vector.memset(warm_in[:], 0.0)
         nc.scalar.activation(warm_out[:], warm_in[:], ACT.Sigmoid)
-
-        nc.vector.memset(table_scales[:].bitcast(I32), 0)
-        for g in gates:
-            nc.vector.memset(u_scales[g][:].bitcast(I32), 0)
-        for g in gates:
-            nc.vector.memset(bias_rows[g][:], 0.0)
+        nc.vector.memset(all_u_scales[:].bitcast(I32), 0)
+        for tile in list(bias_rows.values()) + [weight_rows]:
+            nc.vector.memset(tile[:], 0.0)
         make_identity(nc, identity[:])
-        for page in pages:
+        for page in pages[:2]:
             nc.vector.memset(page[:].bitcast(I32), 0)
+        nc.gpsimd.memset(pages[2][:].bitcast(I32), 0)
 
         def load_scale_rows(tile, dram):
             for q in range(4):
-                rows = tile[QUADRANT * q : QUADRANT * q + 4, :]
-                nc.sync.dma_start(rows.bitcast(I32), dram[0, 4 * q : 4 * q + 4, :].bitcast(I32))
+                part = tile[QUADRANT * q : QUADRANT * q + 4, :]
+                nc.sync.dma_start(part.bitcast(I32), dram[0, 4 * q : 4 * q + 4, :].bitcast(I32))
 
         def load_rows(tile, dram):
             nc.sync.dma_start(tile[:], dram.rearrange("(p i) c -> p i c", i=PACK))
@@ -135,46 +103,49 @@ def tile_list_tgn_gruP_kernel(
         def load_u_words(g):
             nc.sync.dma_start(u_words[g][:].bitcast(I32), u_words_dram[g][0].bitcast(I32))
 
+        def load_u_scales(g):
+            load_scale_rows(u_scales[g], u_scales_dram[g])
+
         def load_bias(g):
-            nc.sync.dma_start(bias_rows[g][0:BLOCKS, :], bias_dram[g].rearrange("(b q) -> b q", q=P))
+            first = BLOCKS if g == "z" else 0
+            nc.sync.dma_start(bias_rows["r" if g == "r" else "n"][first : first + BLOCKS, :], bias_dram[g].rearrange("(b q) -> b q", q=P))
 
         def load_state(b):
             nc.sync.dma_start(state[b][:], hT[b * P : (b + 1) * P, :])
 
+        def load_event_weight(c):
+            nc.sync.dma_start(event_weight[c], wgo[:, c * HALF : (c + 1) * HALF])
+
         nc.sync.dma_start(offsets[:], offs)
-        nc.sync.dma_start(table_words[:], tab_words[0].rearrange("p c i -> p (c i)").bitcast(I32))
+        load_w("r", 0)
         load_scale_rows(table_scales, tab_scales)
         load_rows(x_raw[0], x[:, 0:HALF])
-        load_w("r", 0)
-        load_bias("r")
         load_u_words("r")
-        load_scale_rows(u_scales["r"], ur_scales)
+        load_bias("r")
+        nc.sync.dma_start(table_words[:], tab_words[0].rearrange("p c i -> p (c i)").bitcast(I32))
+        load_u_scales("r")
         load_w("n", 0)
         load_u_words("n")
+        load_u_scales("n")
         load_w("z", 0)
         load_bias("n")
-        load_scale_rows(u_scales["n"], un_scales)
-        load_rows(x_raw[1], x[:, HALF:J])
         load_bias("z")
         load_u_words("z")
-        load_scale_rows(u_scales["z"], uz_scales)
         load_state(0)
+        load_u_scales("z")
         load_state(1)
-        nc.sync.dma_start(both_weights[:], wgo)
+        load_event_weight(0)
+        load_rows(x_raw[1], x[:, HALF:J])
+        nc.sync.dma_start(weight_rows[0 : J // P, :], wgo[0].rearrange("(b q) -> b q", q=P))
+        load_w("r", 1)
+        load_w("n", 1)
+        load_w("z", 1)
         load_state(2)
-        for g in ("z", "r", "n"):
-            load_w(g, 1)
         load_state(3)
+        load_event_weight(1)
 
         def listed(c):
             return offsets[:, c * (HALF // 16) : (c + 1) * (HALF // 16)]
-
-        all_words = held("picked_words", [P, J], U32)
-        all_scales = held("picked_scales", [P, J], U8)
-        nc.vector.tensor_copy(all_words[:], table_words[:].bitcast(U32).indirect(offsets[:]))
-        nc.vector.tensor_copy(all_scales[:], table_scales[:].indirect(offsets[:]))
-        picked_words = [all_words[:, c * HALF : (c + 1) * HALF] for c in range(HALVES)]
-        picked_scales = [all_scales[:, c * HALF : (c + 1) * HALF] for c in range(HALVES)]
 
         def copy_on(engine, out, in_):
             if engine == "scalar":
@@ -195,161 +166,207 @@ def tile_list_tgn_gruP_kernel(
                 )
 
         def quantise(name, grouped, width, on=None):
-            codes = held(name + "_codes", [P, width], U32)
-            if name + "_scales" in PLACES:
-                scales = placed(name + "_scales", [P, width], U8)
-            else:
-                scales = held(name + "_scales", [P, width], U8, on)
+            codes = held(name + "_codes", [P, width], U32, on)
+            scales = held(name + "_scales", [P, width], U8)
             nc.vector.quantize_mx(out=codes[:].bitcast(FP8X4), scales=scales[:], in_=grouped)
             return codes, scales
 
-        x_mx, w_mx = {}, {}
+        x_mx, w_mx, w_grouped = {}, {}, {}
 
-        def quantise_w(name, grouped, parts, on=None):
-            codes, scales = quantise(name, grouped, len(parts) * SPAN, on)
-            for i, (g, span) in enumerate(parts):
-                for b in range(2):
-                    cols = slice(i * SPAN + b * P, i * SPAN + (b + 1) * P)
-                    w_mx[g, 2 * span + b] = (codes[:, cols], scales[:, cols])
+        def round_w(g, span, engine, on=None):
+            w_grouped[g, span] = held("w_grouped_%s%d" % (g, span), [P, SPAN * PACK], BF16, on)
+            round_rows(w_grouped[g, span][:], w_raw[g, span][:], engine)
 
-        x_grouped_0 = held("x_grouped_0", [P, HALF * PACK], BF16)
-        w_grouped_r = placed("w_grouped_r", [P, SPAN * PACK], BF16)
-        w_grouped_n = held("w_grouped_n", [P, SPAN * PACK], BF16)
+        def quantise_w(g, span, on=None):
+            codes, scales = quantise("w_%s%d" % (g, span), w_grouped[g, span][:], SPAN, on)
+            for b in range(2):
+                w_mx[g, 2 * span + b] = (codes[:, b * P : (b + 1) * P], scales[:, b * P : (b + 1) * P])
 
-        across = [bank("across_%d" % i) for i in range(2)]
-        back = [bank("back_%d" % i) for i in range(2)]
+        x_grouped = {}
+
+        def round_x(c, shares):
+            x_grouped[c] = held("x_grouped_%d" % c, [P, HALF * PACK], BF16)
+            first = 0
+            for engine, width in shares:
+                cols = slice(first, first + width)
+                round_rows(x_grouped[c][:, PACK * cols.start : PACK * cols.stop], x_raw[c][:, :, cols], engine)
+                first = cols.stop
+
+        def quantise_x(c):
+            x_mx[c] = quantise("x_%d" % c, x_grouped[c][:], HALF)
+
+        picked_scales = held("picked_scales", [P, J], U8)
+        picked_words = [held("picked_words_%d" % c, [P, HALF], U32) for c in range(HALVES)]
+
+        def pick_words(c):
+            nc.vector.tensor_copy(picked_words[c][:], table_words[:].bitcast(U32).indirect(listed(c)))
+
+        gate_banks = [bank("gate_bank_%d" % i) for i in range(2)]
+        state_banks = [bank("state_bank_%d" % i) for i in range(2)]
+        message_bank = bank("message_bank")
+        sum_bank, back_bank, third_bank = bank("sum_bank"), bank("back_bank"), bank("third_bank")
 
         bias = {g: held("bias_" + g, [P, BLOCKS], F32) for g in gates}
+        weight_columns = held("weight_columns", [P, J // P], F32)
 
-        def turn_bias(g, target, sign):
+        def turn_bias(g, target):
             nc.tensor.transpose(target[:, 0:P], bias_rows[g][:], identity[:])
-            nc.scalar.activation(bias[g][:], target[:, 0:BLOCKS], ACT.Copy, scale=sign)
+            nc.scalar.copy(bias[g][:], target[:, 0:BLOCKS])
+            if g == "n":
+                nc.scalar.activation(bias["z"][:], target[:, BLOCKS : 2 * BLOCKS], ACT.Copy, scale=-1.0)
 
-        def round_x(grouped, c, engines):
-            share = HALF // len(engines)
-            for i, engine in enumerate(engines):
-                cols = slice(i * share, (i + 1) * share)
-                round_rows(grouped[:, PACK * cols.start : PACK * cols.stop], x_raw[c][:, :, cols], engine)
-
-        round_x(x_grouped_0, 0, ("scalar", "gpsimd"))
-        round_rows(w_grouped_r[:], w_raw["r", 0][:], "scalar")
-        turn_bias("r", back[1], 1.0)
-        round_rows(w_grouped_n[:], w_raw["n", 0][:], "scalar")
-        x_mx[0] = quantise("x_0", x_grouped_0[:], HALF)
-        quantise_w("w_r", w_grouped_r[:], [("r", 0)])
-        quantise_w("w_n", w_grouped_n[:], [("n", 0)])
-        pages.append(placed("page_2", [P, T], F32))
-        nc.vector.memset(pages[2][:].bitcast(I32), 0)
-
-        units = [(b, c) for b in range(BLOCKS) for c in range(HALVES)]
-        last = len(units) - 1
+        def turn_weights():
+            nc.tensor.transpose(back_bank[:, 0:P], weight_rows[:], identity[:])
+            nc.scalar.copy(weight_columns[:], back_bank[:, 0 : J // P])
 
         def message_pass(acc, g, u, start, stop):
-            b, c = units[u]
+            b, c = UNITS[u]
             nc.tensor.matmul_mx(
                 out=acc[:], lhsT=w_mx[g, b][0].bitcast(FP8X4), lhsT_scale=w_mx[g, b][1],
                 rhs=x_mx[c][0][:].bitcast(FP8X4), rhs_scale=x_mx[c][1][:], start=start, stop=stop,
             )
 
         def state_pass(acc, g, u, start, stop):
-            b, c = units[u]
+            b, c = UNITS[u]
             nc.tensor.matmul_mx(
                 out=acc[:], lhsT=u_words[g][:, 2 * b * P : 2 * (b + 1) * P].bitcast(FP4X4),
                 lhsT_scale=u_scales[g][:, b * P : (b + 1) * P],
-                rhs=picked_words[c].bitcast(FP8X4), rhs_scale=picked_scales[c], start=start, stop=stop,
+                rhs=picked_words[c][:].bitcast(FP8X4), rhs_scale=picked_scales[:, c * HALF : (c + 1) * HALF],
+                start=start, stop=stop,
             )
 
-        reset_bank, update_bank = bank("reset_bank"), bank("update_bank")
-        state_bank, message_bank = bank("state_bank"), bank("message_bank")
-        sr = {u: reset_bank for u in range(last + 1)}
-        hn = {u: state_bank for u in range(last + 1)}
-        xn = {u: message_bank for u in range(last + 1)}
-        sr[2], sr[1] = across[0], update_bank
-        hn[2] = hn[3] = across[1]
-        for u in range(4):
-            xn[u] = hn[u]
-        sz = {u: update_bank for u in range(last + 1)}
-        sz[1], sz[3] = reset_bank, state_bank
-        for u in range(5, last + 1, HALVES):
-            sr[u], hn[u], xn[u] = across[0], across[1], back[1]
-
-        def block_tile(name):
-            return held(name, [P, J], F32)
-
-        def half(tile, u):
-            return tile[:, (u % HALVES) * HALF : (u % HALVES + 1) * HALF]
-
-        block_keep = {1: block_tile("keep_odd"), 2: block_tile("keep_even")}
-        block_keep[3] = block_keep[1]
-        block_picked = {}
-        keep_gate = {u: unit_tile("keep_gate_of_%d" % u) for u in range(HALVES)}
-        for u in range(HALVES, last + 1):
-            keep_gate[u] = half(block_keep[u // HALVES], u)
-        reset_tiles = [unit_tile("reset_%d" % c) for c in range(HALVES)]
-        reset = {u: reset_tiles[u % HALVES] for u in range(last + 1)}
-        reset[0], reset[2] = placed_unit_tile("reset_of_0"), placed_unit_tile("reset_of_2")
-        reset[3] = unit_tile("reset_of_3")
-        picked = {1: unit_tile("picked_of_1")}
-        summed = {u: unit_tile("summed_of_%d" % u) for u in (0, 2)}
-        gated = {0: summed[0], 2: placed_unit_tile("gated_of_2")}
-        cand, moved, scaled, updated = {}, {}, {}, {}
-
-        def reset_sigmoid(u):
-            b = units[u][0]
-            nc.scalar.activation(reset[u], sr[u][:], ACT.Sigmoid, bias=bias["r"][:, b : b + 1])
+        hn = {u: state_banks[u % 2] for u in range(LAST + 1)}
+        xn = {u: message_bank for u in range(LAST + 1)}
+        xn[1] = xn[3] = third_bank
+        reset_on = {4: "reset_0", 5: "reset_1", 6: "bias_rows_r", 7: "bias_rows_n"}
+        hn[6], hn[7] = back_bank, gate_banks[1]
+        gated_on = {2: "w_grouped_n1", 4: "gated_0", 5: "gated_1", 6: "w_grouped_r1", 7: "scaled_0"}
+        summed_on = {2: "summed_0", 3: "summed_1", 4: "moved_1", 5: "moved_3", 6: "w_grouped_r0", 7: "picked_1"}
+        moved_on = {1: "moved_0", 2: "moved_1", 4: "moved_0", 5: "x_grouped_0", 6: "last_input", 7: "moved_0"}
+        updated_on = {2: "summed_0", 3: "updated_0", 4: "summed_1", 5: "gated_3", 6: "cand_0"}
+        cand_on = {4: "turned_0", 5: "moved_1", 6: "turned_2", 7: "turned_1"}
+        turned_on = {2: "turned_0", 3: "turned_1", 4: "turned_2", 5: "cand_0"}
+        message_on = {4: "w_grouped_r0", 5: "w_grouped_n0", 6: "x_grouped_0", 7: "picked_1"}
+        reset, keep, gated, summed, cand, picked, moved, scaled, updated, message = [{} for _ in range(10)]
 
         def reset_gate(u):
-            message_pass(sr[u], "r", u, True, False)
-            state_pass(sr[u], "r", u, False, True)
-            reset_sigmoid(u)
+            b = UNITS[u][0]
+            acc = gate_banks[u % 2]
+            opening, closing = (message_pass, state_pass) if u < 2 else (state_pass, message_pass)
+            opening(acc, "r", u, True, False)
+            closing(acc, "r", u, False, True)
+            if u in (2, 3):
+                reset[u] = shared.tile([P, HALF], F32, name="reset_%d" % u, align_bytes=64, offset=(u - 2) * 2048)[:]
+            else:
+                reset[u] = unit_tile("reset_%d" % u, reset_on.get(u))
+            nc.scalar.activation(reset[u], acc[:], ACT.Sigmoid, bias=bias["r"][:, b : b + 1])
+
+        def keep_gate(u):
+            b = UNITS[u][0]
+            acc = gate_banks[u % 2 if u < LAST else 0]
+            message_pass(acc, "z", u, True, False)
+            state_pass(acc, "z", u, False, True)
+            keep[u] = unit_tile("keep_%d" % u, "keep_%d" % (u % 4))
+            nc.scalar.activation(keep[u], acc[:], ACT.Sigmoid, bias=bias["z"][:, b : b + 1], scale=-1.0)
 
         def state_product(u):
             state_pass(hn[u], "n", u, True, True)
 
         def message_product(u):
             message_pass(xn[u], "n", u, True, True)
-
-        def update_gate(u):
-            b = units[u][0]
-            opening, closing = (state_pass, message_pass) if b == 0 else (message_pass, state_pass)
-            opening(sz[u], "z", u, True, False)
-            closing(sz[u], "z", u, False, True)
-            nc.scalar.activation(keep_gate[u], sz[u][:], ACT.Sigmoid, bias=bias["z"][:, b : b + 1], scale=-1.0)
+            if u in SUM_ON_GPSIMD:
+                message[u] = unit_tile("message_%d" % u, message_on[u])
+                nc.scalar.copy(message[u], xn[u][:])
 
         def reset_state(u):
+            gated[u] = unit_tile("gated_%d" % u, gated_on.get(u))
             nc.vector.tensor_tensor(gated[u], hn[u][:], reset[u], ALU.mult)
 
         def candidate_sum(u):
-            nc.vector.tensor_tensor(summed[u], xn[u][:], gated[u], ALU.add)
+            summed[u] = unit_tile("summed_%d" % u, summed_on.get(u))
+            if u in SUM_ON_GPSIMD:
+                nc.gpsimd.tensor_tensor(summed[u], message[u], gated[u], ALU.add)
+            else:
+                nc.vector.tensor_tensor(summed[u], xn[u][:], gated[u], ALU.add)
 
-        def candidate_tanh(u):
-            b = units[u][0]
+        def candidate(u):
+            b = UNITS[u][0]
+            cand[u] = unit_tile("cand_%d" % u, cand_on.get(u))
             nc.scalar.activation(cand[u], summed[u], ACT.Tanh, bias=bias["n"][:, b : b + 1])
 
-        def difference(u):
-            b, c = units[u]
-            nc.vector.tensor_tensor(moved[u], state[b][:].indirect(listed(c)), cand[u], ALU.subtract)
+        def pick(u, on=None):
+            b, c = UNITS[u]
+            picked[u] = unit_tile("picked_%d" % u, on)
+            nc.vector.tensor_copy(picked[u], state[b][:].indirect(listed(c)))
 
-        def scale_by_keep(engine, u):
-            engine.tensor_tensor(scaled[u], moved[u], keep_gate[u], ALU.mult)
-
-        def add_candidate(engine, out, u):
-            engine.tensor_tensor(out, scaled[u], cand[u], ALU.add)
-
-        def weigh(engine, out, unweighed, u):
-            engine.tensor_tensor(out, unweighed, event_weight[units[u][1]], ALU.mult)
+        def pick_block(b, on):
+            both = held("picked_block_%d" % b, [P, J], F32, on)
+            nc.vector.tensor_copy(both[:], state[b][:].indirect(offsets[:]))
+            for c in range(HALVES):
+                picked[UNITS.index((b, c))] = both[:, c * HALF : (c + 1) * HALF]
 
         def window(u):
-            b, c = units[u]
+            b, c = UNITS[u]
             return pages[b % PAGES][:].indirect(listed(c))
+
+        turned = {}
+
+        def turn_part(part, target, first):
+            for q in range(HALF // P):
+                cols = slice(q * P, (q + 1) * P)
+                nc.tensor.matmul(
+                    target[:, cols], lhsT=part[:, cols], rhs=identity[:], start=first and q == 0,
+                    stop=not first and q == HALF // P - 1, is_transpose=True,
+                )
+
+        def turn_sum(u, target):
+            c = UNITS[u][1]
+            turn_part(cand[u], target, True)
+            turn_part(picked[u], target, False)
+            turned[u] = unit_tile("turned_%d" % u, turned_on[u])
+            for q in range(HALF // P):
+                cols = slice(q * P, (q + 1) * P)
+                place = c * (HALF // P) + q
+                nc.scalar.activation(turned[u][:, cols], target[:, cols], ACT.Copy, scale=weight_columns[:, place : place + 1])
+
+        def turn_home(u, target):
+            for q in range(HALF // P):
+                cols = slice(q * P, (q + 1) * P)
+                nc.tensor.transpose(target[:, cols], turned[u][:, cols], identity[:])
+            updated[u] = unit_tile("updated_%d" % u, updated_on[u])
+            nc.scalar.copy(updated[u], target[:])
+
+        def subtract(u):
+            moved[u] = unit_tile("moved_%d" % u, moved_on.get(u))
+            nc.gpsimd.tensor_tensor(moved[u], picked[u], cand[u], ALU.subtract)
+
+        def scale(u):
+            nc.gpsimd.tensor_tensor(picked[u], moved[u], keep[u], ALU.mult)
+
+        def add_candidate(u):
+            nc.gpsimd.tensor_tensor(moved[u], picked[u], cand[u], ALU.add)
+
+        def weigh(u):
+            updated[u] = unit_tile("updated_%d" % u, updated_on[u])
+            nc.gpsimd.tensor_tensor(updated[u], moved[u], event_weight[UNITS[u][1]], ALU.mult)
 
         def store_block(b):
             nc.sync.dma_start(out_0[b * P : (b + 1) * P, :], pages[b % PAGES][:])
 
+        def put(u):
+            b, c = UNITS[u]
+            if u < LAST:
+                nc.vector.tensor_copy(window(u), updated[u])
+            else:
+                nc.vector.tensor_tensor(window(u), updated[u], event_weight[c], ALU.mult)
+            if c == HALVES - 1:
+                store_block(b)
+
         y_pairs = [held("y_pairs_%d" % s, [P, HALF], BF16) for s in range(SLICES)]
-        first_grouped = held("y_grouped_of_blocks_0_1", [P, 2, QUARTER * PACK], BF16)
+        first_grouped = held("y_grouped_of_blocks_0_1", [P, 2, QUARTER * PACK], BF16, "x_raw_0")
         y_grouped = {b: first_grouped[:, b, :] for b in range(2)}
-        y_grouped[BLOCKS - 1] = held("y_grouped_of_block_3", [P, QUARTER * PACK], BF16)[:]
+        for b, on in ((2, "w_raw_r0"), (3, "w_raw_n0")):
+            y_grouped[b] = held("y_grouped_of_block_%d" % b, [P, QUARTER * PACK], BF16, on)[:]
 
         def turn_out(b, s, target, engine):
             for a in range(QUARTERS):
@@ -376,165 +393,147 @@ def tile_list_tgn_gruP_kernel(
                 source[:, 0 : count * 2 * P].rearrange("r (s h t) -> r s t h", s=count, h=2),
             )
 
-        def regroup(b):
-            for s in range(SLICES):
-                turn_out(b, s, across[s % 2], "scalar")
-            for pair in range(SLICES // 2):
-                turn_back(2 * pair, back[pair], 0)
-                turn_back(2 * pair + 1, back[pair], 2 * P)
-                weave(b, 2 * pair, 2, back[pair], "scalar")
+        def regroup_back(b, pair, target):
+            turn_back(2 * pair, target, 0)
+            turn_back(2 * pair + 1, target, 2 * P)
+            weave(b, 2 * pair, 2, target, "scalar")
 
-        y_scales = held("y_scales", [P, BLOCKS, QUARTER], U8)
-
-        def pick(u):
-            b, c = units[u]
-            nc.vector.tensor_copy(picked[u], state[b][:].indirect(listed(c)))
-
-        def subtract(u):
-            nc.gpsimd.tensor_tensor(moved[u], picked[u], cand[u], ALU.subtract)
-
-        for u in (0, 2):
-            state_pass(sr[u], "r", u, True, False)
-        for u in (0, 2):
-            message_pass(sr[u], "r", u, False, True)
-            reset_sigmoid(u)
+        def gates_of(u):
+            reset_gate(u)
             state_product(u)
-        turn_bias("n", back[0], 1.0)
-        w_grouped_z = held("w_grouped_z", [P, SPAN * PACK], BF16)
-        round_rows(w_grouped_z[:], w_raw["z", 0][:], "scalar")
-        for step in (reset_state, message_product, candidate_sum):
-            for u in (0, 2):
-                step(u)
-        quantise_w("w_z", w_grouped_z[:], [("z", 0)])
-        x_grouped_1 = held("x_grouped_1", [P, HALF * PACK], BF16)
-        round_x(x_grouped_1, 1, ("gpsimd", "scalar"))
-        x_mx[1] = quantise("x_1", x_grouped_1[:], HALF)
-        turn_bias("z", back[1], -1.0)
-        cand[0] = placed_unit_tile("cand_of_0")
-        block_cand = {1: placed("cand_of_block_1", [P, J], F32), 2: block_tile("cand_of_block_2")}
-        block_cand[3] = block_tile("cand_of_block_3")
-        for u in range(HALVES, last + 1):
-            cand[u] = half(block_cand[u // HALVES], u)
-        candidate_tanh(0)
-        update_gate(0)
-        moved[0] = unit_tile("moved_of_0")
-        difference(0)
+            message_product(u)
+
+        nc.vector.tensor_copy(picked_scales[:], table_scales[:].indirect(offsets[:]))
+        round_w("r", 0, "scalar")
+        quantise_w("r", 0, on="table_scales")
+        round_x(0, X_SHARES)
+        quantise_x(0)
+        pick_words(0)
+        pick_words(1)
+        turn_bias("r", back_bank)
+        round_w("n", 0, "gpsimd")
+        for u in (0, 1):
+            reset_gate(u)
+            state_product(u)
+        quantise_w("n", 0)
+        round_w("z", 0, "gpsimd", on="w_grouped_n0")
+        reset_state(0)
+        for u in (0, 1):
+            message_product(u)
+        turn_bias("n", sum_bank)
+        reset_state(1)
+        candidate_sum(0)
+        quantise_w("z", 0)
+        candidate_sum(1)
+        for u in (0, 1):
+            candidate(u)
+            keep_gate(u)
+        moved[0] = unit_tile("moved_0")
+        nc.vector.tensor_tensor(moved[0], state[0][:].indirect(listed(0)), cand[0], ALU.subtract)
+        scaled[0] = unit_tile("scaled_0")
+        pick(2)
+        nc.vector.tensor_tensor(scaled[0], moved[0], keep[0], ALU.mult)
+        nc.vector.tensor_tensor(moved[0], scaled[0], cand[0], ALU.add)
         pick(1)
-        scaled[0] = summed[0]
-        scale_by_keep(nc.gpsimd, 0)
-        cand[1] = summed[1] = unit_tile("cand_of_1")
-        gated[1] = placed_unit_tile("gated_of_1")
-        gated[3], summed[3] = placed_unit_tile("gated_of_3"), cand[3]
-        reset_gate(1)
-        update_gate(1)
-        reset_gate(3)
-        for u in (1, 3):
-            state_product(u)
-        candidate_tanh(2)
-        for step in (reset_state, message_product, candidate_sum):
-            for u in (1, 3):
-                step(u)
-        candidate_tanh(1)
-        candidate_tanh(3)
-        update_gate(2)
-        update_gate(3)
-
-        def pick_block(b):
-            block_picked[b] = placed("picked_of_block_%d" % b, [P, J], F32)
-            nc.vector.tensor_copy(block_picked[b][:], state[b][:].indirect(offsets[:]))
-
-        pick_block(1)
-        late_rn = placed("late_rn", [P, 2, SPAN * PACK], BF16)
-        late_z = placed("late_z", [P, SPAN * PACK], BF16)
-        round_rows(late_z[:], w_raw["z", 1][:], "scalar")
-        round_rows(late_rn[:, 0, :], w_raw["r", 1][:], "scalar")
-        round_rows(late_rn[:, 1, :], w_raw["n", 1][:], "scalar")
-        for u in range(4, last + 1):
-            gated[u] = summed[u] = cand[u]
-        gated[5] = placed_unit_tile("gated_of_5")
-
-        spare = placed_unit_tile("spare")
-        moved[1], scaled[1] = spare, picked[1]
-        updated[0] = unit_tile("updated_of_0")
-        add_candidate(nc.gpsimd, spare, 0)
-        weigh(nc.gpsimd, updated[0], spare, 0)
+        updated[0] = unit_tile("updated_0")
+        nc.vector.tensor_tensor(updated[0], moved[0], event_weight[0], ALU.mult)
         subtract(1)
-        scale_by_keep(nc.gpsimd, 1)
-        nc.vector.tensor_copy(window(0), updated[0])
-        wide_spare = placed("wide_spare", [P, J], F32)
-        nc.gpsimd.tensor_tensor(wide_spare[:], block_picked[1][:], block_cand[1][:], ALU.subtract)
-
-        quantise_w("late_z", late_z[:], [("z", 1)], on="w_raw_n1")
-        quantise_w("late_rn", late_rn[:].rearrange("p g c -> p (g c)"), [("r", 1), ("n", 1)])
-        unweighed, updated[1] = placed_unit_tile("unweighed_of_1"), unit_tile("updated_of_1")
-        add_candidate(nc.vector, unweighed, 1)
-        weigh(nc.vector, updated[1], unweighed, 1)
-
-        def prepare(b):
-            pair = (HALVES * b, HALVES * b + 1)
-            for u in pair:
-                reset_gate(u)
-                state_product(u)
-                message_product(u)
-            pick_block(b)
-            for u in pair:
-                reset_state(u)
-            for u in pair:
-                candidate_sum(u)
-                candidate_tanh(u)
-            for u in pair:
-                update_gate(u)
-
-        def scale_and_add(b, values):
-            nc.gpsimd.tensor_tensor(values[:], wide_spare[:], block_keep[b][:], ALU.mult)
-            nc.gpsimd.tensor_tensor(wide_spare[:], values[:], block_cand[b][:], ALU.add)
-
-        prepare(2)
-        nc.vector.tensor_copy(window(1), updated[1])
-        store_block(0)
-
-        values = placed("scaled_of_block_1", [P, J], F32)
-        scale_and_add(1, values)
-        nc.gpsimd.tensor_tensor(values[:], wide_spare[:], both_weights[:], ALU.mult)
-        prepare(3)
-        nc.vector.tensor_copy(pages[1][:].indirect(offsets[:]), values[:])
-        store_block(1)
-
-        values = block_picked[2]
-        nc.gpsimd.tensor_tensor(wide_spare[:], values[:], block_cand[2][:], ALU.subtract)
-        scale_and_add(2, values)
+        scale(1)
+        put(0)
+        round_x(1, (("scalar", HALF),))
+        turn_weights()
+        round_w("r", 1, "scalar")
+        round_w("n", 1, "scalar")
+        round_w("z", 1, "scalar")
+        quantise_x(1)
+        pick(3, on="x_grouped_1")
+        for g in gates:
+            quantise_w(g, 1)
+        unweighed = unit_tile("unweighed_1", "w_grouped_z1")
+        nc.gpsimd.tensor_tensor(unweighed, picked[1], cand[1], ALU.add)
+        for u in (2, 3):
+            gates_of(u)
+        for u in (2, 3):
+            reset_state(u)
+        updated[1] = shared.tile([P, HALF], F32, name="updated_1", align_bytes=64, offset=0)[:]
+        nc.gpsimd.tensor_tensor(updated[1], unweighed, event_weight[0], ALU.mult)
+        for step in (candidate_sum, keep_gate, candidate):
+            for u in (2, 3):
+                step(u)
+        pick(4, gated_on[2])
+        subtract(2)
+        scale(2)
+        put(1)
         for u in (4, 5):
-            weigh(nc.gpsimd, half(values, u), half(wide_spare, u), u)
-            nc.vector.tensor_copy(window(u), half(values, u))
-        store_block(2)
-
-        regroup(0)
-        final = BLOCKS - 1
-        last_spare = half(wide_spare, last)
-        for u in (last - 1, last):
-            picked[u] = scaled[u] = half(block_picked[final], u)
-            moved[u] = last_spare
-            subtract(u)
-            scale_by_keep(nc.gpsimd, u)
-            add_candidate(nc.gpsimd, last_spare, u)
-            if u < last:
-                weigh(nc.gpsimd, picked[u], last_spare, u)
-                nc.vector.tensor_copy(window(u), picked[u])
-            else:
-                weigh(nc.vector, window(u), last_spare, u)
-        store_block(final)
-
-        sum_banks = (reset_bank, update_bank, state_bank, message_bank)
-        regroup(1)
-        for s, target in enumerate((across[0], across[1], back[0], back[1])):
-            turn_out(2, s, target, "scalar")
-        y_grouped[2] = placed("y_grouped_of_block_2", [P, QUARTER * PACK], BF16)[:]
+            gates_of(u)
+        subtract(3)
+        for u in (4, 5):
+            reset_state(u)
+        gates_of(6)
+        reset_gate(7)
+        for u in (4, 5):
+            keep_gate(u)
+        state_product(7)
+        message_product(7)
+        turn_sum(2, sum_bank)
+        scale(3)
+        candidate_sum(4)
+        candidate_sum(5)
+        for u in (6, 7):
+            reset_state(u)
+        pick(5, reset_on[5])
+        candidate_sum(7)
+        pick_block(3, reset_on[6])
+        turn_home(2, state_banks[1])
+        for u in (4, 5):
+            candidate(u)
+        put(2)
+        turn_sum(3, third_bank)
+        turn_home(3, back_bank)
+        for u in (6, 7):
+            keep_gate(u)
+        candidate(7)
+        subtract(4)
+        candidate_sum(6)
+        scale(4)
+        subtract(5)
+        subtract(7)
+        scale(5)
+        put(3)
+        turn_sum(4, sum_bank)
+        turn_home(4, state_banks[0])
+        candidate(6)
+        put(4)
+        turn_sum(5, third_bank)
+        turn_home(5, back_bank)
+        put(5)
+        subtract(6)
+        scale(7)
+        scale(6)
+        add_candidate(6)
+        weigh(6)
+        updated[LAST] = unit_tile("updated_7", "last_input")
+        nc.gpsimd.tensor_tensor(updated[LAST], picked[LAST], cand[LAST], ALU.add)
+        ring = (sum_bank, state_banks[0], third_bank, back_bank)
+        for b in range(BLOCKS - 1):
+            for s in range(SLICES):
+                turn_out(b, s, ring[(2 * b + s) % 4], "scalar")
+            if b == 0:
+                put(6)
+            if b < 2:
+                for pair in range(2):
+                    regroup_back(b, pair, ring[(2 * b + pair) % 4])
+        out_banks = (gate_banks[0], gate_banks[1], message_bank, state_banks[1])
         for s in range(SLICES):
-            turn_back(s, sum_banks[s], 0)
-            weave(2, s, 1, sum_banks[s], "scalar")
-        for s, engine in enumerate(("scalar", "scalar", "scalar", "vector")):
-            turn_out(final, s, sum_banks[s], engine)
-        y_codes = placed("y_codes", [P, BLOCKS, QUARTER], U32)
+            turn_back(s, out_banks[s], 0)
+            weave(2, s, 1, out_banks[s], "scalar")
+        put(LAST)
+
+        final = BLOCKS - 1
+        for s in range(3):
+            turn_out(final, s, out_banks[s], "scalar")
+        y_codes = held("y_codes", [P, BLOCKS, QUARTER], U32, "last_input")
+        y_scales = held("y_scales", [P, BLOCKS, QUARTER], U8)
 
         def quantise_y(blocks, cols, grouped):
             nc.vector.quantize_mx(
@@ -553,7 +552,8 @@ def tile_list_tgn_gruP_kernel(
         quantise_y(slice(0, 2), slice(0, QUARTER), first_grouped[:].rearrange("r b c -> r (b c)"))
         store_words(slice(0, 2))
         quantise_y(slice(2, final), slice(0, QUARTER), y_grouped[2])
-        for pair, targets in enumerate((back, across)):
+        turn_out(final, 3, out_banks[3], "vector")
+        for pair, targets in enumerate((ring[:2], ring[2:])):
             for i, engine in enumerate(("scalar", "vector")):
                 turn_back(2 * pair + i, targets[i], 0)
                 weave(final, 2 * pair + i, 1, targets[i], engine)

@@ -76,7 +76,7 @@ def tile_list_tgn_gruP_kernel(
         pages = [held("page_%d" % i, [P, T], F32) for i in range(PAGES)]
         identity = held("identity", [P, P], F32)
 
-        nc.gpsimd.memset(table_scales[:].bitcast(I32), 0)
+        nc.vector.memset(table_scales[:].bitcast(I32), 0)
         warm_in = held("warm_in", [P, 8], F32)
         warm_out = held("warm_out", [P, 8], F32)
         nc.vector.memset(warm_in[:], 0.0)
@@ -85,9 +85,8 @@ def tile_list_tgn_gruP_kernel(
         for tile in list(bias_rows.values()) + [weight_rows]:
             nc.vector.memset(tile[:], 0.0)
         make_identity(nc, identity[:])
-        for page in pages[:2]:
+        for page in pages:
             nc.vector.memset(page[:].bitcast(I32), 0)
-        nc.gpsimd.memset(pages[2][:].bitcast(I32), 0)
 
         def load_scale_rows(tile, dram):
             for q in range(4):

@@ -30,8 +30,8 @@ SLICES = QUARTER // P
 PAGES = 3
 UNITS = [(0, 0), (1, 0), (0, 1), (1, 1), (2, 0), (2, 1), (3, 0), (3, 1)]
 LAST = len(UNITS) - 1
-ON_TENSOR = (2, 3, 4, 5)
-SUM_ON_GPSIMD = (4, 5, 6)
+ON_TENSOR = (2, 3, 4)
+SUM_ON_GPSIMD = ()
 X_SHARES = (("scalar", 224), ("vector", 288))
 
 
@@ -63,8 +63,9 @@ def tile_list_tgn_gruP_kernel(
         offsets = own.tile([P, J // 16], U16, name="offsets")
         table_words = held("table_words", [P, T], I32)
         table_scales = held("table_scales", [P, T], U8)
-        w_raw = {(g, s): held("w_raw_%s%d" % (g, s), [P, PACK, SPAN], F32) for g in gates for s in range(2) if (g, s) != ("z", 1)}
+        w_raw = {(g, s): held("w_raw_%s%d" % (g, s), [P, PACK, SPAN], F32) for g in gates for s in range(2) if (g, s) not in (("z", 1), ("n", 0))}
         w_raw["z", 1] = shared.tile([P, PACK, SPAN], F32, name="w_raw_z1", align_bytes=64, offset=0)
+        w_raw["n", 0] = shared.tile([P, PACK, SPAN], F32, name="w_raw_n0", align_bytes=64, offset=4096)
         u_words = {g: held("u_words_" + g, [P, 2 * N], U8) for g in gates}
         all_u_scales = held("u_scales", [P, len(gates) * N], U8)
         u_scales = {g: all_u_scales[:, i * N : (i + 1) * N] for i, g in enumerate(gates)}
@@ -73,7 +74,7 @@ def tile_list_tgn_gruP_kernel(
         x_raw = [held("x_raw_%d" % c, [P, PACK, HALF], F32) for c in range(HALVES)]
         state = [held("state_%d" % b, [P, T], F32) for b in range(BLOCKS)]
         event_weight = [unit_tile("event_weight_%d" % c) for c in range(HALVES)]
-        pages = [held("page_%d" % i, [P, T], F32) for i in range(PAGES)]
+        pages = {0: held("page_0", [P, T], F32)}
         identity = held("identity", [P, P], F32)
 
         nc.vector.memset(table_scales[:].bitcast(I32), 0)
@@ -85,8 +86,14 @@ def tile_list_tgn_gruP_kernel(
         for tile in list(bias_rows.values()) + [weight_rows]:
             nc.vector.memset(tile[:], 0.0)
         make_identity(nc, identity[:])
-        for page in pages:
-            nc.vector.memset(page[:].bitcast(I32), 0)
+        nc.vector.memset(pages[0][:].bitcast(I32), 0)
+
+        def clear_page(i, on):
+            if on is None:
+                pages[i] = shared.tile([P, T], F32, name="page_%d" % i, align_bytes=64, offset=8192)
+            else:
+                pages[i] = held("page_%d" % i, [P, T], F32, on)
+            nc.gpsimd.memset(pages[i][:].bitcast(I32), 0)
 
         def load_scale_rows(tile, dram):
             for q in range(4):
@@ -117,15 +124,15 @@ def tile_list_tgn_gruP_kernel(
 
         nc.sync.dma_start(offsets[:], offs)
         load_w("r", 0)
+        load_u_words("n")
         load_scale_rows(table_scales, tab_scales)
         load_rows(x_raw[0], x[:, 0:HALF])
-        load_u_words("r")
         load_bias("r")
         nc.sync.dma_start(table_words[:], tab_words[0].rearrange("p c i -> p (c i)").bitcast(I32))
-        load_u_scales("r")
-        load_w("n", 0)
-        load_u_words("n")
         load_u_scales("n")
+        load_w("n", 0)
+        load_u_words("r")
+        load_u_scales("r")
         load_w("z", 0)
         load_bias("n")
         load_bias("z")
@@ -173,7 +180,10 @@ def tile_list_tgn_gruP_kernel(
         x_mx, w_mx, w_grouped = {}, {}, {}
 
         def round_w(g, span, engine, on=None):
-            w_grouped[g, span] = held("w_grouped_%s%d" % (g, span), [P, SPAN * PACK], BF16, on)
+            if (g, span) == ("r", 0):
+                w_grouped[g, span] = shared.tile([P, SPAN * PACK], BF16, name="w_grouped_r0", align_bytes=64, offset=12288)
+            else:
+                w_grouped[g, span] = held("w_grouped_%s%d" % (g, span), [P, SPAN * PACK], BF16, on)
             round_rows(w_grouped[g, span][:], w_raw[g, span][:], engine)
 
         def quantise_w(g, span, on=None):
@@ -184,7 +194,10 @@ def tile_list_tgn_gruP_kernel(
         x_grouped = {}
 
         def round_x(c, shares):
-            x_grouped[c] = held("x_grouped_%d" % c, [P, HALF * PACK], BF16)
+            if c == 0:
+                x_grouped[c] = shared.tile([P, HALF * PACK], BF16, name="x_grouped_0", align_bytes=64, offset=8192)
+            else:
+                x_grouped[c] = held("x_grouped_%d" % c, [P, HALF * PACK], BF16)
             first = 0
             for engine, width in shares:
                 cols = slice(first, first + width)
@@ -236,33 +249,38 @@ def tile_list_tgn_gruP_kernel(
 
         hn = {u: state_banks[u % 2] for u in range(LAST + 1)}
         xn = {u: message_bank for u in range(LAST + 1)}
-        xn[1] = xn[3] = third_bank
-        reset_on = {4: "reset_0", 5: "reset_1", 6: "bias_rows_r", 7: "bias_rows_n"}
-        hn[6], hn[7] = back_bank, gate_banks[1]
-        gated_on = {2: "w_grouped_n1", 4: "gated_0", 5: "gated_1", 6: "w_grouped_r1", 7: "scaled_0"}
-        summed_on = {2: "summed_0", 3: "summed_1", 4: "moved_1", 5: "moved_3", 6: "w_grouped_r0", 7: "picked_1"}
-        moved_on = {1: "moved_0", 2: "moved_1", 4: "moved_0", 5: "x_grouped_0", 6: "last_input", 7: "moved_0"}
-        updated_on = {2: "summed_0", 3: "updated_0", 4: "summed_1", 5: "gated_3", 6: "cand_0"}
-        cand_on = {4: "turned_0", 5: "moved_1", 6: "turned_2", 7: "turned_1"}
-        turned_on = {2: "turned_0", 3: "turned_1", 4: "turned_2", 5: "cand_0"}
-        message_on = {4: "w_grouped_r0", 5: "w_grouped_n0", 6: "x_grouped_0", 7: "picked_1"}
+        xn[0], xn[1] = gate_banks
+        xn[3] = third_bank
+        keep_bank = {u: gate_banks[u % 2] for u in range(LAST)}
+        keep_bank.update({0: state_banks[0], 1: state_banks[1], LAST: gate_banks[0]})
+        reset_bank = {u: gate_banks[u % 2] for u in range(LAST + 1)}
+        xn[5] = third_bank
+        hn[6], hn[7], xn[6], xn[7] = gate_banks[0], gate_banks[1], back_bank, state_banks[1]
+        reset_on = {}
+        gated_on = {2: "w_grouped_n1", 4: "gated_0", 5: "gated_1", 6: "gated_0", 7: "gated_1"}
+        summed_on = {u: "summed_%d" % (u % 2) for u in range(6)}
+        moved_on = {1: "moved_0", 2: "moved_1", 4: "moved_0", 5: "moved_1", 6: "last_input", 7: "cand_1"}
+        updated_on = {2: "scaled_0", 3: "reset_6", 4: "x_grouped_1", 5: "moved_0", 6: "scaled_0"}
+        cand_on = {4: "turned_2", 5: "summed_0", 6: "turned_3", 7: "summed_6"}
+        turned_on = {2: "turned_2", 3: "turned_3", 4: "cand_0"}
+        message_on = {}
         reset, keep, gated, summed, cand, picked, moved, scaled, updated, message = [{} for _ in range(10)]
 
         def reset_gate(u):
             b = UNITS[u][0]
-            acc = gate_banks[u % 2]
+            acc = reset_bank[u]
             opening, closing = (message_pass, state_pass) if u < 2 else (state_pass, message_pass)
             opening(acc, "r", u, True, False)
             closing(acc, "r", u, False, True)
-            if u in (2, 3):
-                reset[u] = shared.tile([P, HALF], F32, name="reset_%d" % u, align_bytes=64, offset=(u - 2) * 2048)[:]
+            if u < 4:
+                reset[u] = shared.tile([P, HALF], F32, name="reset_%d" % u, align_bytes=64, offset=((u + 2) % 4) * 2048)[:]
             else:
                 reset[u] = unit_tile("reset_%d" % u, reset_on.get(u))
             nc.scalar.activation(reset[u], acc[:], ACT.Sigmoid, bias=bias["r"][:, b : b + 1])
 
         def keep_gate(u):
             b = UNITS[u][0]
-            acc = gate_banks[u % 2 if u < LAST else 0]
+            acc = keep_bank[u]
             message_pass(acc, "z", u, True, False)
             state_pass(acc, "z", u, False, True)
             keep[u] = unit_tile("keep_%d" % u, "keep_%d" % (u % 4))
@@ -332,6 +350,8 @@ def tile_list_tgn_gruP_kernel(
             for q in range(HALF // P):
                 cols = slice(q * P, (q + 1) * P)
                 nc.tensor.transpose(target[:, cols], turned[u][:, cols], identity[:])
+
+        def fetch(u, target):
             updated[u] = unit_tile("updated_%d" % u, updated_on[u])
             nc.scalar.copy(updated[u], target[:])
 
@@ -364,7 +384,7 @@ def tile_list_tgn_gruP_kernel(
         y_pairs = [held("y_pairs_%d" % s, [P, HALF], BF16) for s in range(SLICES)]
         first_grouped = held("y_grouped_of_blocks_0_1", [P, 2, QUARTER * PACK], BF16, "x_raw_0")
         y_grouped = {b: first_grouped[:, b, :] for b in range(2)}
-        for b, on in ((2, "w_raw_r0"), (3, "w_raw_n0")):
+        for b, on in ((2, "w_raw_r0"), (3, "w_raw_z0")):
             y_grouped[b] = held("y_grouped_of_block_%d" % b, [P, QUARTER * PACK], BF16, on)[:]
 
         def turn_out(b, s, target, engine):
@@ -407,10 +427,11 @@ def tile_list_tgn_gruP_kernel(
         quantise_w("r", 0, on="table_scales")
         round_x(0, X_SHARES)
         quantise_x(0)
+        clear_page(1, None)
         pick_words(0)
         pick_words(1)
         turn_bias("r", back_bank)
-        round_w("n", 0, "gpsimd")
+        round_w("n", 0, "scalar")
         for u in (0, 1):
             reset_gate(u)
             state_product(u)
@@ -466,63 +487,66 @@ def tile_list_tgn_gruP_kernel(
         for u in (4, 5):
             gates_of(u)
         subtract(3)
-        for u in (4, 5):
-            reset_state(u)
-        gates_of(6)
-        reset_gate(7)
-        for u in (4, 5):
-            keep_gate(u)
-        state_product(7)
-        message_product(7)
-        turn_sum(2, sum_bank)
+        for step in (reset_state, candidate_sum):
+            for u in (4, 5):
+                step(u)
         scale(3)
-        candidate_sum(4)
-        candidate_sum(5)
-        for u in (6, 7):
-            reset_state(u)
-        pick(5, reset_on[5])
-        candidate_sum(7)
-        pick_block(3, reset_on[6])
+        clear_page(2, "moved_3")
+        turn_sum(2, sum_bank)
         turn_home(2, state_banks[1])
         for u in (4, 5):
             candidate(u)
-        put(2)
-        turn_sum(3, third_bank)
-        turn_home(3, back_bank)
-        for u in (6, 7):
+        fetch(2, state_banks[1])
+        for u in (4, 5):
             keep_gate(u)
-        candidate(7)
-        subtract(4)
-        candidate_sum(6)
-        scale(4)
-        subtract(5)
-        subtract(7)
-        scale(5)
-        put(3)
+        for step in (reset_gate, keep_gate):
+            for u in (6, 7):
+                step(u)
+        pick(5, "reset_4")
+        pick_block(3, "reset_5")
+        put(2)
+        turn_sum(3, sum_bank)
+        turn_home(3, state_banks[0])
+        for u in (6, 7):
+            state_product(u)
+            message_product(u)
+        for u in (6, 7):
+            reset_state(u)
+        fetch(3, state_banks[0])
+        for u in (6, 7):
+            candidate_sum(u)
+        for step in (subtract, scale):
+            for u in (4, 5):
+                step(u)
         turn_sum(4, sum_bank)
-        turn_home(4, state_banks[0])
         candidate(6)
+        turn_home(4, state_banks[0])
+        candidate(7)
+        fetch(4, state_banks[0])
+        add_candidate(5)
+        weigh(5)
+        put(3)
         put(4)
-        turn_sum(5, third_bank)
-        turn_home(5, back_bank)
         put(5)
         subtract(6)
-        scale(7)
+        subtract(7)
         scale(6)
+        scale(7)
         add_candidate(6)
         weigh(6)
         updated[LAST] = unit_tile("updated_7", "last_input")
         nc.gpsimd.tensor_tensor(updated[LAST], picked[LAST], cand[LAST], ALU.add)
-        ring = (sum_bank, state_banks[0], third_bank, back_bank)
+        ring = (sum_bank, state_banks[0])
+        late_ring = (sum_bank, state_banks[0], message_bank, third_bank)
         for b in range(BLOCKS - 1):
             for s in range(SLICES):
-                turn_out(b, s, ring[(2 * b + s) % 4], "scalar")
+                turn_out(b, s, (ring if b == 0 else late_ring)[s % (2 if b == 0 else 4)], "scalar")
             if b == 0:
                 put(6)
             if b < 2:
                 for pair in range(2):
-                    regroup_back(b, pair, ring[(2 * b + pair) % 4])
-        out_banks = (gate_banks[0], gate_banks[1], message_bank, state_banks[1])
+                    regroup_back(b, pair, (message_bank, third_bank)[pair])
+        out_banks = (gate_banks[0], gate_banks[1], back_bank, state_banks[1])
         for s in range(SLICES):
             turn_back(s, out_banks[s], 0)
             weave(2, s, 1, out_banks[s], "scalar")
@@ -552,7 +576,7 @@ def tile_list_tgn_gruP_kernel(
         store_words(slice(0, 2))
         quantise_y(slice(2, final), slice(0, QUARTER), y_grouped[2])
         turn_out(final, 3, out_banks[3], "vector")
-        for pair, targets in enumerate((ring[:2], ring[2:])):
+        for pair, targets in enumerate((late_ring[:2], late_ring[2:])):
             for i, engine in enumerate(("scalar", "vector")):
                 turn_back(2 * pair + i, targets[i], 0)
                 weave(final, 2 * pair + i, 1, targets[i], engine)

@@ -74,7 +74,7 @@ def tile_list_tgn_gruP_kernel(
         x_raw = [held("x_raw_%d" % c, [P, PACK, HALF], F32) for c in range(HALVES)]
         state = [held("state_%d" % b, [P, T], F32) for b in range(BLOCKS)]
         event_weight = [unit_tile("event_weight_%d" % c) for c in range(HALVES)]
-        pages = {0: held("page_0", [P, T], F32)}
+        pages = {i: held("page_%d" % i, [P, T], F32) for i in (0, 2)}
         identity = held("identity", [P, P], F32)
 
         nc.vector.memset(table_scales[:].bitcast(I32), 0)
@@ -86,7 +86,8 @@ def tile_list_tgn_gruP_kernel(
         for tile in list(bias_rows.values()) + [weight_rows]:
             nc.vector.memset(tile[:], 0.0)
         make_identity(nc, identity[:])
-        nc.vector.memset(pages[0][:].bitcast(I32), 0)
+        for i in (0, 2):
+            nc.vector.memset(pages[i][:].bitcast(I32), 0)
 
         def clear_page(i, on):
             if on is None:
@@ -491,7 +492,6 @@ def tile_list_tgn_gruP_kernel(
             for u in (4, 5):
                 step(u)
         scale(3)
-        clear_page(2, "moved_3")
         turn_sum(2, sum_bank)
         turn_home(2, state_banks[1])
         for u in (4, 5):

@@ -30,8 +30,8 @@ SLICES = QUARTER // P
 PAGES = 3
 UNITS = [(0, 0), (1, 0), (0, 1), (1, 1), (2, 0), (2, 1), (3, 0), (3, 1)]
 LAST = len(UNITS) - 1
-ON_TENSOR = (2, 3, 4)
-SUM_ON_GPSIMD = ()
+ON_TENSOR = (2, 3, 4, 5)
+SUM_ON_GPSIMD = (4, 5, 6)
 X_SHARES = (("scalar", 224), ("vector", 288))
 
 
@@ -50,6 +50,9 @@ def tile_list_tgn_gruP_kernel(
 
         def unit_tile(name, on=None):
             return held(name, [P, HALF], F32, on)[:]
+
+        def placed(name, offset):
+            return shared.tile([P, HALF], F32, name=name, align_bytes=64, offset=offset)[:]
 
         def bank(name):
             return psum.tile([P, HALF], F32, name=name)
@@ -255,16 +258,16 @@ def tile_list_tgn_gruP_kernel(
         keep_bank = {u: gate_banks[u % 2] for u in range(LAST)}
         keep_bank.update({0: state_banks[0], 1: state_banks[1], LAST: gate_banks[0]})
         reset_bank = {u: gate_banks[u % 2] for u in range(LAST + 1)}
-        xn[5] = third_bank
-        hn[6], hn[7], xn[6], xn[7] = gate_banks[0], gate_banks[1], back_bank, state_banks[1]
-        reset_on = {}
-        gated_on = {2: "w_grouped_n1", 4: "gated_0", 5: "gated_1", 6: "gated_0", 7: "gated_1"}
-        summed_on = {u: "summed_%d" % (u % 2) for u in range(6)}
-        moved_on = {1: "moved_0", 2: "moved_1", 4: "moved_0", 5: "moved_1", 6: "last_input", 7: "cand_1"}
-        updated_on = {2: "scaled_0", 3: "reset_6", 4: "x_grouped_1", 5: "moved_0", 6: "scaled_0"}
-        cand_on = {4: "turned_2", 5: "summed_0", 6: "turned_3", 7: "summed_6"}
-        turned_on = {2: "turned_2", 3: "turned_3", 4: "cand_0"}
-        message_on = {}
+        reset_on = {6: "bias_rows_r", 7: "bias_rows_n"}
+        reset_on.update({4: "reset_4", 5: "reset_5"})
+        hn[6], hn[7] = back_bank, gate_banks[1]
+        gated_on = {2: "w_grouped_n1", 4: "gated_0", 5: "gated_1", 6: "w_grouped_r1", 7: "scaled_0"}
+        summed_on = {2: "summed_0", 3: "summed_1", 4: "moved_1", 5: "moved_3", 6: "message_4", 7: "picked_1"}
+        moved_on = {1: "moved_0", 2: "moved_1", 4: "moved_0", 5: "message_6", 6: "last_input", 7: "moved_0"}
+        updated_on = {2: "summed_0", 3: "updated_0", 4: "summed_1", 5: "gated_3"}
+        cand_on = {4: "turned_0", 5: "moved_1", 6: "turned_2", 7: "turned_1"}
+        turned_on = {2: "turned_0", 3: "turned_1", 4: "turned_2"}
+        message_on = {4: "message_4", 5: "w_grouped_n0", 6: "message_6"}
         reset, keep, gated, summed, cand, picked, moved, scaled, updated, message = [{} for _ in range(10)]
 
         def reset_gate(u):
@@ -341,7 +344,7 @@ def tile_list_tgn_gruP_kernel(
             c = UNITS[u][1]
             turn_part(cand[u], target, True)
             turn_part(picked[u], target, False)
-            turned[u] = unit_tile("turned_%d" % u, turned_on[u])
+            turned[u] = placed("turned_5", 19456) if u == 5 else unit_tile("turned_%d" % u, turned_on[u])
             for q in range(HALF // P):
                 cols = slice(q * P, (q + 1) * P)
                 place = c * (HALF // P) + q
@@ -367,11 +370,19 @@ def tile_list_tgn_gruP_kernel(
             nc.gpsimd.tensor_tensor(moved[u], picked[u], cand[u], ALU.add)
 
         def weigh(u):
-            updated[u] = unit_tile("updated_%d" % u, updated_on[u])
+            updated[u] = placed("updated_6", 18432)
             nc.gpsimd.tensor_tensor(updated[u], moved[u], event_weight[UNITS[u][1]], ALU.mult)
 
         def store_block(b):
             nc.sync.dma_start(out_0[b * P : (b + 1) * P, :], pages[b % PAGES][:])
+
+        rows = {}
+
+        def load_back(b):
+            rows[b] = held("rows_of_block_%d" % b, [P, PACK, QUARTER], F32, "state_%d" % b)
+            for a in range(QUARTERS):
+                source = out_0[b * P : (b + 1) * P, a * QUARTER : (a + 1) * QUARTER]
+                nc.sync.dma_start(rows[b][QUADRANT * a : QUADRANT * (a + 1)], source.rearrange("(r i) c -> r i c", i=PACK))
 
         def put(u):
             b, c = UNITS[u]
@@ -381,12 +392,11 @@ def tile_list_tgn_gruP_kernel(
                 nc.vector.tensor_tensor(window(u), updated[u], event_weight[c], ALU.mult)
             if c == HALVES - 1:
                 store_block(b)
+                if b == 0:
+                    load_back(b)
 
         y_pairs = [held("y_pairs_%d" % s, [P, HALF], BF16) for s in range(SLICES)]
-        first_grouped = held("y_grouped_of_blocks_0_1", [P, 2, QUARTER * PACK], BF16, "x_raw_0")
-        y_grouped = {b: first_grouped[:, b, :] for b in range(2)}
-        for b, on in ((2, "w_raw_r0"), (3, "w_raw_z0")):
-            y_grouped[b] = held("y_grouped_of_block_%d" % b, [P, QUARTER * PACK], BF16, on)[:]
+        y_grouped = {}
 
         def turn_out(b, s, target, engine):
             for a in range(QUARTERS):
@@ -412,11 +422,6 @@ def tile_list_tgn_gruP_kernel(
                 words.rearrange("r (s t h) -> r s t h", s=count, h=2),
                 source[:, 0 : count * 2 * P].rearrange("r (s h t) -> r s t h", s=count, h=2),
             )
-
-        def regroup_back(b, pair, target):
-            turn_back(2 * pair, target, 0)
-            turn_back(2 * pair + 1, target, 2 * P)
-            weave(b, 2 * pair, 2, target, "scalar")
 
         def gates_of(u):
             reset_gate(u)
@@ -488,72 +493,78 @@ def tile_list_tgn_gruP_kernel(
         for u in (4, 5):
             gates_of(u)
         subtract(3)
-        for step in (reset_state, candidate_sum):
-            for u in (4, 5):
-                step(u)
-        scale(3)
-        turn_sum(2, sum_bank)
-        turn_home(2, state_banks[1])
         for u in (4, 5):
-            candidate(u)
-        fetch(2, state_banks[1])
+            reset_state(u)
+        gates_of(6)
+        reset_gate(7)
         for u in (4, 5):
             keep_gate(u)
-        for step in (reset_gate, keep_gate):
-            for u in (6, 7):
-                step(u)
-        pick(5, "reset_4")
-        pick_block(3, "reset_5")
-        put(2)
-        turn_sum(3, sum_bank)
-        turn_home(3, state_banks[0])
-        for u in (6, 7):
-            state_product(u)
-            message_product(u)
+        state_product(7)
+        message_product(7)
+        turn_sum(2, sum_bank)
+        scale(3)
+        candidate_sum(4)
+        candidate_sum(5)
         for u in (6, 7):
             reset_state(u)
-        fetch(3, state_banks[0])
+        pick(5, reset_on[5])
+        candidate_sum(7)
+        pick_block(3, reset_on[6])
+        turn_home(2, state_banks[1])
+        fetch(2, state_banks[1])
+        for u in (4, 5):
+            candidate(u)
+        put(2)
+        turn_sum(3, third_bank)
+        turn_home(3, back_bank)
+        fetch(3, back_bank)
         for u in (6, 7):
-            candidate_sum(u)
-        for step in (subtract, scale):
-            for u in (4, 5):
-                step(u)
-        turn_sum(4, sum_bank)
-        candidate(6)
-        turn_home(4, state_banks[0])
+            keep_gate(u)
         candidate(7)
-        fetch(4, state_banks[0])
-        add_candidate(5)
-        weigh(5)
+        subtract(4)
+        candidate_sum(6)
+        scale(4)
+        subtract(5)
+        subtract(7)
+        scale(5)
         put(3)
+        turn_sum(4, sum_bank)
+        turn_home(4, state_banks[0])
+        fetch(4, state_banks[0])
+        candidate(6)
         put(4)
+        turn_sum(5, third_bank)
+        turn_home(5, back_bank)
+        fetch(5, back_bank)
         put(5)
         subtract(6)
-        subtract(7)
-        scale(6)
         scale(7)
+        scale(6)
         add_candidate(6)
         weigh(6)
         updated[LAST] = unit_tile("updated_7", "last_input")
         nc.gpsimd.tensor_tensor(updated[LAST], picked[LAST], cand[LAST], ALU.add)
-        ring = (sum_bank, state_banks[0])
-        late_ring = (sum_bank, state_banks[0], message_bank, third_bank)
-        for b in range(BLOCKS - 1):
-            for s in range(SLICES):
-                turn_out(b, s, (ring if b == 0 else late_ring)[s % (2 if b == 0 else 4)], "scalar")
-            if b == 0:
-                put(6)
-            if b < 2:
-                for pair in range(2):
-                    regroup_back(b, pair, (message_bank, third_bank)[pair])
-        out_banks = (gate_banks[0], gate_banks[1], back_bank, state_banks[1])
+        put(6)
+        ring = (third_bank, back_bank, sum_bank, state_banks[0])
+        first_grouped = held("y_grouped_of_block_1", [P, QUARTER * PACK], BF16, "x_raw_0")
+        y_grouped[1] = first_grouped[:]
+        for s in range(SLICES):
+            turn_out(1, s, ring[s % 2], "scalar")
+        for pair in range(2):
+            turn_back(2 * pair, ring[2 + pair], 0)
+            turn_back(2 * pair + 1, ring[2 + pair], 2 * P)
+            weave(1, 2 * pair, 2, ring[2 + pair], "scalar")
+        for s in range(SLICES):
+            turn_out(2, s, ring[s], "scalar")
+        out_banks = (gate_banks[0], gate_banks[1], message_bank, state_banks[1])
+        y_grouped[2] = shared.tile([P, QUARTER * PACK], BF16, name="y_grouped_of_block_2", align_bytes=64, offset=16384)[:]
         for s in range(SLICES):
             turn_back(s, out_banks[s], 0)
             weave(2, s, 1, out_banks[s], "scalar")
         put(LAST)
 
         final = BLOCKS - 1
-        for s in range(3):
+        for s in range(SLICES):
             turn_out(final, s, out_banks[s], "scalar")
         y_codes = held("y_codes", [P, BLOCKS, QUARTER], U32, "last_input")
         y_scales = held("y_scales", [P, BLOCKS, QUARTER], U8)
@@ -572,17 +583,20 @@ def tile_list_tgn_gruP_kernel(
                 source = y_codes[QUADRANT * a : QUADRANT * (a + 1), blocks, :]
                 nc.sync.dma_start(word_rows[:, blocks, a * QUARTER : (a + 1) * QUARTER], source.bitcast(I32))
 
-        quantise_y(slice(0, 2), slice(0, QUARTER), first_grouped[:].rearrange("r b c -> r (b c)"))
-        store_words(slice(0, 2))
-        quantise_y(slice(2, final), slice(0, QUARTER), y_grouped[2])
-        turn_out(final, 3, out_banks[3], "vector")
-        for pair, targets in enumerate((late_ring[:2], late_ring[2:])):
+        for b in (1, 2):
+            quantise_y(slice(b, b + 1), slice(0, QUARTER), y_grouped[b])
+        store_words(slice(1, final))
+        y_grouped[0] = held("y_grouped_of_block_0", [P, QUARTER * PACK], BF16, "event_weight_1")[:]
+        round_rows(y_grouped[0], rows[0][:], "vector")
+        quantise_y(slice(0, 1), slice(0, QUARTER), y_grouped[0])
+        y_grouped[final] = held("y_grouped_of_block_3", [P, QUARTER * PACK], BF16, "state_0")[:]
+        for pair, targets in enumerate(((sum_bank, state_banks[0]), (third_bank, back_bank))):
             for i, engine in enumerate(("scalar", "vector")):
                 turn_back(2 * pair + i, targets[i], 0)
                 weave(final, 2 * pair + i, 1, targets[i], engine)
             cols = slice(2 * pair * P, 2 * (pair + 1) * P)
             quantise_y(slice(final, BLOCKS), cols, y_grouped[final][:, PACK * cols.start : PACK * cols.stop])
-        store_words(slice(2, BLOCKS))
+        store_words(slice(0, BLOCKS, final))
         scale_rows = out_2[0].rearrange("(b j) t -> j b t", j=4)
         for a in range(QUARTERS):
             source = y_scales[QUADRANT * a : QUADRANT * a + 4]

@@ -31,7 +31,7 @@ PAGES = 3
 UNITS = [(0, 0), (1, 0), (0, 1), (1, 1), (2, 0), (2, 1), (3, 0), (3, 1)]
 LAST = len(UNITS) - 1
 ON_TENSOR = (2, 3, 4, 5)
-SUM_ON_GPSIMD = (4, 5, 6)
+SUM_ON_GPSIMD = ()
 X_SHARES = (("scalar", 224), ("vector", 288))
 
 
@@ -258,16 +258,21 @@ def tile_list_tgn_gruP_kernel(
         keep_bank = {u: gate_banks[u % 2] for u in range(LAST)}
         keep_bank.update({0: state_banks[0], 1: state_banks[1], LAST: gate_banks[0]})
         reset_bank = {u: gate_banks[u % 2] for u in range(LAST + 1)}
-        reset_on = {6: "bias_rows_r", 7: "bias_rows_n"}
-        reset_on.update({4: "reset_4", 5: "reset_5"})
-        hn[6], hn[7] = back_bank, gate_banks[1]
-        gated_on = {2: "w_grouped_n1", 4: "gated_0", 5: "gated_1", 6: "w_grouped_r1", 7: "scaled_0"}
-        summed_on = {2: "summed_0", 3: "summed_1", 4: "moved_1", 5: "moved_3", 6: "message_4", 7: "picked_1"}
-        moved_on = {1: "moved_0", 2: "moved_1", 4: "moved_0", 5: "message_6", 6: "last_input", 7: "moved_0"}
-        updated_on = {2: "summed_0", 3: "updated_0", 4: "summed_1", 5: "gated_3"}
-        cand_on = {4: "turned_0", 5: "moved_1", 6: "turned_2", 7: "turned_1"}
+        xn[5] = third_bank
+        hn[6], hn[7], xn[6], xn[7] = gate_banks[0], gate_banks[1], back_bank, back_bank
+        keep_bank.update({6: state_banks[1], 7: state_banks[1]})
+        reset_on = {}
+        gated_on = {2: "w_grouped_n1", 4: "gated_0", 5: "gated_1"}
+        summed_on = {u: "summed_%d" % (u % 2) for u in range(6)}
+        moved_on = {1: "moved_0", 2: "moved_1", 4: "moved_0", 5: "gated_3"}
+        updated_on = {2: "scaled_0", 3: "updated_0", 4: "picked_2", 5: "picked_1"}
+        cand_on = {4: "turned_0", 5: "summed_0"}
         turned_on = {2: "turned_0", 3: "turned_1", 4: "turned_2"}
-        message_on = {4: "message_4", 5: "w_grouped_n0", 6: "message_6"}
+        message_on = {}
+
+        def pair_tile(name, on=None):
+            both = held(name, [P, J], F32, on)
+            return both[:], {u: both[:, UNITS[u][1] * HALF : (UNITS[u][1] + 1) * HALF] for u in (6, 7)}
         reset, keep, gated, summed, cand, picked, moved, scaled, updated, message = [{} for _ in range(10)]
 
         def reset_gate(u):
@@ -278,6 +283,8 @@ def tile_list_tgn_gruP_kernel(
             closing(acc, "r", u, False, True)
             if u < 4:
                 reset[u] = shared.tile([P, HALF], F32, name="reset_%d" % u, align_bytes=64, offset=((u + 2) % 4) * 2048)[:]
+            elif u == LAST:
+                reset[u] = placed("reset_7", 29696)
             else:
                 reset[u] = unit_tile("reset_%d" % u, reset_on.get(u))
             nc.scalar.activation(reset[u], acc[:], ACT.Sigmoid, bias=bias["r"][:, b : b + 1])
@@ -287,7 +294,8 @@ def tile_list_tgn_gruP_kernel(
             acc = keep_bank[u]
             message_pass(acc, "z", u, True, False)
             state_pass(acc, "z", u, False, True)
-            keep[u] = unit_tile("keep_%d" % u, "keep_%d" % (u % 4))
+            if u < 6:
+                keep[u] = unit_tile("keep_%d" % u, "keep_%d" % (u % 4))
             nc.scalar.activation(keep[u], acc[:], ACT.Sigmoid, bias=bias["z"][:, b : b + 1], scale=-1.0)
 
         def state_product(u):
@@ -300,7 +308,8 @@ def tile_list_tgn_gruP_kernel(
                 nc.scalar.copy(message[u], xn[u][:])
 
         def reset_state(u):
-            gated[u] = unit_tile("gated_%d" % u, gated_on.get(u))
+            if u < 6:
+                gated[u] = unit_tile("gated_%d" % u, gated_on.get(u))
             nc.vector.tensor_tensor(gated[u], hn[u][:], reset[u], ALU.mult)
 
         def candidate_sum(u):
@@ -321,8 +330,9 @@ def tile_list_tgn_gruP_kernel(
             nc.vector.tensor_copy(picked[u], state[b][:].indirect(listed(c)))
 
         def pick_block(b, on):
-            both = held("picked_block_%d" % b, [P, J], F32, on)
+            both = shared.tile([P, J], F32, name="picked_block_%d" % b, align_bytes=64, offset=on)
             nc.vector.tensor_copy(both[:], state[b][:].indirect(offsets[:]))
+            picked["block", b] = both[:]
             for c in range(HALVES):
                 picked[UNITS.index((b, c))] = both[:, c * HALF : (c + 1) * HALF]
 
@@ -356,7 +366,7 @@ def tile_list_tgn_gruP_kernel(
                 nc.tensor.transpose(target[:, cols], turned[u][:, cols], identity[:])
 
         def fetch(u, target):
-            updated[u] = unit_tile("updated_%d" % u, updated_on[u])
+            updated[u] = placed("updated_2", 28672) if u == 2 else unit_tile("updated_%d" % u, updated_on[u])
             nc.scalar.copy(updated[u], target[:])
 
         def subtract(u):
@@ -368,10 +378,6 @@ def tile_list_tgn_gruP_kernel(
 
         def add_candidate(u):
             nc.gpsimd.tensor_tensor(moved[u], picked[u], cand[u], ALU.add)
-
-        def weigh(u):
-            updated[u] = placed("updated_6", 18432)
-            nc.gpsimd.tensor_tensor(updated[u], moved[u], event_weight[UNITS[u][1]], ALU.mult)
 
         def store_block(b):
             nc.sync.dma_start(out_0[b * P : (b + 1) * P, :], pages[b % PAGES][:])
@@ -386,7 +392,7 @@ def tile_list_tgn_gruP_kernel(
 
         def put(u):
             b, c = UNITS[u]
-            if u < LAST:
+            if b < BLOCKS - 1:
                 nc.vector.tensor_copy(window(u), updated[u])
             else:
                 nc.vector.tensor_tensor(window(u), updated[u], event_weight[c], ALU.mult)
@@ -493,59 +499,62 @@ def tile_list_tgn_gruP_kernel(
         for u in (4, 5):
             gates_of(u)
         subtract(3)
-        for u in (4, 5):
-            reset_state(u)
-        gates_of(6)
-        reset_gate(7)
+        scale(3)
+        for step in (reset_state, candidate_sum):
+            for u in (4, 5):
+                step(u)
         for u in (4, 5):
             keep_gate(u)
-        state_product(7)
-        message_product(7)
-        turn_sum(2, sum_bank)
-        scale(3)
-        candidate_sum(4)
-        candidate_sum(5)
+        messages, message_half = pair_tile("messages_of_block_3", "gated_3")
+        gated_pair, halves = pair_tile("gated_of_block_3", "w_raw_n1")
+        gated.update(halves)
         for u in (6, 7):
-            reset_state(u)
-        pick(5, reset_on[5])
-        candidate_sum(7)
-        pick_block(3, reset_on[6])
+            gates_of(u)
+            nc.scalar.copy(message_half[u], xn[u][:])
+        turn_sum(2, sum_bank)
         turn_home(2, state_banks[1])
-        fetch(2, state_banks[1])
         for u in (4, 5):
             candidate(u)
+        for u in (6, 7):
+            reset_state(u)
+        pick(5, "reset_4")
+        fetch(2, state_banks[1])
+        pick_block(3, 30720)
         put(2)
-        turn_sum(3, third_bank)
+        turn_sum(3, sum_bank)
         turn_home(3, back_bank)
         fetch(3, back_bank)
+        keep_pair, halves = pair_tile("keep_of_block_3", "w_raw_r0")
+        keep.update(halves)
         for u in (6, 7):
             keep_gate(u)
-        candidate(7)
         subtract(4)
-        candidate_sum(6)
         scale(4)
+        summed_pair, _ = pair_tile("summed_of_block_3", moved_on[4])
+        nc.gpsimd.tensor_tensor(summed_pair, messages, gated_pair, ALU.add)
         subtract(5)
-        subtract(7)
         scale(5)
         put(3)
         turn_sum(4, sum_bank)
         turn_home(4, state_banks[0])
         fetch(4, state_banks[0])
-        candidate(6)
+        cand_pair, halves = pair_tile("cand_of_block_3", turned_on[4])
+        cand.update(halves)
+        nc.scalar.activation(cand_pair, summed_pair, ACT.Tanh, bias=bias["n"][:, BLOCKS - 1 : BLOCKS])
         put(4)
-        turn_sum(5, third_bank)
+        turn_sum(5, state_banks[0])
         turn_home(5, back_bank)
         fetch(5, back_bank)
         put(5)
-        subtract(6)
-        scale(7)
-        scale(6)
-        add_candidate(6)
-        weigh(6)
-        updated[LAST] = unit_tile("updated_7", "last_input")
-        nc.gpsimd.tensor_tensor(updated[LAST], picked[LAST], cand[LAST], ALU.add)
+        moved_pair, _ = pair_tile("moved_of_block_3", moved_on[5])
+        nc.gpsimd.tensor_tensor(moved_pair, picked["block", BLOCKS - 1], cand_pair, ALU.subtract)
+        nc.gpsimd.tensor_tensor(picked["block", BLOCKS - 1], moved_pair, keep_pair, ALU.mult)
+        unweighed = shared.tile([P, J], F32, name="unweighed_of_block_3", align_bytes=64, offset=18432)
+        nc.gpsimd.tensor_tensor(unweighed[:], picked["block", BLOCKS - 1], cand_pair, ALU.add)
+        for u in (6, 7):
+            updated[u] = unweighed[:, UNITS[u][1] * HALF : (UNITS[u][1] + 1) * HALF]
         put(6)
-        ring = (third_bank, back_bank, sum_bank, state_banks[0])
+        ring = (state_banks[0], back_bank, sum_bank, third_bank)
         first_grouped = held("y_grouped_of_block_1", [P, QUARTER * PACK], BF16, "x_raw_0")
         y_grouped[1] = first_grouped[:]
         for s in range(SLICES):
@@ -557,7 +566,7 @@ def tile_list_tgn_gruP_kernel(
         for s in range(SLICES):
             turn_out(2, s, ring[s], "scalar")
         out_banks = (gate_banks[0], gate_banks[1], message_bank, state_banks[1])
-        y_grouped[2] = shared.tile([P, QUARTER * PACK], BF16, name="y_grouped_of_block_2", align_bytes=64, offset=16384)[:]
+        y_grouped[2] = held("y_grouped_of_block_2", [P, QUARTER * PACK], BF16, "w_raw_z0")[:]
         for s in range(SLICES):
             turn_back(s, out_banks[s], 0)
             weave(2, s, 1, out_banks[s], "scalar")
@@ -566,7 +575,7 @@ def tile_list_tgn_gruP_kernel(
         final = BLOCKS - 1
         for s in range(SLICES):
             turn_out(final, s, out_banks[s], "scalar")
-        y_codes = held("y_codes", [P, BLOCKS, QUARTER], U32, "last_input")
+        y_codes = shared.tile([P, BLOCKS, QUARTER], U32, name="y_codes", align_bytes=64, offset=20480)
         y_scales = held("y_scales", [P, BLOCKS, QUARTER], U8)
 
         def quantise_y(blocks, cols, grouped):

@@ -76,7 +76,8 @@ def tile_list_tgn_gruP_kernel(
         weight_rows = held("weight_rows", [P, P], F32)
         x_raw = [held("x_raw_%d" % c, [P, PACK, HALF], F32) for c in range(HALVES)]
         state = [held("state_%d" % b, [P, T], F32) for b in range(BLOCKS)]
-        event_weight = [unit_tile("event_weight_%d" % c) for c in range(HALVES)]
+        both_weights = held("event_weight", [P, J], F32)
+        event_weight = [both_weights[:, c * HALF : (c + 1) * HALF] for c in range(HALVES)]
         pages = {i: held("page_%d" % i, [P, T], F32) for i in (0, 2)}
         identity = held("identity", [P, P], F32)
 
@@ -264,7 +265,7 @@ def tile_list_tgn_gruP_kernel(
         reset_on = {}
         gated_on = {2: "w_grouped_n1", 4: "gated_0", 5: "gated_1"}
         summed_on = {u: "summed_%d" % (u % 2) for u in range(6)}
-        moved_on = {1: "moved_0", 2: "moved_1", 4: "moved_0", 5: "gated_3"}
+        moved_on = {1: "moved_0", 2: "moved_1", 3: "moved_1", 4: "moved_0", 5: "gated_3"}
         updated_on = {2: "scaled_0", 3: "updated_0", 4: "picked_2", 5: "picked_1"}
         cand_on = {4: "turned_0", 5: "summed_0"}
         turned_on = {2: "turned_0", 3: "turned_1", 4: "turned_2"}
@@ -392,10 +393,7 @@ def tile_list_tgn_gruP_kernel(
 
         def put(u):
             b, c = UNITS[u]
-            if b < BLOCKS - 1:
-                nc.vector.tensor_copy(window(u), updated[u])
-            else:
-                nc.vector.tensor_tensor(window(u), updated[u], event_weight[c], ALU.mult)
+            nc.vector.tensor_copy(window(u), updated[u])
             if c == HALVES - 1:
                 store_block(b)
                 if b == 0:
@@ -478,9 +476,10 @@ def tile_list_tgn_gruP_kernel(
         round_w("n", 1, "scalar")
         round_w("z", 1, "scalar")
         quantise_x(1)
-        pick(3, on="x_grouped_1")
-        for g in gates:
-            quantise_w(g, 1)
+        quantise_w("r", 1)
+        quantise_w("n", 1)
+        pick(3, on="w_grouped_r1")
+        quantise_w("z", 1)
         unweighed = unit_tile("unweighed_1", "w_grouped_z1")
         nc.gpsimd.tensor_tensor(unweighed, picked[1], cand[1], ALU.add)
         for u in (2, 3):
@@ -517,7 +516,7 @@ def tile_list_tgn_gruP_kernel(
             candidate(u)
         for u in (6, 7):
             reset_state(u)
-        pick(5, "reset_4")
+        pick(5, "reset_6")
         fetch(2, state_banks[1])
         pick_block(3, 30720)
         put(2)
@@ -551,9 +550,8 @@ def tile_list_tgn_gruP_kernel(
         nc.gpsimd.tensor_tensor(picked["block", BLOCKS - 1], moved_pair, keep_pair, ALU.mult)
         unweighed = shared.tile([P, J], F32, name="unweighed_of_block_3", align_bytes=64, offset=18432)
         nc.gpsimd.tensor_tensor(unweighed[:], picked["block", BLOCKS - 1], cand_pair, ALU.add)
-        for u in (6, 7):
-            updated[u] = unweighed[:, UNITS[u][1] * HALF : (UNITS[u][1] + 1) * HALF]
-        put(6)
+        nc.vector.tensor_tensor(pages[0][:].indirect(offsets[:]), unweighed[:], both_weights[:], ALU.mult)
+        store_block(BLOCKS - 1)
         ring = (state_banks[0], back_bank, sum_bank, third_bank)
         first_grouped = held("y_grouped_of_block_1", [P, QUARTER * PACK], BF16, "x_raw_0")
         y_grouped[1] = first_grouped[:]
@@ -570,7 +568,6 @@ def tile_list_tgn_gruP_kernel(
         for s in range(SLICES):
             turn_back(s, out_banks[s], 0)
             weave(2, s, 1, out_banks[s], "scalar")
-        put(LAST)
 
         final = BLOCKS - 1
         for s in range(SLICES):
@@ -595,7 +592,7 @@ def tile_list_tgn_gruP_kernel(
         for b in (1, 2):
             quantise_y(slice(b, b + 1), slice(0, QUARTER), y_grouped[b])
         store_words(slice(1, final))
-        y_grouped[0] = held("y_grouped_of_block_0", [P, QUARTER * PACK], BF16, "event_weight_1")[:]
+        y_grouped[0] = held("y_grouped_of_block_0", [P, QUARTER * PACK], BF16, "event_weight")[:]
         round_rows(y_grouped[0], rows[0][:], "vector")
         quantise_y(slice(0, 1), slice(0, QUARTER), y_grouped[0])
         y_grouped[final] = held("y_grouped_of_block_3", [P, QUARTER * PACK], BF16, "state_0")[:]

@@ -78,7 +78,7 @@ def tile_list_tgn_gruP_kernel(
         state = [held("state_%d" % b, [P, T], F32) for b in range(BLOCKS)]
         both_weights = held("event_weight", [P, J], F32)
         event_weight = [both_weights[:, c * HALF : (c + 1) * HALF] for c in range(HALVES)]
-        pages = {i: held("page_%d" % i, [P, T], F32) for i in (0, 2)}
+        pages = {i: held("page_%d" % i, [P, T], F32) for i in range(PAGES)}
         identity = held("identity", [P, P], F32)
 
         nc.vector.memset(table_scales[:].bitcast(I32), 0)
@@ -90,20 +90,14 @@ def tile_list_tgn_gruP_kernel(
         for tile in list(bias_rows.values()) + [weight_rows]:
             nc.vector.memset(tile[:], 0.0)
         make_identity(nc, identity[:])
-        for i in (0, 2):
+        for i in range(PAGES):
             nc.vector.memset(pages[i][:].bitcast(I32), 0)
 
-        def clear_page(i, on):
-            if on is None:
-                pages[i] = shared.tile([P, T], F32, name="page_%d" % i, align_bytes=64, offset=8192)
-            else:
-                pages[i] = held("page_%d" % i, [P, T], F32, on)
-            nc.gpsimd.memset(pages[i][:].bitcast(I32), 0)
 
-        def load_scale_rows(tile, dram):
+        def load_scale_rows(tile, dram, queue=nc.sync):
             for q in range(4):
                 part = tile[QUADRANT * q : QUADRANT * q + 4, :]
-                nc.sync.dma_start(part.bitcast(I32), dram[0, 4 * q : 4 * q + 4, :].bitcast(I32))
+                queue.dma_start(part.bitcast(I32), dram[0, 4 * q : 4 * q + 4, :].bitcast(I32))
 
         def load_rows(tile, dram):
             nc.sync.dma_start(tile[:], dram.rearrange("(p i) c -> p i c", i=PACK))
@@ -115,11 +109,12 @@ def tile_list_tgn_gruP_kernel(
             nc.sync.dma_start(u_words[g][:].bitcast(I32), u_words_dram[g][0].bitcast(I32))
 
         def load_u_scales(g):
-            load_scale_rows(u_scales[g], u_scales_dram[g])
+            load_scale_rows(u_scales[g], u_scales_dram[g], nc.gpsimd if g == "z" else nc.sync)
 
         def load_bias(g):
             first = BLOCKS if g == "z" else 0
-            nc.sync.dma_start(bias_rows["r" if g == "r" else "n"][first : first + BLOCKS, :], bias_dram[g].rearrange("(b q) -> b q", q=P))
+            queue = nc.sync if g == "r" else nc.gpsimd
+            queue.dma_start(bias_rows["r" if g == "r" else "n"][first : first + BLOCKS, :], bias_dram[g].rearrange("(b q) -> b q", q=P))
 
         def load_state(b):
             nc.sync.dma_start(state[b][:], hT[b * P : (b + 1) * P, :])
@@ -437,7 +432,6 @@ def tile_list_tgn_gruP_kernel(
         quantise_w("r", 0, on="table_scales")
         round_x(0, X_SHARES)
         quantise_x(0)
-        clear_page(1, None)
         pick_words(0)
         pick_words(1)
         turn_bias("r", back_bank)
@@ -450,7 +444,7 @@ def tile_list_tgn_gruP_kernel(
         reset_state(0)
         for u in (0, 1):
             message_product(u)
-        turn_bias("n", sum_bank)
+        turn_bias("n", state_banks[0])
         reset_state(1)
         candidate_sum(0)
         quantise_w("z", 0)
@@ -595,6 +589,7 @@ def tile_list_tgn_gruP_kernel(
         y_grouped[0] = held("y_grouped_of_block_0", [P, QUARTER * PACK], BF16, "event_weight")[:]
         round_rows(y_grouped[0], rows[0][:], "vector")
         quantise_y(slice(0, 1), slice(0, QUARTER), y_grouped[0])
+        store_words(slice(0, 1))
         y_grouped[final] = held("y_grouped_of_block_3", [P, QUARTER * PACK], BF16, "state_0")[:]
         for pair, targets in enumerate(((sum_bank, state_banks[0]), (third_bank, back_bank))):
             for i, engine in enumerate(("scalar", "vector")):
@@ -602,7 +597,7 @@ def tile_list_tgn_gruP_kernel(
                 weave(final, 2 * pair + i, 1, targets[i], engine)
             cols = slice(2 * pair * P, 2 * (pair + 1) * P)
             quantise_y(slice(final, BLOCKS), cols, y_grouped[final][:, PACK * cols.start : PACK * cols.stop])
-        store_words(slice(0, BLOCKS, final))
+        store_words(slice(final, BLOCKS))
         scale_rows = out_2[0].rearrange("(b j) t -> j b t", j=4)
         for a in range(QUARTERS):
             source = y_scales[QUADRANT * a : QUADRANT * a + 4]

from contextlib import ExitStack

import concourse.mybir as mybir
from concourse.masks import make_identity

K, N, T, J = 512, 512, 2048, 1024
FLOPS = 6 * 2 * K * N * J

F32 = mybir.dt.float32
BF16 = mybir.dt.bfloat16
I32 = mybir.dt.int32
U32 = mybir.dt.uint32
U16 = mybir.dt.uint16
U8 = mybir.dt.uint8
FP8X4 = mybir.dt.float8_e4m3fn_x4
FP4X4 = mybir.dt.float4_e2m1fn_x4
ALU = mybir.AluOpType
ACT = mybir.ActivationFunctionType

P = 128
PACK = 4
QUADRANT = 32
HALF = 512
HALVES = J // HALF
BLOCKS = N // P
SPAN = 2 * P
QUARTERS = P // QUADRANT
QUARTER = T // QUARTERS
SLICES = QUARTER // P
PAGES = 3
UNITS = [(0, 0), (1, 0), (0, 1), (1, 1), (2, 0), (2, 1), (3, 0), (3, 1)]
LAST = len(UNITS) - 1
ON_TENSOR = (2, 3, 4, 5)
SUM_ON_GPSIMD = ()
X_SHARES = (("scalar", 224), ("vector", 288))


def tile_list_tgn_gruP_kernel(
    tc, x, tab_words, tab_scales, wz, uz_words, uz_scales, wr, ur_words, ur_scales,
    wn, un_words, un_scales, bz, br, bn, hT, wgo, offs, out_0, out_1, out_2,
):
    nc = tc.nc
    with ExitStack() as ctx:
        own = ctx.enter_context(tc.tile_pool(name="keep", bufs=1))
        shared = ctx.enter_context(tc.tile_pool(name="shared", bufs=1))
        psum = ctx.enter_context(tc.psum_pool(name="psum", bufs=1))

        def held(name, shape, dtype, on=None):
            return own.tile(shape, dtype, name=name, tag=on or name, align_bytes=64)

        def unit_tile(name, on=None):
            return held(name, [P, HALF], F32, on)[:]

        def placed(name, offset):
            return shared.tile([P, HALF], F32, name=name, align_bytes=64, offset=offset)[:]

        def bank(name):
            return psum.tile([P, HALF], F32, name=name)

        gates = ("r", "n", "z")
        w_dram = {"r": wr, "n": wn, "z": wz}
        u_words_dram = {"r": ur_words, "n": un_words, "z": uz_words}
        u_scales_dram = {"r": ur_scales, "n": un_scales, "z": uz_scales}
        bias_dram = {"r": br, "n": bn, "z": bz}

        offsets = own.tile([P, J // 16], U16, name="offsets")
        table_words = held("table_words", [P, T], I32)
        table_scales = held("table_scales", [P, T], U8)
        w_raw = {(g, s): held("w_raw_%s%d" % (g, s), [P, PACK, SPAN], F32) for g in gates for s in range(2) if (g, s) not in (("z", 1), ("n", 0))}
        w_raw["z", 1] = shared.tile([P, PACK, SPAN], F32, name="w_raw_z1", align_bytes=64, offset=0)
        w_raw["n", 0] = shared.tile([P, PACK, SPAN], F32, name="w_raw_n0", align_bytes=64, offset=4096)
        u_words = {g: held("u_words_" + g, [P, 2 * N], U8) for g in gates}
        all_u_scales = held("u_scales", [P, len(gates) * N], U8)
        u_scales = {g: all_u_scales[:, i * N : (i + 1) * N] for i, g in enumerate(gates)}
        bias_rows = {g: held("bias_rows_" + g, [P, P], F32) for g in ("r", "n")}
        weight_rows = held("weight_rows", [P, P], F32)
        x_raw = [held("x_raw_%d" % c, [P, PACK, HALF], F32) for c in range(HALVES)]
        state = [held("state_%d" % b, [P, T], F32) for b in range(BLOCKS)]
        both_weights = held("event_weight", [P, J], F32)
        event_weight = [both_weights[:, c * HALF : (c + 1) * HALF] for c in range(HALVES)]
        pages = {i: held("page_%d" % i, [P, T], F32) for i in range(PAGES)}
        identity = held("identity", [P, P], F32)

        nc.vector.memset(table_scales[:].bitcast(I32), 0)
        warm_in = held("warm_in", [P, 8], F32)
        warm_out = held("warm_out", [P, 8], F32)
        nc.vector.memset(warm_in[:], 0.0)
        nc.scalar.activation(warm_out[:], warm_in[:], ACT.Sigmoid)
        nc.vector.memset(all_u_scales[:].bitcast(I32), 0)
        for tile in list(bias_rows.values()) + [weight_rows]:
            nc.vector.memset(tile[:], 0.0)
        make_identity(nc, identity[:])
        for i in range(PAGES):
            nc.vector.memset(pages[i][:].bitcast(I32), 0)


        def load_scale_rows(tile, dram, queue=nc.sync):
            for q in range(4):
                part = tile[QUADRANT * q : QUADRANT * q + 4, :]
                queue.dma_start(part.bitcast(I32), dram[0, 4 * q : 4 * q + 4, :].bitcast(I32))

        def load_rows(tile, dram):
            nc.sync.dma_start(tile[:], dram.rearrange("(p i) c -> p i c", i=PACK))

        def load_w(g, span):
            load_rows(w_raw[g, span], w_dram[g][:, span * SPAN : (span + 1) * SPAN])

        def load_u_words(g):
            nc.sync.dma_start(u_words[g][:].bitcast(I32), u_words_dram[g][0].bitcast(I32))

        def load_u_scales(g):
            load_scale_rows(u_scales[g], u_scales_dram[g], nc.gpsimd if g == "z" else nc.sync)

        def load_bias(g):
            first = BLOCKS if g == "z" else 0
            queue = nc.sync if g == "r" else nc.gpsimd
            queue.dma_start(bias_rows["r" if g == "r" else "n"][first : first + BLOCKS, :], bias_dram[g].rearrange("(b q) -> b q", q=P))

        def load_state(b):
            nc.sync.dma_start(state[b][:], hT[b * P : (b + 1) * P, :])

        def load_event_weight(c):
            nc.sync.dma_start(event_weight[c], wgo[:, c * HALF : (c + 1) * HALF])

        nc.sync.dma_start(offsets[:], offs)
        load_w("r", 0)
        load_u_words("n")
        load_scale_rows(table_scales, tab_scales)
        load_rows(x_raw[0], x[:, 0:HALF])
        load_bias("r")
        nc.sync.dma_start(table_words[:], tab_words[0].rearrange("p c i -> p (c i)").bitcast(I32))
        load_u_scales("n")
        load_w("n", 0)
        load_u_words("r")
        load_u_scales("r")
        load_w("z", 0)
        load_bias("n")
        load_bias("z")
        load_u_words("z")
        load_state(0)
        load_u_scales("z")
        load_state(1)
        load_event_weight(0)
        load_rows(x_raw[1], x[:, HALF:J])
        nc.sync.dma_start(weight_rows[0 : J // P, :], wgo[0].rearrange("(b q) -> b q", q=P))
        load_w("r", 1)
        load_w("n", 1)
        load_w("z", 1)
        load_state(2)
        load_state(3)
        load_event_weight(1)

        def listed(c):
            return offsets[:, c * (HALF // 16) : (c + 1) * (HALF // 16)]

        def copy_on(engine, out, in_):
            if engine == "scalar":
                nc.scalar.copy(out, in_)
            elif engine == "gpsimd":
                nc.gpsimd.tensor_scalar(out, in_, 1.0, 0.0, ALU.mult, ALU.add)
            else:
                nc.vector.tensor_copy(out, in_)

        def round_rows(grouped, raw, engine):
            if engine == "gpsimd":
                copy_on(engine, grouped.rearrange("p (c i) -> p c i", i=PACK), raw.rearrange("p i c -> p c i"))
            else:
                copy_on(
                    engine,
                    grouped.rearrange("p (c d i) -> p c i d", d=4, i=PACK),
                    raw.rearrange("p i (c d) -> p c i d", d=4),
                )

        def quantise(name, grouped, width, on=None):
            codes = held(name + "_codes", [P, width], U32, on)
            scales = held(name + "_scales", [P, width], U8)
            nc.vector.quantize_mx(out=codes[:].bitcast(FP8X4), scales=scales[:], in_=grouped)
            return codes, scales

        x_mx, w_mx, w_grouped = {}, {}, {}

        def round_w(g, span, engine, on=None):
            if (g, span) == ("r", 0):
                w_grouped[g, span] = shared.tile([P, SPAN * PACK], BF16, name="w_grouped_r0", align_bytes=64, offset=12288)
            else:
                w_grouped[g, span] = held("w_grouped_%s%d" % (g, span), [P, SPAN * PACK], BF16, on)
            round_rows(w_grouped[g, span][:], w_raw[g, span][:], engine)

        def quantise_w(g, span, on=None):
            codes, scales = quantise("w_%s%d" % (g, span), w_grouped[g, span][:], SPAN, on)
            for b in range(2):
                w_mx[g, 2 * span + b] = (codes[:, b * P : (b + 1) * P], scales[:, b * P : (b + 1) * P])

        x_grouped = {}

        def round_x(c, shares):
            if c == 0:
                x_grouped[c] = shared.tile([P, HALF * PACK], BF16, name="x_grouped_0", align_bytes=64, offset=8192)
            else:
                x_grouped[c] = held("x_grouped_%d" % c, [P, HALF * PACK], BF16)
            first = 0
            for engine, width in shares:
                cols = slice(first, first + width)
                round_rows(x_grouped[c][:, PACK * cols.start : PACK * cols.stop], x_raw[c][:, :, cols], engine)
                first = cols.stop

        def quantise_x(c):
            x_mx[c] = quantise("x_%d" % c, x_grouped[c][:], HALF)

        picked_scales = held("picked_scales", [P, J], U8)
        picked_words = [held("picked_words_%d" % c, [P, HALF], U32) for c in range(HALVES)]

        def pick_words(c):
            nc.vector.tensor_copy(picked_words[c][:], table_words[:].bitcast(U32).indirect(listed(c)))

        gate_banks = [bank("gate_bank_%d" % i) for i in range(2)]
        state_banks = [bank("state_bank_%d" % i) for i in range(2)]
        message_bank = bank("message_bank")
        sum_bank, back_bank, third_bank = bank("sum_bank"), bank("back_bank"), bank("third_bank")

        bias = {g: held("bias_" + g, [P, BLOCKS], F32) for g in gates}
        weight_columns = held("weight_columns", [P, J // P], F32)

        def turn_bias(g, target):
            nc.tensor.transpose(target[:, 0:P], bias_rows[g][:], identity[:])
            nc.scalar.copy(bias[g][:], target[:, 0:BLOCKS])
            if g == "n":
                nc.scalar.activation(bias["z"][:], target[:, BLOCKS : 2 * BLOCKS], ACT.Copy, scale=-1.0)

        def turn_weights():
            nc.tensor.transpose(back_bank[:, 0:P], weight_rows[:], identity[:])
            nc.scalar.copy(weight_columns[:], back_bank[:, 0 : J // P])

        def message_pass(acc, g, u, start, stop):
            b, c = UNITS[u]
            nc.tensor.matmul_mx(
                out=acc[:], lhsT=w_mx[g, b][0].bitcast(FP8X4), lhsT_scale=w_mx[g, b][1],
                rhs=x_mx[c][0][:].bitcast(FP8X4), rhs_scale=x_mx[c][1][:], start=start, stop=stop,
            )

        def state_pass(acc, g, u, start, stop):
            b, c = UNITS[u]
            nc.tensor.matmul_mx(
                out=acc[:], lhsT=u_words[g][:, 2 * b * P : 2 * (b + 1) * P].bitcast(FP4X4),
                lhsT_scale=u_scales[g][:, b * P : (b + 1) * P],
                rhs=picked_words[c][:].bitcast(FP8X4), rhs_scale=picked_scales[:, c * HALF : (c + 1) * HALF],
                start=start, stop=stop,
            )

        hn = {u: state_banks[u % 2] for u in range(LAST + 1)}
        xn = {u: message_bank for u in range(LAST + 1)}
        xn[0], xn[1] = gate_banks
        xn[3] = third_bank
        keep_bank = {u: gate_banks[u % 2] for u in range(LAST)}
        keep_bank.update({0: state_banks[0], 1: state_banks[1], LAST: gate_banks[0]})
        reset_bank = {u: gate_banks[u % 2] for u in range(LAST + 1)}
        xn[5] = third_bank
        hn[6], hn[7], xn[6], xn[7] = gate_banks[0], gate_banks[1], back_bank, back_bank
        keep_bank.update({6: state_banks[1], 7: state_banks[1]})
        reset_on = {}
        gated_on = {2: "w_grouped_n1", 4: "gated_0", 5: "gated_1"}
        summed_on = {u: "summed_%d" % (u % 2) for u in range(6)}
        moved_on = {1: "moved_0", 2: "moved_1", 3: "moved_1", 4: "moved_0", 5: "gated_3"}
        updated_on = {2: "scaled_0", 3: "updated_0", 4: "picked_2", 5: "picked_1"}
        cand_on = {4: "turned_0", 5: "summed_0"}
        turned_on = {2: "turned_0", 3: "turned_1", 4: "turned_2"}
        message_on = {}

        def pair_tile(name, on=None):
            both = held(name, [P, J], F32, on)
            return both[:], {u: both[:, UNITS[u][1] * HALF : (UNITS[u][1] + 1) * HALF] for u in (6, 7)}
        reset, keep, gated, summed, cand, picked, moved, scaled, updated, message = [{} for _ in range(10)]

        def reset_gate(u):
            b = UNITS[u][0]
            acc = reset_bank[u]
            opening, closing = (message_pass, state_pass) if u < 2 else (state_pass, message_pass)
            opening(acc, "r", u, True, False)
            closing(acc, "r", u, False, True)
            if u < 4:
                reset[u] = shared.tile([P, HALF], F32, name="reset_%d" % u, align_bytes=64, offset=((u + 2) % 4) * 2048)[:]
            elif u == LAST:
                reset[u] = placed("reset_7", 29696)
            else:
                reset[u] = unit_tile("reset_%d" % u, reset_on.get(u))
            nc.scalar.activation(reset[u], acc[:], ACT.Sigmoid, bias=bias["r"][:, b : b + 1])

        def keep_gate(u):
            b = UNITS[u][0]
            acc = keep_bank[u]
            message_pass(acc, "z", u, True, False)
            state_pass(acc, "z", u, False, True)
            if u < 6:
                keep[u] = unit_tile("keep_%d" % u, "keep_%d" % (u % 4))
            nc.scalar.activation(keep[u], acc[:], ACT.Sigmoid, bias=bias["z"][:, b : b + 1], scale=-1.0)

        def state_product(u):
            state_pass(hn[u], "n", u, True, True)

        def message_product(u):
            message_pass(xn[u], "n", u, True, True)
            if u in SUM_ON_GPSIMD:
                message[u] = unit_tile("message_%d" % u, message_on[u])
                nc.scalar.copy(message[u], xn[u][:])

        def reset_state(u):
            if u < 6:
                gated[u] = unit_tile("gated_%d" % u, gated_on.get(u))
            nc.vector.tensor_tensor(gated[u], hn[u][:], reset[u], ALU.mult)

        def candidate_sum(u):
            summed[u] = unit_tile("summed_%d" % u, summed_on.get(u))
            if u in SUM_ON_GPSIMD:
                nc.gpsimd.tensor_tensor(summed[u], message[u], gated[u], ALU.add)
            else:
                nc.vector.tensor_tensor(summed[u], xn[u][:], gated[u], ALU.add)

        def candidate(u):
            b = UNITS[u][0]
            cand[u] = unit_tile("cand_%d" % u, cand_on.get(u))
            nc.scalar.activation(cand[u], summed[u], ACT.Tanh, bias=bias["n"][:, b : b + 1])

        def pick(u, on=None):
            b, c = UNITS[u]
            picked[u] = unit_tile("picked_%d" % u, on)
            nc.vector.tensor_copy(picked[u], state[b][:].indirect(listed(c)))

        def pick_block(b, on):
            both = shared.tile([P, J], F32, name="picked_block_%d" % b, align_bytes=64, offset=on)
            nc.vector.tensor_copy(both[:], state[b][:].indirect(offsets[:]))
            picked["block", b] = both[:]
            for c in range(HALVES):
                picked[UNITS.index((b, c))] = both[:, c * HALF : (c + 1) * HALF]

        def window(u):
            b, c = UNITS[u]
            return pages[b % PAGES][:].indirect(listed(c))

        turned = {}

        def turn_part(part, target, first):
            for q in range(HALF // P):
                cols = slice(q * P, (q + 1) * P)
                nc.tensor.matmul(
                    target[:, cols], lhsT=part[:, cols], rhs=identity[:], start=first and q == 0,
                    stop=not first and q == HALF // P - 1, is_transpose=True,
                )

        def turn_sum(u, target):
            c = UNITS[u][1]
            turn_part(cand[u], target, True)
            turn_part(picked[u], target, False)
            turned[u] = placed("turned_5", 19456) if u == 5 else unit_tile("turned_%d" % u, turned_on[u])
            for q in range(HALF // P):
                cols = slice(q * P, (q + 1) * P)
                place = c * (HALF // P) + q
                nc.scalar.activation(turned[u][:, cols], target[:, cols], ACT.Copy, scale=weight_columns[:, place : place + 1])

        def turn_home(u, target):
            for q in range(HALF // P):
                cols = slice(q * P, (q + 1) * P)
                nc.tensor.transpose(target[:, cols], turned[u][:, cols], identity[:])

        def fetch(u, target):
            updated[u] = placed("updated_2", 28672) if u == 2 else unit_tile("updated_%d" % u, updated_on[u])
            nc.scalar.copy(updated[u], target[:])

        def subtract(u):
            moved[u] = unit_tile("moved_%d" % u, moved_on.get(u))
            nc.gpsimd.tensor_tensor(moved[u], picked[u], cand[u], ALU.subtract)

        def scale(u):
            nc.gpsimd.tensor_tensor(picked[u], moved[u], keep[u], ALU.mult)

        def add_candidate(u):
            nc.gpsimd.tensor_tensor(moved[u], picked[u], cand[u], ALU.add)

        def store_block(b):
            nc.sync.dma_start(out_0[b * P : (b + 1) * P, :], pages[b % PAGES][:])

        rows = {}

        def load_back(b):
            rows[b] = held("rows_of_block_%d" % b, [P, PACK, QUARTER], F32, "state_%d" % b)
            for a in range(QUARTERS):
                source = out_0[b * P : (b + 1) * P, a * QUARTER : (a + 1) * QUARTER]
                nc.sync.dma_start(rows[b][QUADRANT * a : QUADRANT * (a + 1)], source.rearrange("(r i) c -> r i c", i=PACK))

        def put(u):
            b, c = UNITS[u]
            nc.vector.tensor_copy(window(u), updated[u])
            if c == HALVES - 1:
                store_block(b)
                if b == 0:
                    load_back(b)

        y_pairs = [held("y_pairs_%d" % s, [P, HALF], BF16) for s in range(SLICES)]
        y_grouped = {}

        def turn_out(b, s, target, engine):
            for a in range(QUARTERS):
                first = a * QUARTER + s * P
                nc.tensor.transpose(target[:, a * P : (a + 1) * P], pages[b % PAGES][:, first : first + P], identity[:])
            copy_on(
                engine,
                y_pairs[s][:].rearrange("t (h r e) -> t h r e", h=2, e=2),
                target[:].rearrange("t (r h e) -> t h r e", h=2, e=2),
            )

        def turn_back(s, target, first):
            words = y_pairs[s][:].bitcast(F32)
            for h in range(2):
                nc.tensor.transpose(
                    target[:, first + h * P : first + (h + 1) * P], words[:, h * P : (h + 1) * P], identity[:]
                )

        def weave(b, first, count, source, engine):
            words = y_grouped[b].bitcast(F32)[:, first * 2 * P : (first + count) * 2 * P]
            copy_on(
                engine,
                words.rearrange("r (s t h) -> r s t h", s=count, h=2),
                source[:, 0 : count * 2 * P].rearrange("r (s h t) -> r s t h", s=count, h=2),
            )

        def gates_of(u):
            reset_gate(u)
            state_product(u)
            message_product(u)

        nc.vector.tensor_copy(picked_scales[:], table_scales[:].indirect(offsets[:]))
        round_w("r", 0, "scalar")
        quantise_w("r", 0, on="table_scales")
        round_x(0, X_SHARES)
        quantise_x(0)
        pick_words(0)
        pick_words(1)
        turn_bias("r", back_bank)
        round_w("n", 0, "scalar")
        for u in (0, 1):
            reset_gate(u)
            state_product(u)
        quantise_w("n", 0)
        round_w("z", 0, "gpsimd", on="w_grouped_n0")
        reset_state(0)
        for u in (0, 1):
            message_product(u)
        turn_bias("n", state_banks[0])
        reset_state(1)
        candidate_sum(0)
        quantise_w("z", 0)
        candidate_sum(1)
        for u in (0, 1):
            candidate(u)
            keep_gate(u)
        moved[0] = unit_tile("moved_0")
        nc.vector.tensor_tensor(moved[0], state[0][:].indirect(listed(0)), cand[0], ALU.subtract)
        scaled[0] = unit_tile("scaled_0")
        pick(2)
        nc.vector.tensor_tensor(scaled[0], moved[0], keep[0], ALU.mult)
        nc.vector.tensor_tensor(moved[0], scaled[0], cand[0], ALU.add)
        pick(1)
        updated[0] = unit_tile("updated_0")
        nc.vector.tensor_tensor(updated[0], moved[0], event_weight[0], ALU.mult)
        subtract(1)
        scale(1)
        put(0)
        round_x(1, (("scalar", HALF),))
        turn_weights()
        round_w("r", 1, "scalar")
        round_w("n", 1, "scalar")
        round_w("z", 1, "scalar")
        quantise_x(1)
        quantise_w("r", 1)
        quantise_w("n", 1)
        pick(3, on="w_grouped_r1")
        quantise_w("z", 1)
        unweighed = unit_tile("unweighed_1", "w_grouped_z1")
        nc.gpsimd.tensor_tensor(unweighed, picked[1], cand[1], ALU.add)
        for u in (2, 3):
            gates_of(u)
        for u in (2, 3):
            reset_state(u)
        updated[1] = shared.tile([P, HALF], F32, name="updated_1", align_bytes=64, offset=0)[:]
        nc.gpsimd.tensor_tensor(updated[1], unweighed, event_weight[0], ALU.mult)
        for step in (candidate_sum, keep_gate, candidate):
            for u in (2, 3):
                step(u)
        pick(4, gated_on[2])
        subtract(2)
        scale(2)
        put(1)
        for u in (4, 5):
            gates_of(u)
        subtract(3)
        scale(3)
        for step in (reset_state, candidate_sum):
            for u in (4, 5):
                step(u)
        for u in (4, 5):
            keep_gate(u)
        messages, message_half = pair_tile("messages_of_block_3", "gated_3")
        gated_pair, halves = pair_tile("gated_of_block_3", "w_raw_n1")
        gated.update(halves)
        for u in (6, 7):
            gates_of(u)
            nc.scalar.copy(message_half[u], xn[u][:])
        turn_sum(2, sum_bank)
        turn_home(2, state_banks[1])
        for u in (4, 5):
            candidate(u)
        for u in (6, 7):
            reset_state(u)
        pick(5, "reset_6")
        fetch(2, state_banks[1])
        pick_block(3, 30720)
        put(2)
        turn_sum(3, sum_bank)
        turn_home(3, back_bank)
        fetch(3, back_bank)
        keep_pair, halves = pair_tile("keep_of_block_3", "w_raw_r0")
        keep.update(halves)
        for u in (6, 7):
            keep_gate(u)
        subtract(4)
        scale(4)
        summed_pair, _ = pair_tile("summed_of_block_3", moved_on[4])
        nc.gpsimd.tensor_tensor(summed_pair, messages, gated_pair, ALU.add)
        subtract(5)
        scale(5)
        put(3)
        turn_sum(4, sum_bank)
        turn_home(4, state_banks[0])
        fetch(4, state_banks[0])
        cand_pair, halves = pair_tile("cand_of_block_3", turned_on[4])
        cand.update(halves)
        nc.scalar.activation(cand_pair, summed_pair, ACT.Tanh, bias=bias["n"][:, BLOCKS - 1 : BLOCKS])
        put(4)
        turn_sum(5, state_banks[0])
        turn_home(5, back_bank)
        fetch(5, back_bank)
        put(5)
        moved_pair, _ = pair_tile("moved_of_block_3", moved_on[5])
        nc.gpsimd.tensor_tensor(moved_pair, picked["block", BLOCKS - 1], cand_pair, ALU.subtract)
        nc.gpsimd.tensor_tensor(picked["block", BLOCKS - 1], moved_pair, keep_pair, ALU.mult)
        unweighed = shared.tile([P, J], F32, name="unweighed_of_block_3", align_bytes=64, offset=18432)
        nc.gpsimd.tensor_tensor(unweighed[:], picked["block", BLOCKS - 1], cand_pair, ALU.add)
        nc.vector.tensor_tensor(pages[0][:].indirect(offsets[:]), unweighed[:], both_weights[:], ALU.mult)
        store_block(BLOCKS - 1)
        ring = (state_banks[0], back_bank, sum_bank, third_bank)
        first_grouped = held("y_grouped_of_block_1", [P, QUARTER * PACK], BF16, "x_raw_0")
        y_grouped[1] = first_grouped[:]
        for s in range(SLICES):
            turn_out(1, s, ring[s % 2], "scalar")
        for pair in range(2):
            turn_back(2 * pair, ring[2 + pair], 0)
            turn_back(2 * pair + 1, ring[2 + pair], 2 * P)
            weave(1, 2 * pair, 2, ring[2 + pair], "scalar")
        for s in range(SLICES):
            turn_out(2, s, ring[s], "scalar")
        out_banks = (gate_banks[0], gate_banks[1], message_bank, state_banks[1])
        y_grouped[2] = held("y_grouped_of_block_2", [P, QUARTER * PACK], BF16, "w_raw_z0")[:]
        for s in range(SLICES):
            turn_back(s, out_banks[s], 0)
            weave(2, s, 1, out_banks[s], "scalar")

        final = BLOCKS - 1
        for s in range(SLICES):
            turn_out(final, s, out_banks[s], "scalar")
        y_codes = shared.tile([P, BLOCKS, QUARTER], U32, name="y_codes", align_bytes=64, offset=20480)
        y_scales = held("y_scales", [P, BLOCKS, QUARTER], U8)

        def quantise_y(blocks, cols, grouped):
            nc.vector.quantize_mx(
                out=y_codes[:, blocks, cols].rearrange("r b c -> r (b c)").bitcast(FP8X4),
                scales=y_scales[:, blocks, cols].rearrange("r b c -> r (b c)"),
                in_=grouped,
            )

        word_rows = out_1[0].rearrange("p c i -> p (c i)").bitcast(I32).rearrange("(b r) t -> r b t", r=QUADRANT)

        def store_words(blocks):
            for a in range(QUARTERS):
                source = y_codes[QUADRANT * a : QUADRANT * (a + 1), blocks, :]
                nc.sync.dma_start(word_rows[:, blocks, a * QUARTER : (a + 1) * QUARTER], source.bitcast(I32))

        for b in (1, 2):
            quantise_y(slice(b, b + 1), slice(0, QUARTER), y_grouped[b])
        store_words(slice(1, final))
        y_grouped[0] = held("y_grouped_of_block_0", [P, QUARTER * PACK], BF16, "event_weight")[:]
        round_rows(y_grouped[0], rows[0][:], "vector")
        quantise_y(slice(0, 1), slice(0, QUARTER), y_grouped[0])
        store_words(slice(0, 1))
        y_grouped[final] = held("y_grouped_of_block_3", [P, QUARTER * PACK], BF16, "state_0")[:]
        for pair, targets in enumerate(((sum_bank, state_banks[0]), (third_bank, back_bank))):
            for i, engine in enumerate(("scalar", "vector")):
                turn_back(2 * pair + i, targets[i], 0)
                weave(final, 2 * pair + i, 1, targets[i], engine)
            cols = slice(2 * pair * P, 2 * (pair + 1) * P)
            quantise_y(slice(final, BLOCKS), cols, y_grouped[final][:, PACK * cols.start : PACK * cols.stop])
        store_words(slice(final, BLOCKS))
        scale_rows = out_2[0].rearrange("(b j) t -> j b t", j=4)
        for a in range(QUARTERS):
            source = y_scales[QUADRANT * a : QUADRANT * a + 4]
            nc.sync.dma_start(scale_rows[:, :, a * QUARTER : (a + 1) * QUARTER].bitcast(I32), source.bitcast(I32))
